import numpy as np
import ml_dtypes


def mxq(x, axis, fmt="e4m3"):
    dtype, down = {"e4m3": (ml_dtypes.float8_e4m3fn, 7), "e5m2": (ml_dtypes.float8_e5m2, 14)}[fmt]
    v = np.moveaxis(np.asarray(x, np.float32).astype(ml_dtypes.bfloat16).astype(np.float64), axis, -1)
    blocks = v.reshape(v.shape[:-1] + (-1, 32))
    amax = np.abs(blocks).max(-1, keepdims=True)
    byte = np.maximum(np.where(amax > 0, np.frexp(amax)[1] - 1 + 127, 0) - down, 1)
    scale = np.exp2(byte - 127.0)
    codes = (blocks / scale).astype(np.float32).astype(dtype).astype(np.float64)
    return np.moveaxis((codes * scale).reshape(v.shape), -1, axis)


WIDE = False


def mx_kscale(k):
    if not WIDE:
        return np.ones(k)
    levels = np.array([10, -10, 5, -5, 0])
    if k % 512:
        return np.exp2(np.random.permutation(np.resize(levels, k // 32))).repeat(32)
    a = np.empty((k // 512, 16))
    for p in range(k // 512):
        a[p, :8] = np.random.permutation(np.resize(levels, 8))
        for g in range(8):
            far = levels[np.abs(levels - a[p, g]) >= 10]
            a[p, g + 8] = far[np.random.randint(len(far))]
    return np.exp2(a.ravel()).repeat(32)


BF16 = ml_dtypes.bfloat16


def bf(x):
    return np.asarray(x, np.float32).astype(BF16)


def f64(x):
    return np.asarray(x).astype(np.float64)

def planes(Y):
    n, m = Y.shape
    b = f64(bf(Y)).reshape(n // 32, 32, m)
    amax = np.abs(b).max(1)
    byte = np.clip(np.where(amax > 0, np.frexp(amax)[1] - 1 + 127 - 7, 1), 1, 254)
    codes = (b * np.exp2(127.0 - byte)[:, None, :]).reshape(n, m).astype(np.float32).astype(ml_dtypes.float8_e4m3fn).view(np.uint8)
    words = codes.reshape(n // 512, 128, 4, m).transpose(0, 1, 3, 2)
    return np.ascontiguousarray(words), np.ascontiguousarray(byte.astype(np.uint8).reshape(n // 512, 16, m))


N, J, P, H, C, O = 1024, 4, 3, 512, 512, 512
JC = J * C

SLOPE = 0.2


def setup_inputs():
    t, u = mx_kscale(H), mx_kscale(JC)
    return {
        "rel": bf(np.random.standard_normal((N, J, P))),
        "w1": bf(np.random.standard_normal((P, H)) / np.sqrt(P) * t),
        "b1": bf(np.random.standard_normal(H) * 0.4 * t),
        "w2": bf(np.random.standard_normal((H, C)) / np.sqrt(H) / t[:, None]),
        "b2": bf(np.random.standard_normal(C) * 0.4),
        "f": bf(np.random.standard_normal((N, J, C)) * u.reshape(J, C)),
        "wo": bf(np.random.standard_normal((J, C, O)) / np.sqrt(JC) / u.reshape(J, C, 1)),
    }


def _offset_layer(rel, w1, b1):
    a = rel[:, :, 0, None] * w1[0]
    for i in range(1, w1.shape[0]):
        a = a + rel[:, :, i, None] * w1[i]
    return a + b1


def _leaky(a):
    return np.where(a > 0, a, SLOPE * a)


def core(rel, w1, b1, w2, b2, f, wo):
    rel, w1, b1, w2, b2, f, wo = f64(rel), f64(w1), f64(b1), f64(w2), f64(b2), f64(f), f64(wo)
    n, j, c = f.shape
    o = wo.shape[-1]
    a = _offset_layer(rel, w1, b1)
    m = _leaky(a)
    k = (mxq(m, 2, "e4m3") @ mxq(w2, 0, "e4m3")) + b2
    p = k * f
    return mxq(p.reshape(n, j * c), 1, "e4m3") @ mxq(wo.reshape(j * c, o), 0, "e4m3")


def reference(rel, w1, b1, w2, b2, f, wo):
    R_out = core(rel, w1, b1, w2, b2, f, wo)
    words, scales = planes(R_out.T)
    return R_out, words, scales

@@ -1,0 +1,374 @@
+from contextlib import ExitStack
+
+import concourse.mybir as mybir
+from concourse.masks import make_identity
+
+F32 = mybir.dt.float32
+BF16 = mybir.dt.bfloat16
+U32 = mybir.dt.uint32
+I32 = mybir.dt.int32
+U8 = mybir.dt.uint8
+FP8X4 = mybir.dt.float8_e4m3fn_x4
+ALU = mybir.AluOpType
+ACT = mybir.ActivationFunctionType
+
+N, J, H, C, O = 1024, 4, 512, 512, 512
+FLOPS = 2 * N * J * H * C + 2 * N * J * C * O
+GROUPS = [(0, 256), (256, 256), (512, 256), (768, 256)]
+UNITS = [(g, j) for g in range(len(GROUPS)) for j in range(J)]
+SLOPE = 0.2
+
+
+def tile_rangeviewmetakernelfourneighbour_x1_kernel(tc, rel, w1, b1, w2, b2, f, wo, out_0, out_1, out_2):
+    nc = tc.nc
+    with ExitStack() as ctx:
+        keep = ctx.enter_context(tc.tile_pool(name="keep", bufs=1))
+        work = ctx.enter_context(tc.tile_pool(name="work", bufs=2))
+        psum = ctx.enter_context(tc.psum_pool(name="psum", bufs=1))
+        ctx.enter_context(tc.manual_schedule())
+
+        w2_raw = keep.tile([128, 4, 512], BF16, name="w2_raw")
+        rel_raw = keep.tile([128, 8, 12], BF16, name="rel_raw")
+        w1_raw = keep.tile([128, 3, 512], BF16, name="w1_raw")
+        b1_raw = keep.tile([128, 4], BF16, name="b1_raw")
+        b2_raw = keep.tile([128, 4], BF16, name="b2_raw")
+        wo_raw = [keep.tile([128, 4, 512], BF16, name=f"wo_raw{j}") for j in range(J)]
+        f_sb = [keep.tile([128, J, 512], BF16, name=f"f_sb{a}") for a in range(8)]
+
+        def load_w2():
+            nc.sync.dma_start(out=w2_raw[:], in_=w2.rearrange("(p k) c -> p k c", k=4))
+
+        def load_rel():
+            nc.sync.dma_start(out=rel_raw[:], in_=rel.rearrange("(a p) j i -> p a (j i)", p=128))
+            nc.sync.dma_start(out=b1_raw[:], in_=b1.rearrange("(p t) -> p t", t=4))
+            nc.sync.dma_start(out=b2_raw[:], in_=b2.rearrange("(p t) -> p t", t=4))
+
+        def load_w1():
+            nc.sync.dma_start(out=w1_raw[:], in_=w1.partition_broadcast(128))
+
+        def load_wo(j):
+            nc.sync.dma_start(out=wo_raw[j][:], in_=wo[j].rearrange("(p k) c -> p k c", k=4))
+
+        def load_f(a):
+            nc.sync.dma_start(out=f_sb[a][:], in_=f[a * 128 : (a + 1) * 128])
+
+        load_w2()
+        load_wo(0)
+        load_rel()
+        load_w1()
+        load_wo(1)
+        load_wo(2)
+        load_f(0)
+        load_f(1)
+        load_wo(3)
+        for a in range(2, 8):
+            load_f(a)
+
+        ident = keep.tile([128, 128], F32, name="ident")
+        make_identity(nc, ident[:])
+
+        b1c = keep.tile([128, 4], F32, name="b1c")
+        b2c = keep.tile([128, 4], F32, name="b2c")
+        relf = keep.tile([128, 8, 12], F32, name="relf")
+        w1p = keep.tile([128, 3, 4, 128], BF16, name="w1p")
+
+        def permute(eng, i):
+            v = w1_raw[:, i, :].rearrange("p (q t) -> p t q", t=4)
+            if eng == "v":
+                nc.vector.tensor_copy(out=w1p[:, i], in_=v)
+            else:
+                nc.scalar.copy(w1p[:, i], v)
+
+        w2_q = keep.tile([128, 512], U32, name="w2_q", align_bytes=64)
+        w2_s = keep.tile([128, 512], U8, name="w2_s", align_bytes=64)
+        wo_q = [keep.tile([128, 512], U32, name=f"wo_q{j}", align_bytes=64) for j in range(J)]
+        wo_s = [keep.tile([128, 512], U8, name=f"wo_s{j}", align_bytes=64) for j in range(J)]
+        w_grp = {}
+
+        def interleave(key, raw, on_scalar, parts=(0, 1, 2, 3)):
+            if key not in w_grp:
+                w_grp[key] = work.tile([128, 2048], BF16, name="w_grp", align_bytes=64, bufs=4)
+            dst = w_grp[key][:].rearrange("p (t m k) -> p t m k", t=4, k=4)
+            src = raw[:].rearrange("p k (m t) -> p t m k", t=4)
+            for t in parts:
+                if t in on_scalar:
+                    nc.scalar.copy(dst[:, t], src[:, t])
+                else:
+                    nc.vector.tensor_copy(out=dst[:, t], in_=src[:, t])
+
+        def quant_w(key, q, s):
+            nc.vector.quantize_mx(out=q[:].bitcast(FP8X4), scales=s[:], in_=w_grp[key][:])
+
+        prods, a_ps, a_sb, m_bf, m_q, k_ps, k_sb, f_ps, p_bf = {}, {}, {}, {}, {}, {}, {}, {}, {}
+        p_q = {}
+
+        def halves(u):
+            return GROUPS[UNITS[u][0]][1] // 128
+
+        def s_prod(u):
+            if u == 0:
+                return ((0, 1), (0, 2), (1, 1))
+            if u < 3:
+                return ()
+            return ((0, 1), (0, 2), (1, 1))
+
+        def prod(u, h, i):
+            if u not in prods:
+                prods[u] = [work.tile([128, 3, 512], F32, name=f"prod{x}", align_bytes=64) for x in range(halves(u))]
+            g, j = UNITS[u]
+            a = GROUPS[g][0] // 128 + h
+            col = relf[:, a, 3 * j + i : 3 * j + i + 1]
+            src = w1p[:, i].rearrange("p t q -> p (t q)")
+            dst = prods[u][h][:, i, :]
+            if (h, i) in s_prod(u):
+                nc.scalar.activation(dst, src, ACT.Identity, scale=col)
+            else:
+                nc.vector.tensor_scalar(out=dst, in0=src, scalar1=col, scalar2=None, op0=ALU.mult)
+
+        def tr_a(u, tp):
+            bank = psum.tile([128, 2, 128 * halves(u)], F32, name=f"a_ps{tp}")
+            a_ps.setdefault(u, []).append(bank)
+            for h in range(halves(u)):
+                for tl in range(2):
+                    t = 2 * tp + tl
+                    for i in range(3):
+                        nc.tensor.matmul(bank[:, tl, h * 128 : (h + 1) * 128], lhsT=prods[u][h][:, i, t * 128 : (t + 1) * 128], rhs=ident[:], start=(i == 0), stop=(i == 2), is_transpose=True)
+
+        def rd_a(u, tp):
+            if tp == 0:
+                a_sb[u] = work.tile([128, 4, 128 * halves(u)], F32, name="a_sb", align_bytes=64)
+            for tl in range(2):
+                t = 2 * tp + tl
+                nc.scalar.activation(a_sb[u][:, t, :], a_ps[u][tp][:, tl, :], ACT.Identity, bias=b1c[:, t : t + 1])
+
+        def leaky(u):
+            m_bf[u] = work.tile([128, 128 * halves(u), 4], BF16, name="m_bf", align_bytes=64)
+            a = a_sb[u][:].rearrange("p t r -> p r t")
+            nc.vector.scalar_tensor_tensor(out=m_bf[u][:], in0=a, scalar=SLOPE, in1=a, op0=ALU.mult, op1=ALU.max)
+
+        def quant_m(u):
+            rows = 128 * halves(u)
+            m_q[u] = (work.tile([128, rows], U32, name="m_q", align_bytes=64), work.tile([128, rows], U8, name="m_s", align_bytes=64))
+            nc.vector.quantize_mx(out=m_q[u][0][:].bitcast(FP8X4), scales=m_q[u][1][:], in_=m_bf[u][:].rearrange("p r t -> p (r t)"))
+
+        def mx1(u):
+            k_ps[u] = []
+            for tp in range(2):
+                bank = psum.tile([128, 2, 128 * halves(u)], F32, name=f"k_ps{tp}")
+                k_ps[u].append(bank)
+                for tl in range(2):
+                    cols = slice((2 * tp + tl) * 128, (2 * tp + tl + 1) * 128)
+                    nc.tensor.matmul_mx(bank[:, tl, :], lhsT=w2_q[:, cols].bitcast(FP8X4), lhsT_scale=w2_s[:, cols], rhs=m_q[u][0][:].bitcast(FP8X4), rhs_scale=m_q[u][1][:], start=True, stop=True)
+
+        def rd_k(u):
+            k_sb[u] = work.tile([128, 4, 128 * halves(u)], F32, name="k_sb", align_bytes=64)
+            for t in range(4):
+                nc.scalar.activation(k_sb[u][:, t, :], k_ps[u][t // 2][:, t % 2, :], ACT.Identity, bias=b2c[:, t : t + 1])
+
+        def tr_f(u, part):
+            g, j = UNITS[u]
+            if part == 0:
+                f_ps[u] = psum.tile([128, 2, 128 * halves(u)], F32, name="f_ps", bufs=2)
+            pairs = [(h, e) for h in range(halves(u)) for e in range(2)]
+            for h, e in pairs[: len(pairs) // 2] if part == 0 else pairs[len(pairs) // 2 :]:
+                words = f_sb[GROUPS[g][0] // 128 + h][:, j, :].bitcast(F32)
+                nc.tensor.transpose(f_ps[u][:, e, h * 128 : (h + 1) * 128], words[:, e : 256 : 2], ident[:])
+
+        def times_f(u, parts):
+            p_bf[u] = work.tile([128, 128 * halves(u), 4], BF16, name="p_bf", align_bytes=64)
+            rows = 128 * halves(u) // parts
+            for x in range(parts):
+                r = slice(x * rows, (x + 1) * rows)
+                for tp in range(2):
+                    fv = f_ps[u][:, tp, r].bitcast(BF16).rearrange("p (n e) -> p n e", e=2)
+                    kv = k_sb[u][:, 2 * tp : 2 * tp + 2, r].rearrange("p e n -> p n e")
+                    nc.vector.tensor_tensor(out=p_bf[u][:, r, 2 * tp : 2 * tp + 2], in0=fv, in1=kv, op=ALU.mult)
+
+        def quant_p(u, parts):
+            g, j = UNITS[u]
+            rows = GROUPS[g][1]
+            if j == 0:
+                p_q[g] = (work.tile([128, J, rows], U32, name="p_q", align_bytes=64, bufs=3), work.tile([128, J, rows], U8, name="p_s", align_bytes=64, bufs=3))
+            for x in range(parts):
+                r = slice(x * rows // parts, (x + 1) * rows // parts)
+                nc.vector.quantize_mx(out=p_q[g][0][:, j, r].bitcast(FP8X4), scales=p_q[g][1][:, j, r], in_=p_bf[u][:, r, :].rearrange("p n t -> p (n t)"))
+
+        o_ps, o_bf, t_ps = {}, {}, {}
+        o_q = keep.tile([128, N], U32, name="o_q", align_bytes=64)
+        o_s = keep.tile([128, N], U8, name="o_s", align_bytes=64)
+
+        def group_of(a):
+            g = [x for x in range(len(GROUPS)) if GROUPS[x][0] <= a * 128][-1]
+            r = a * 128 - GROUPS[g][0]
+            return g, slice(r, r + 128)
+
+        def mx2_planes(a, ts):
+            g, rows = group_of(a)
+            if a not in o_ps:
+                o_ps[a] = psum.tile([128, 4, 128], F32, name="o_ps", bufs=2)
+            for t in ts:
+                cols = slice(t * 128, (t + 1) * 128)
+                for j in range(J):
+                    nc.tensor.matmul_mx(o_ps[a][:, t, :], lhsT=wo_q[j][:, cols].bitcast(FP8X4), lhsT_scale=wo_s[j][:, cols], rhs=p_q[g][0][:, j, rows].bitcast(FP8X4), rhs_scale=p_q[g][1][:, j, rows], start=(j == 0), stop=(j == J - 1))
+
+        def mx2_rows(a, js, tag="o_ps", bufs=2):
+            g, rows = group_of(a)
+            if a not in t_ps:
+                t_ps[a] = psum.tile([128, 4, 128], F32, name=tag, bufs=bufs)
+            for j in js:
+                nc.tensor.matmul_mx(t_ps[a][:].rearrange("n t m -> n (t m)"), lhsT=p_q[g][0][:, j, rows].bitcast(FP8X4), lhsT_scale=p_q[g][1][:, j, rows], rhs=wo_q[j][:].bitcast(FP8X4), rhs_scale=wo_s[j][:], start=(j == 0), stop=(j == J - 1))
+
+        def group_o(a, eng="v"):
+            o_bf[a] = work.tile([128, 128, 4], BF16, name="o_bf", align_bytes=64)
+            src = o_ps[a][:].rearrange("p t n -> p n t")
+            if eng == "v":
+                nc.vector.tensor_copy(out=o_bf[a][:], in_=src)
+            else:
+                nc.scalar.activation(o_bf[a][:], src, ACT.Identity)
+
+        def quant_o(a):
+            cols = slice(a * 128, (a + 1) * 128)
+            nc.vector.quantize_mx(out=o_q[:, cols].bitcast(FP8X4), scales=o_s[:, cols], in_=o_bf[a][:].rearrange("p n t -> p (n t)"))
+            nc.sync.dma_start(out=out_1[0, :, cols, :].rearrange("p m t -> p (m t)").bitcast(I32), in_=o_q[:, cols].bitcast(I32))
+
+        def store_scales(c0, c1, queue):
+            for q in range(4):
+                queue.dma_start(out=out_2[0, 4 * q : 4 * q + 4, c0:c1].bitcast(I32), in_=o_s[32 * q : 32 * q + 4, c0:c1].bitcast(I32))
+
+        def rd_t(a, eng="s"):
+            r = work.tile([128, 128, 4], F32, name="r_sb", align_bytes=64)
+            src = t_ps[a][:].rearrange("n t m -> n m t")
+            if eng == "v":
+                nc.vector.tensor_copy(out=r[:], in_=src)
+            else:
+                nc.scalar.activation(r[:], src, ACT.Identity)
+            nc.sync.dma_start(out=out_0[a * 128 : (a + 1) * 128, :], in_=r[:].rearrange("n m t -> n (m t)"))
+
+        def stand_in(n):
+            bank = psum.tile([128, 512], F32, name="o_ps", bufs=2)
+            for r in range(n):
+                nc.tensor.matmul_mx(bank[:], lhsT=w2_q[:, 0:128].bitcast(FP8X4), lhsT_scale=w2_s[:, 0:128], rhs=w2_q[:].bitcast(FP8X4), rhs_scale=w2_s[:], start=True, stop=True)
+
+        n_units = len(UNITS)
+        last = n_units - 1
+        ok = lambda u: 0 <= u < n_units
+        queue = []
+        pending_planes, pending_rows = [], []
+        prep = {
+            0: [(1, "i")],
+            1: [(1, "q"), (2, "i")],
+            2: [(2, "q"), (3, "i")],
+            3: [(3, "q")],
+            4: [],
+            5: [],
+            6: [],
+        }
+
+        def do_prep(key, what, scalar_parts=()):
+            raw, q, sc = (w2_raw, w2_q, w2_s) if key == "w2" else (wo_raw[key], wo_q[key], wo_s[key])
+            if what == "i":
+                interleave(key, raw, scalar_parts)
+            else:
+                quant_w(key, q, sc)
+
+        do_prep("w2", "i", (2, 3))
+        do_prep("w2", "q")
+        do_prep(0, "i", (2, 3))
+        do_prep(0, "q")
+        stand_in(6)
+        nc.scalar.activation(b1c[:], b1_raw[:], ACT.Identity)
+        nc.scalar.activation(b2c[:], b2_raw[:], ACT.Identity)
+        nc.vector.tensor_copy(out=relf[:], in_=rel_raw[:])
+        permute("v", 0)
+        permute("s", 1)
+        permute("s", 2)
+        for s in range(n_units + 3):
+            planes, rows = pending_planes, pending_rows
+            pending_planes, pending_rows = [], []
+            now = queue[:1]
+            queue = queue[1:]
+            if ok(s - 3):
+                rd_k(s - 3)
+            if ok(s - 2):
+                leaky(s - 2)
+            if ok(s - 1):
+                tr_a(s - 1, 0)
+            if ok(s - 2):
+                tr_f(s - 2, 0)
+            todo = [(h, i) for h in range(halves(s)) for i in range(3)] if ok(s) else []
+            for h, i in todo[:3]:
+                prod(s, h, i)
+            if ok(s - 1):
+                rd_a(s - 1, 0)
+            for kind, a in now:
+                if kind == "p":
+                    mx2_planes(a, (0, 1, 2))
+                else:
+                    mx2_rows(a, (0, 1, 2))
+            if ok(s - 1) and not now and 0 < s < 7:
+                stand_in(2)
+            if ok(s - 2):
+                quant_m(s - 2)
+            for h, i in todo[3:5]:
+                prod(s, h, i)
+            if ok(s - 1):
+                tr_a(s - 1, 1)
+            if ok(s - 2):
+                tr_f(s - 2, 1)
+            for a in rows:
+                rd_t(a)
+            for a in planes:
+                group_o(a, "s")
+            if ok(s - 3):
+                times_f(s - 3, 2 if s - 3 == last else 1)
+            if ok(s - 2):
+                mx1(s - 2)
+            for kind, a in now:
+                if kind == "p":
+                    mx2_planes(a, (3,))
+                    pending_planes.append(a)
+                else:
+                    mx2_rows(a, (3,))
+                    pending_rows.append(a)
+            if ok(s - 1) and not now and 0 < s < 7:
+                stand_in(0)
+            for h, i in todo[5:]:
+                prod(s, h, i)
+            if ok(s - 3):
+                quant_p(s - 3, 2 if s - 3 == last else 1)
+                g, j = UNITS[s - 3]
+                if j == J - 1 and s - 3 < last:
+                    for a in range(GROUPS[g][0] // 128, (GROUPS[g][0] + GROUPS[g][1]) // 128):
+                        queue += [("p", a), ("r", a)]
+            for a in planes:
+                quant_o(a)
+            if ok(s - 1):
+                rd_a(s - 1, 1)
+            if s == last + 2:
+                mx2_rows(6, (0, 1), "a_ps0", 1)
+                mx2_rows(7, (0, 1), "a_ps1", 1)
+            if s == last + 3:
+                mx2_rows(6, (2,))
+                mx2_rows(7, (2,))
+            for p in prep.get(s, ()):
+                do_prep(*p)
+            if s == 0:
+                stand_in(0)
+            if s == last:
+                store_scales(0, 512, nc.sync)
+        for a in pending_planes:
+            group_o(a)
+            quant_o(a)
+        for a in pending_rows:
+            rd_t(a)
+        mx2_planes(6, (0, 1, 2, 3))
+        mx2_planes(7, (0, 1, 2, 3))
+        mx2_rows(6, (3,))
+        mx2_rows(7, (3,))
+        group_o(6, "s")
+        group_o(7)
+        rd_t(6)
+        rd_t(7, "s")
+        quant_o(6)
+        quant_o(7)
+        store_scales(512, 1024, nc.scalar)

@@ -14,9 +14,9 @@ ACT = mybir.ActivationFunctionType
 
 N, J, H, C, O = 1024, 4, 512, 512, 512
 FLOPS = 2 * N * J * H * C + 2 * N * J * C * O
-GROUPS = [(0, 256), (256, 256), (512, 256), (768, 256)]
-UNITS = [(g, j) for g in range(len(GROUPS)) for j in range(J)]
 SLOPE = 0.2
+TILES = N // 128
+UNITS = [(0, (0, 1)), (0, (2, 3))] + [(a, (0, 1, 2, 3)) for a in range(1, TILES - 1)] + [(TILES - 1, (0, 1)), (TILES - 1, (2, 3))]
 
 
 def tile_rangeviewmetakernelfourneighbour_x1_kernel(tc, rel, w1, b1, w2, b2, f, wo, out_0, out_1, out_2):
@@ -27,348 +27,278 @@ def tile_rangeviewmetakernelfourneighbour_x1_kernel(tc, rel, w1, b1, w2, b2, f, 
         psum = ctx.enter_context(tc.psum_pool(name="psum", bufs=1))
         ctx.enter_context(tc.manual_schedule())
 
-        w2_raw = keep.tile([128, 4, 512], BF16, name="w2_raw")
-        rel_raw = keep.tile([128, 8, 12], BF16, name="rel_raw")
+        rel_raw = keep.tile([128, TILES, 12], BF16, name="rel_raw")
         w1_raw = keep.tile([128, 3, 512], BF16, name="w1_raw")
         b1_raw = keep.tile([128, 4], BF16, name="b1_raw")
         b2_raw = keep.tile([128, 4], BF16, name="b2_raw")
+        w2_raw = keep.tile([128, 4, 512], BF16, name="w2_raw")
         wo_raw = [keep.tile([128, 4, 512], BF16, name=f"wo_raw{j}") for j in range(J)]
-        f_sb = [keep.tile([128, J, 512], BF16, name=f"f_sb{a}") for a in range(8)]
+        f_sb = [keep.tile([128, J, 512], BF16, name=f"f_sb{a}") for a in range(TILES)]
 
-        def load_w2():
-            nc.sync.dma_start(out=w2_raw[:], in_=w2.rearrange("(p k) c -> p k c", k=4))
-
-        def load_rel():
-            nc.sync.dma_start(out=rel_raw[:], in_=rel.rearrange("(a p) j i -> p a (j i)", p=128))
-            nc.sync.dma_start(out=b1_raw[:], in_=b1.rearrange("(p t) -> p t", t=4))
-            nc.sync.dma_start(out=b2_raw[:], in_=b2.rearrange("(p t) -> p t", t=4))
-
-        def load_w1():
-            nc.sync.dma_start(out=w1_raw[:], in_=w1.partition_broadcast(128))
-
-        def load_wo(j):
+        nc.sync.dma_start(out=w1_raw[:], in_=w1.partition_broadcast(128))
+        nc.sync.dma_start(out=rel_raw[:], in_=rel.rearrange("(a p) j i -> p a (j i)", p=128))
+        nc.sync.dma_start(out=b1_raw[:], in_=b1.rearrange("(p t) -> p t", t=4))
+        nc.sync.dma_start(out=b2_raw[:], in_=b2.rearrange("(p t) -> p t", t=4))
+        nc.sync.dma_start(out=w2_raw[:], in_=w2.rearrange("(p k) c -> p k c", k=4))
+        nc.sync.dma_start(out=f_sb[0][:], in_=f[0:128])
+        for j in range(J):
             nc.sync.dma_start(out=wo_raw[j][:], in_=wo[j].rearrange("(p k) c -> p k c", k=4))
-
-        def load_f(a):
+        for a in range(1, TILES):
             nc.sync.dma_start(out=f_sb[a][:], in_=f[a * 128 : (a + 1) * 128])
-
-        load_w2()
-        load_wo(0)
-        load_rel()
-        load_w1()
-        load_wo(1)
-        load_wo(2)
-        load_f(0)
-        load_f(1)
-        load_wo(3)
-        for a in range(2, 8):
-            load_f(a)
 
         ident = keep.tile([128, 128], F32, name="ident")
         make_identity(nc, ident[:])
 
         b1c = keep.tile([128, 4], F32, name="b1c")
         b2c = keep.tile([128, 4], F32, name="b2c")
-        relf = keep.tile([128, 8, 12], F32, name="relf")
-        w1p = keep.tile([128, 3, 4, 128], BF16, name="w1p")
+        relf = keep.tile([128, TILES, 12], F32, name="relf")
+        w1p = [keep.tile([128, 4, 128], BF16, name=f"w1p{i}") for i in range(3)]
 
-        def permute(eng, i):
-            v = w1_raw[:, i, :].rearrange("p (q t) -> p t q", t=4)
-            if eng == "v":
-                nc.vector.tensor_copy(out=w1p[:, i], in_=v)
-            else:
-                nc.scalar.copy(w1p[:, i], v)
-
-        w2_q = keep.tile([128, 512], U32, name="w2_q", align_bytes=64)
-        w2_s = keep.tile([128, 512], U8, name="w2_s", align_bytes=64)
-        wo_q = [keep.tile([128, 512], U32, name=f"wo_q{j}", align_bytes=64) for j in range(J)]
-        wo_s = [keep.tile([128, 512], U8, name=f"wo_s{j}", align_bytes=64) for j in range(J)]
+        w_q = [keep.tile([128, 512], U32, name=f"w_q{x}", align_bytes=64) for x in range(J + 1)]
+        w_s = [keep.tile([128, 512], U8, name=f"w_s{x}", align_bytes=64) for x in range(J + 1)]
+        w_raw = wo_raw + [w2_raw]
         w_grp = {}
 
-        def interleave(key, raw, on_scalar, parts=(0, 1, 2, 3)):
-            if key not in w_grp:
-                w_grp[key] = work.tile([128, 2048], BF16, name="w_grp", align_bytes=64, bufs=4)
-            dst = w_grp[key][:].rearrange("p (t m k) -> p t m k", t=4, k=4)
-            src = raw[:].rearrange("p k (m t) -> p t m k", t=4)
-            for t in parts:
-                if t in on_scalar:
-                    nc.scalar.copy(dst[:, t], src[:, t])
-                else:
-                    nc.vector.tensor_copy(out=dst[:, t], in_=src[:, t])
-
-        def quant_w(key, q, s):
-            nc.vector.quantize_mx(out=q[:].bitcast(FP8X4), scales=s[:], in_=w_grp[key][:])
-
-        prods, a_ps, a_sb, m_bf, m_q, k_ps, k_sb, f_ps, p_bf = {}, {}, {}, {}, {}, {}, {}, {}, {}
-        p_q = {}
-
-        def halves(u):
-            return GROUPS[UNITS[u][0]][1] // 128
-
-        def s_prod(u):
-            if u == 0:
-                return ((0, 1), (0, 2), (1, 1))
-            if u < 3:
-                return ()
-            return ((0, 1), (0, 2), (1, 1))
-
-        def prod(u, h, i):
-            if u not in prods:
-                prods[u] = [work.tile([128, 3, 512], F32, name=f"prod{x}", align_bytes=64) for x in range(halves(u))]
-            g, j = UNITS[u]
-            a = GROUPS[g][0] // 128 + h
-            col = relf[:, a, 3 * j + i : 3 * j + i + 1]
-            src = w1p[:, i].rearrange("p t q -> p (t q)")
-            dst = prods[u][h][:, i, :]
-            if (h, i) in s_prod(u):
-                nc.scalar.activation(dst, src, ACT.Identity, scale=col)
+        def group_w(x):
+            w_grp[x] = work.tile([128, 2048], BF16, name="w_grp", align_bytes=64)
+            dst = w_grp[x][:].rearrange("p (t m k) -> p t m k", t=4, k=4)
+            src = w_raw[x][:].rearrange("p k (m t) -> p t m k", t=4)
+            if x in ():
+                nc.scalar.copy(dst, src)
             else:
-                nc.vector.tensor_scalar(out=dst, in0=src, scalar1=col, scalar2=None, op0=ALU.mult)
+                nc.vector.tensor_copy(out=dst, in_=src)
 
-        def tr_a(u, tp):
-            bank = psum.tile([128, 2, 128 * halves(u)], F32, name=f"a_ps{tp}")
-            a_ps.setdefault(u, []).append(bank)
-            for h in range(halves(u)):
-                for tl in range(2):
-                    t = 2 * tp + tl
-                    for i in range(3):
-                        nc.tensor.matmul(bank[:, tl, h * 128 : (h + 1) * 128], lhsT=prods[u][h][:, i, t * 128 : (t + 1) * 128], rhs=ident[:], start=(i == 0), stop=(i == 2), is_transpose=True)
+        def quant_w(x):
+            nc.vector.quantize_mx(out=w_q[x][:].bitcast(FP8X4), scales=w_s[x][:], in_=w_grp[x][:])
 
-        def rd_a(u, tp):
-            if tp == 0:
-                a_sb[u] = work.tile([128, 4, 128 * halves(u)], F32, name="a_sb", align_bytes=64)
-            for tl in range(2):
-                t = 2 * tp + tl
-                nc.scalar.activation(a_sb[u][:, t, :], a_ps[u][tp][:, tl, :], ACT.Identity, bias=b1c[:, t : t + 1])
-
-        def leaky(u):
-            m_bf[u] = work.tile([128, 128 * halves(u), 4], BF16, name="m_bf", align_bytes=64)
-            a = a_sb[u][:].rearrange("p t r -> p r t")
-            nc.vector.scalar_tensor_tensor(out=m_bf[u][:], in0=a, scalar=SLOPE, in1=a, op0=ALU.mult, op1=ALU.max)
-
-        def quant_m(u):
-            rows = 128 * halves(u)
-            m_q[u] = (work.tile([128, rows], U32, name="m_q", align_bytes=64), work.tile([128, rows], U8, name="m_s", align_bytes=64))
-            nc.vector.quantize_mx(out=m_q[u][0][:].bitcast(FP8X4), scales=m_q[u][1][:], in_=m_bf[u][:].rearrange("p r t -> p (r t)"))
-
-        def mx1(u):
-            k_ps[u] = []
-            for tp in range(2):
-                bank = psum.tile([128, 2, 128 * halves(u)], F32, name=f"k_ps{tp}")
-                k_ps[u].append(bank)
-                for tl in range(2):
-                    cols = slice((2 * tp + tl) * 128, (2 * tp + tl + 1) * 128)
-                    nc.tensor.matmul_mx(bank[:, tl, :], lhsT=w2_q[:, cols].bitcast(FP8X4), lhsT_scale=w2_s[:, cols], rhs=m_q[u][0][:].bitcast(FP8X4), rhs_scale=m_q[u][1][:], start=True, stop=True)
-
-        def rd_k(u):
-            k_sb[u] = work.tile([128, 4, 128 * halves(u)], F32, name="k_sb", align_bytes=64)
-            for t in range(4):
-                nc.scalar.activation(k_sb[u][:, t, :], k_ps[u][t // 2][:, t % 2, :], ACT.Identity, bias=b2c[:, t : t + 1])
-
-        def tr_f(u, part):
-            g, j = UNITS[u]
-            if part == 0:
-                f_ps[u] = psum.tile([128, 2, 128 * halves(u)], F32, name="f_ps", bufs=2)
-            pairs = [(h, e) for h in range(halves(u)) for e in range(2)]
-            for h, e in pairs[: len(pairs) // 2] if part == 0 else pairs[len(pairs) // 2 :]:
-                words = f_sb[GROUPS[g][0] // 128 + h][:, j, :].bitcast(F32)
-                nc.tensor.transpose(f_ps[u][:, e, h * 128 : (h + 1) * 128], words[:, e : 256 : 2], ident[:])
-
-        def times_f(u, parts):
-            p_bf[u] = work.tile([128, 128 * halves(u), 4], BF16, name="p_bf", align_bytes=64)
-            rows = 128 * halves(u) // parts
-            for x in range(parts):
-                r = slice(x * rows, (x + 1) * rows)
-                for tp in range(2):
-                    fv = f_ps[u][:, tp, r].bitcast(BF16).rearrange("p (n e) -> p n e", e=2)
-                    kv = k_sb[u][:, 2 * tp : 2 * tp + 2, r].rearrange("p e n -> p n e")
-                    nc.vector.tensor_tensor(out=p_bf[u][:, r, 2 * tp : 2 * tp + 2], in0=fv, in1=kv, op=ALU.mult)
-
-        def quant_p(u, parts):
-            g, j = UNITS[u]
-            rows = GROUPS[g][1]
-            if j == 0:
-                p_q[g] = (work.tile([128, J, rows], U32, name="p_q", align_bytes=64, bufs=3), work.tile([128, J, rows], U8, name="p_s", align_bytes=64, bufs=3))
-            for x in range(parts):
-                r = slice(x * rows // parts, (x + 1) * rows // parts)
-                nc.vector.quantize_mx(out=p_q[g][0][:, j, r].bitcast(FP8X4), scales=p_q[g][1][:, j, r], in_=p_bf[u][:, r, :].rearrange("p n t -> p (n t)"))
-
-        o_ps, o_bf, t_ps = {}, {}, {}
+        prods, a_ps, a_sb, m_w, m_bf, m_q = {}, {}, {}, {}, {}, {}
+        k_ps, k_sb, f_ps, p_w, p_bf, p_q = {}, {}, {}, {}, {}, {}
+        o_ps, r_sb, o_w, t_ps, o_bf = {}, {}, {}, {}, {}
         o_q = keep.tile([128, N], U32, name="o_q", align_bytes=64)
         o_s = keep.tile([128, N], U8, name="o_s", align_bytes=64)
 
-        def group_of(a):
-            g = [x for x in range(len(GROUPS)) if GROUPS[x][0] <= a * 128][-1]
-            r = a * 128 - GROUPS[g][0]
-            return g, slice(r, r + 128)
+        def width(u):
+            return 128 * len(UNITS[u][1])
 
-        def mx2_planes(a, ts):
-            g, rows = group_of(a)
-            if a not in o_ps:
-                o_ps[a] = psum.tile([128, 4, 128], F32, name="o_ps", bufs=2)
-            for t in ts:
-                cols = slice(t * 128, (t + 1) * 128)
-                for j in range(J):
-                    nc.tensor.matmul_mx(o_ps[a][:, t, :], lhsT=wo_q[j][:, cols].bitcast(FP8X4), lhsT_scale=wo_s[j][:, cols], rhs=p_q[g][0][:, j, rows].bitcast(FP8X4), rhs_scale=p_q[g][1][:, j, rows], start=(j == 0), stop=(j == J - 1))
-
-        def mx2_rows(a, js, tag="o_ps", bufs=2):
-            g, rows = group_of(a)
-            if a not in t_ps:
-                t_ps[a] = psum.tile([128, 4, 128], F32, name=tag, bufs=bufs)
-            for j in js:
-                nc.tensor.matmul_mx(t_ps[a][:].rearrange("n t m -> n (t m)"), lhsT=p_q[g][0][:, j, rows].bitcast(FP8X4), lhsT_scale=p_q[g][1][:, j, rows], rhs=wo_q[j][:].bitcast(FP8X4), rhs_scale=wo_s[j][:], start=(j == 0), stop=(j == J - 1))
-
-        def group_o(a, eng="v"):
-            o_bf[a] = work.tile([128, 128, 4], BF16, name="o_bf", align_bytes=64)
-            src = o_ps[a][:].rearrange("p t n -> p n t")
-            if eng == "v":
-                nc.vector.tensor_copy(out=o_bf[a][:], in_=src)
+        def product(u, x, on_scalar):
+            a, js = UNITS[u]
+            jl, i = divmod(x, 3)
+            prods[u, x] = work.tile([128, 512], F32, name="prod", bufs=24)
+            col = relf[:, a, 3 * js[jl] + i : 3 * js[jl] + i + 1]
+            src = w1p[i][:].rearrange("p t m -> p (t m)")
+            if on_scalar:
+                nc.scalar.activation(prods[u, x][:], src, ACT.Identity, scale=col)
             else:
-                nc.scalar.activation(o_bf[a][:], src, ACT.Identity)
+                nc.vector.tensor_scalar(out=prods[u, x][:], in0=src, scalar1=col, scalar2=None, op0=ALU.mult)
+
+        def turn_a(u, t):
+            a_ps[u, t] = psum.tile([128, width(u)], F32, name="a_ps", bufs=3)
+            for jl in range(len(UNITS[u][1])):
+                for i in range(3):
+                    nc.tensor.matmul(a_ps[u, t][:, jl * 128 : (jl + 1) * 128], lhsT=prods[u, 3 * jl + i][:, t * 128 : (t + 1) * 128], rhs=ident[:], start=(i == 0), stop=(i == 2), is_transpose=True)
+
+        def empty_a(u, t):
+            if t % 2 == 0:
+                a_sb[u, t // 2] = work.tile([128, 2, width(u)], F32, name="a_sb", bufs=3)
+            nc.scalar.activation(a_sb[u, t // 2][:, t % 2, :], a_ps[u, t][:], ACT.Identity, bias=b1c[:, t : t + 1])
+
+        def leaky(u, h):
+            if h == 0:
+                m_w[u] = work.tile([128, 2, width(u), 2], BF16, name="m_w")
+            a = a_sb[u, h][:].rearrange("p e n -> p n e")
+            nc.vector.scalar_tensor_tensor(out=m_w[u][:, h], in0=a, scalar=SLOPE, in1=a, op0=ALU.mult, op1=ALU.max)
+
+        def join(dst, pairs, on_scalar):
+            words = pairs[:].rearrange("p h n e -> p h (n e)").bitcast(F32).rearrange("p h n -> p n h")
+            out = dst[:].bitcast(F32).rearrange("p (n h) -> p n h", h=2)
+            if on_scalar:
+                nc.scalar.copy(out, words)
+            else:
+                nc.vector.tensor_copy(out=out, in_=words)
+
+        def join_m(u):
+            m_bf[u] = work.tile([128, 4 * width(u)], BF16, name="m_bf", align_bytes=64)
+            join(m_bf[u], m_w[u], u in ())
+
+        def quant_m(u):
+            m_q[u] = (work.tile([128, width(u)], U32, name="m_q", align_bytes=64), work.tile([128, width(u)], U8, name="m_s", align_bytes=64))
+            nc.vector.quantize_mx(out=m_q[u][0][:].bitcast(FP8X4), scales=m_q[u][1][:], in_=m_bf[u][:])
+
+        def mx1(u, t):
+            k_ps[u, t] = psum.tile([128, width(u)], F32, name="k_ps", bufs=2)
+            cols = slice(t * 128, (t + 1) * 128)
+            nc.tensor.matmul_mx(k_ps[u, t][:], lhsT=w_q[J][:, cols].bitcast(FP8X4), lhsT_scale=w_s[J][:, cols], rhs=m_q[u][0][:].bitcast(FP8X4), rhs_scale=m_q[u][1][:], start=True, stop=True)
+
+        def empty_k(u, t):
+            if t % 2 == 0:
+                k_sb[u, t // 2] = work.tile([128, 2, width(u)], F32, name="k_sb", bufs=3)
+            nc.scalar.activation(k_sb[u, t // 2][:, t % 2, :], k_ps[u, t][:], ACT.Identity, bias=b2c[:, t : t + 1])
+
+        def turn_f(u, h):
+            a, js = UNITS[u]
+            f_ps[u, h] = psum.tile([128, width(u)], F32, name="f_ps", bufs=2)
+            for jl, j in enumerate(js):
+                words = f_sb[a][:, j, :].bitcast(F32)
+                nc.tensor.transpose(f_ps[u, h][:, jl * 128 : (jl + 1) * 128], words[:, h:256:2], ident[:])
+
+        def times_f(u, h):
+            if h == 0:
+                p_w[u] = work.tile([128, 2, width(u), 2], BF16, name="p_w")
+            fv = f_ps[u, h][:].bitcast(BF16).rearrange("p (n e) -> p n e", e=2)
+            nc.vector.tensor_tensor(out=p_w[u][:, h], in0=fv, in1=k_sb[u, h][:].rearrange("p e n -> p n e"), op=ALU.mult)
+
+        def join_p(u):
+            p_bf[u] = work.tile([128, 4 * width(u)], BF16, name="p_bf", align_bytes=64)
+            join(p_bf[u], p_w[u], u in ())
+
+        def quant_p(u):
+            p_q[u] = (work.tile([128, width(u)], U32, name="p_q", align_bytes=64, bufs=3), work.tile([128, width(u)], U8, name="p_s", align_bytes=64, bufs=3))
+            nc.vector.quantize_mx(out=p_q[u][0][:].bitcast(FP8X4), scales=p_q[u][1][:], in_=p_bf[u][:])
+
+        def mx2(u, part):
+            a, js = UNITS[u]
+            half = len(js) // 2
+            for jl in range(part * half, (part + 1) * half):
+                j = js[jl]
+                if j == 0:
+                    o_ps[a] = psum.tile([128, 512], F32, name="o_ps")
+                cols = slice(jl * 128, (jl + 1) * 128)
+                nc.tensor.matmul_mx(o_ps[a][:], lhsT=p_q[u][0][:, cols].bitcast(FP8X4), lhsT_scale=p_q[u][1][:, cols], rhs=w_q[j][:].bitcast(FP8X4), rhs_scale=w_s[j][:], start=(j == 0), stop=(j == J - 1))
+
+        def empty_o(a):
+            r_sb[a] = work.tile([128, 512], F32, name="r_sb")
+            nc.scalar.activation(r_sb[a][:].rearrange("n (m t) -> n m t", t=4), o_ps[a][:].rearrange("n (t m) -> n m t", t=4), ACT.Identity)
+            nc.sync.dma_start(out=out_0[a * 128 : (a + 1) * 128, :], in_=r_sb[a][:])
+
+        def mx2_turned(u, part):
+            a = UNITS[u][0]
+            if UNITS[u][1][-1] != J - 1:
+                return
+            if part == 0:
+                t_ps[a] = psum.tile([128, 4, 128], F32, name="a_ps", bufs=3)
+            passes = [(v, jl, j) for v in range(len(UNITS)) if UNITS[v][0] == a for jl, j in enumerate(UNITS[v][1])]
+            for t in (2 * part, 2 * part + 1):
+                cols = slice(t * 128, (t + 1) * 128)
+                for v, jl, j in passes:
+                    rows = slice(jl * 128, (jl + 1) * 128)
+                    nc.tensor.matmul_mx(t_ps[a][:, t, :], lhsT=w_q[j][:, cols].bitcast(FP8X4), lhsT_scale=w_s[j][:, cols], rhs=p_q[v][0][:, rows].bitcast(FP8X4), rhs_scale=p_q[v][1][:, rows], start=(j == 0), stop=(j == J - 1))
+
+        def empty_turned(a):
+            o_bf[a] = work.tile([128, 512], BF16, name="o_bf", align_bytes=64)
+            nc.scalar.activation(o_bf[a][:].rearrange("p (n t) -> p n t", t=4), t_ps[a][:].rearrange("p t n -> p n t"), ACT.Identity)
+
+        def round_o(a):
+            o_w[a] = work.tile([128, 2, 128, 2], BF16, name="o_w")
+            nc.vector.tensor_copy(out=o_w[a][:], in_=r_sb[a][:].rearrange("n (m h e) -> n h m e", h=2, e=2))
+
+        def turn_o(a):
+            t_ps[a] = psum.tile([128, 2, 128], F32, name="a_ps", bufs=3)
+            words = o_w[a][:].rearrange("n h m e -> n h (m e)").bitcast(F32)
+            for h in range(2):
+                nc.tensor.transpose(t_ps[a][:, h, :], words[:, h, :], ident[:])
+
+        def empty_t(a):
+            o_bf[a] = work.tile([128, 512], BF16, name="o_bf", align_bytes=64)
+            nc.scalar.copy(o_bf[a][:].bitcast(F32).rearrange("p (n h) -> p n h", h=2), t_ps[a][:].rearrange("p h n -> p n h"))
 
         def quant_o(a):
             cols = slice(a * 128, (a + 1) * 128)
-            nc.vector.quantize_mx(out=o_q[:, cols].bitcast(FP8X4), scales=o_s[:, cols], in_=o_bf[a][:].rearrange("p n t -> p (n t)"))
+            nc.vector.quantize_mx(out=o_q[:, cols].bitcast(FP8X4), scales=o_s[:, cols], in_=o_bf[a][:])
             nc.sync.dma_start(out=out_1[0, :, cols, :].rearrange("p m t -> p (m t)").bitcast(I32), in_=o_q[:, cols].bitcast(I32))
 
-        def store_scales(c0, c1, queue):
+        def store_scales(c0, c1):
             for q in range(4):
-                queue.dma_start(out=out_2[0, 4 * q : 4 * q + 4, c0:c1].bitcast(I32), in_=o_s[32 * q : 32 * q + 4, c0:c1].bitcast(I32))
-
-        def rd_t(a, eng="s"):
-            r = work.tile([128, 128, 4], F32, name="r_sb", align_bytes=64)
-            src = t_ps[a][:].rearrange("n t m -> n m t")
-            if eng == "v":
-                nc.vector.tensor_copy(out=r[:], in_=src)
-            else:
-                nc.scalar.activation(r[:], src, ACT.Identity)
-            nc.sync.dma_start(out=out_0[a * 128 : (a + 1) * 128, :], in_=r[:].rearrange("n m t -> n (m t)"))
-
-        def stand_in(n):
-            bank = psum.tile([128, 512], F32, name="o_ps", bufs=2)
-            for r in range(n):
-                nc.tensor.matmul_mx(bank[:], lhsT=w2_q[:, 0:128].bitcast(FP8X4), lhsT_scale=w2_s[:, 0:128], rhs=w2_q[:].bitcast(FP8X4), rhs_scale=w2_s[:], start=True, stop=True)
+                nc.sync.dma_start(out=out_2[0, 4 * q : 4 * q + 4, c0:c1].bitcast(I32), in_=o_s[32 * q : 32 * q + 4, c0:c1].bitcast(I32))
 
         n_units = len(UNITS)
-        last = n_units - 1
-        ok = lambda u: 0 <= u < n_units
-        queue = []
-        pending_planes, pending_rows = [], []
-        prep = {
-            0: [(1, "i")],
-            1: [(1, "q"), (2, "i")],
-            2: [(2, "q"), (3, "i")],
-            3: [(3, "q")],
-            4: [],
-            5: [],
-            6: [],
-        }
 
-        def do_prep(key, what, scalar_parts=()):
-            raw, q, sc = (w2_raw, w2_q, w2_s) if key == "w2" else (wo_raw[key], wo_q[key], wo_s[key])
-            if what == "i":
-                interleave(key, raw, scalar_parts)
+        def on(fn, u, *args):
+            if 0 <= u < n_units:
+                fn(u, *args)
+
+        def on_tile(fn, u):
+            if 0 <= u < n_units and UNITS[u][1][-1] == J - 1:
+                fn(UNITS[u][0])
+
+        def products(u, xs, on_scalar):
+            if 0 <= u < n_units:
+                for x in xs:
+                    if x < 3 * len(UNITS[u][1]):
+                        product(u, x, on_scalar)
+
+        nc.vector.tensor_copy(out=relf[:], in_=rel_raw[:])
+        for i in range(3):
+            src = w1_raw[:, i, :].rearrange("p (m t) -> p t m", t=4)
+            if i == 1:
+                nc.scalar.copy(w1p[i][:], src)
             else:
-                quant_w(key, q, sc)
-
-        do_prep("w2", "i", (2, 3))
-        do_prep("w2", "q")
-        do_prep(0, "i", (2, 3))
-        do_prep(0, "q")
-        stand_in(6)
+                nc.vector.tensor_copy(out=w1p[i][:], in_=src)
         nc.scalar.activation(b1c[:], b1_raw[:], ACT.Identity)
         nc.scalar.activation(b2c[:], b2_raw[:], ACT.Identity)
-        nc.vector.tensor_copy(out=relf[:], in_=rel_raw[:])
-        permute("v", 0)
-        permute("s", 1)
-        permute("s", 2)
-        for s in range(n_units + 3):
-            planes, rows = pending_planes, pending_rows
-            pending_planes, pending_rows = [], []
-            now = queue[:1]
-            queue = queue[1:]
-            if ok(s - 3):
-                rd_k(s - 3)
-            if ok(s - 2):
-                leaky(s - 2)
-            if ok(s - 1):
-                tr_a(s - 1, 0)
-            if ok(s - 2):
-                tr_f(s - 2, 0)
-            todo = [(h, i) for h in range(halves(s)) for i in range(3)] if ok(s) else []
-            for h, i in todo[:3]:
-                prod(s, h, i)
-            if ok(s - 1):
-                rd_a(s - 1, 0)
-            for kind, a in now:
-                if kind == "p":
-                    mx2_planes(a, (0, 1, 2))
-                else:
-                    mx2_rows(a, (0, 1, 2))
-            if ok(s - 1) and not now and 0 < s < 7:
-                stand_in(2)
-            if ok(s - 2):
-                quant_m(s - 2)
-            for h, i in todo[3:5]:
-                prod(s, h, i)
-            if ok(s - 1):
-                tr_a(s - 1, 1)
-            if ok(s - 2):
-                tr_f(s - 2, 1)
-            for a in rows:
-                rd_t(a)
-            for a in planes:
-                group_o(a, "s")
-            if ok(s - 3):
-                times_f(s - 3, 2 if s - 3 == last else 1)
-            if ok(s - 2):
-                mx1(s - 2)
-            for kind, a in now:
-                if kind == "p":
-                    mx2_planes(a, (3,))
-                    pending_planes.append(a)
-                else:
-                    mx2_rows(a, (3,))
-                    pending_rows.append(a)
-            if ok(s - 1) and not now and 0 < s < 7:
-                stand_in(0)
-            for h, i in todo[5:]:
-                prod(s, h, i)
-            if ok(s - 3):
-                quant_p(s - 3, 2 if s - 3 == last else 1)
-                g, j = UNITS[s - 3]
-                if j == J - 1 and s - 3 < last:
-                    for a in range(GROUPS[g][0] // 128, (GROUPS[g][0] + GROUPS[g][1]) // 128):
-                        queue += [("p", a), ("r", a)]
-            for a in planes:
-                quant_o(a)
-            if ok(s - 1):
-                rd_a(s - 1, 1)
-            if s == last + 2:
-                mx2_rows(6, (0, 1), "a_ps0", 1)
-                mx2_rows(7, (0, 1), "a_ps1", 1)
-            if s == last + 3:
-                mx2_rows(6, (2,))
-                mx2_rows(7, (2,))
-            for p in prep.get(s, ()):
-                do_prep(*p)
-            if s == 0:
-                stand_in(0)
-            if s == last:
-                store_scales(0, 512, nc.sync)
-        for a in pending_planes:
-            group_o(a)
-            quant_o(a)
-        for a in pending_rows:
-            rd_t(a)
-        mx2_planes(6, (0, 1, 2, 3))
-        mx2_planes(7, (0, 1, 2, 3))
-        mx2_rows(6, (3,))
-        mx2_rows(7, (3,))
-        group_o(6, "s")
-        group_o(7)
-        rd_t(6)
-        rd_t(7, "s")
-        quant_o(6)
-        quant_o(7)
-        store_scales(512, 1024, nc.scalar)
+        products(0, (0, 2, 3, 5), False)
+        products(0, (1, 4), True)
+        prep = {0: [J], 1: [0, 1], 2: [2, 3]}
+        last = n_units - 1
+        for s in range(n_units + 4):
+            mine = (3 if s < 3 else 6)
+            on_v = (0, 3, 6, 9, 5, 11, 8)[:mine]
+            on_s = [x for x in (1, 4, 0, 2, 3, 5, 6, 7, 8, 9, 10, 11) if x not in on_v]
+            on(turn_a, s, 0)
+            on(leaky, s - 1, 1)
+            products(s + 1, on_v[:1], False)
+            products(s + 1, on_s[:2], True)
+            on(mx2, s - 3, 0)
+            if s - 3 == last:
+                mx2(last, 1)
+                mx2_turned(last, 0)
+                mx2_turned(last, 1)
+                empty_turned(TILES - 1)
+                empty_o(TILES - 1)
+                quant_o(TILES - 2)
+                quant_o(TILES - 1)
+                break
+            on(turn_a, s, 1)
+            on(join_m, s - 1)
+            on(empty_a, s, 0)
+            on(times_f, s - 2, 1)
+            on(quant_m, s - 1)
+            on_tile(turn_o, s - 4)
+            on(mx2, s - 3, 1)
+            on(turn_f, s - 1, 0)
+            products(s + 1, on_s[2:3], True)
+            on(empty_a, s, 1)
+            on_tile(empty_t, s - 4)
+            on(turn_a, s, 2)
+            on(join_p, s - 2)
+            for x in prep.get(s, ()):
+                group_w(x)
+            on(leaky, s, 0)
+            on_tile(empty_o, s - 3)
+            on(mx1, s - 1, 0)
+            on(mx1, s - 1, 1)
+            on(turn_a, s, 3)
+            on(quant_p, s - 2)
+            products(s + 1, on_v[1:2], False)
+            for x in prep.get(s, ()):
+                quant_w(x)
+            products(s + 1, on_s[3:4], True)
+            on(empty_a, s, 2)
+            on(empty_k, s - 1, 0)
+            on(empty_k, s - 1, 1)
+            on(mx1, s - 1, 2)
+            on(mx1, s - 1, 3)
+            on(turn_f, s - 1, 1)
+            if s - 4 != last - 2:
+                on_tile(quant_o, s - 4)
+            products(s + 1, on_v[2:4], False)
+            on_tile(round_o, s - 3)
+            products(s + 1, on_v[4:], False)
+            products(s + 1, on_s[4:5], True)
+            on(empty_a, s, 3)
+            products(s + 1, on_s[5:], True)
+            on(times_f, s - 1, 0)
+            on(empty_k, s - 1, 2)
+            on(empty_k, s - 1, 3)
+            if s == n_units:
+                store_scales(0, 512)
+        store_scales(512, 1024)

@@ -16,7 +16,7 @@ N, J, H, C, O = 1024, 4, 512, 512, 512
 FLOPS = 2 * N * J * H * C + 2 * N * J * C * O
 SLOPE = 0.2
 TILES = N // 128
-UNITS = [(0, (0, 1)), (0, (2, 3))] + [(a, (0, 1, 2, 3)) for a in range(1, TILES - 1)] + [(TILES - 1, (0, 1)), (TILES - 1, (2, 3))]
+UNITS = [(a, (0, 1, 2, 3)) for a in range(0, TILES - 1)] + [(TILES - 1, (0, 1)), (TILES - 1, (2, 3))]
 
 
 def tile_rangeviewmetakernelfourneighbour_x1_kernel(tc, rel, w1, b1, w2, b2, f, wo, out_0, out_1, out_2):
@@ -40,10 +40,9 @@ def tile_rangeviewmetakernelfourneighbour_x1_kernel(tc, rel, w1, b1, w2, b2, f, 
         nc.sync.dma_start(out=b1_raw[:], in_=b1.rearrange("(p t) -> p t", t=4))
         nc.sync.dma_start(out=b2_raw[:], in_=b2.rearrange("(p t) -> p t", t=4))
         nc.sync.dma_start(out=w2_raw[:], in_=w2.rearrange("(p k) c -> p k c", k=4))
-        nc.sync.dma_start(out=f_sb[0][:], in_=f[0:128])
         for j in range(J):
             nc.sync.dma_start(out=wo_raw[j][:], in_=wo[j].rearrange("(p k) c -> p k c", k=4))
-        for a in range(1, TILES):
+        for a in range(TILES):
             nc.sync.dma_start(out=f_sb[a][:], in_=f[a * 128 : (a + 1) * 128])
 
         ident = keep.tile([128, 128], F32, name="ident")
@@ -60,7 +59,7 @@ def tile_rangeviewmetakernelfourneighbour_x1_kernel(tc, rel, w1, b1, w2, b2, f, 
         w_grp = {}
 
         def group_w(x):
-            w_grp[x] = work.tile([128, 2048], BF16, name="w_grp", align_bytes=64)
+            w_grp[x] = work.tile([128, 2048], BF16, name="w_grp", align_bytes=64, bufs=3)
             dst = w_grp[x][:].rearrange("p (t m k) -> p t m k", t=4, k=4)
             src = w_raw[x][:].rearrange("p k (m t) -> p t m k", t=4)
             if x in ():
@@ -86,10 +85,19 @@ def tile_rangeviewmetakernelfourneighbour_x1_kernel(tc, rel, w1, b1, w2, b2, f, 
             prods[u, x] = work.tile([128, 512], F32, name="prod", bufs=24)
             col = relf[:, a, 3 * js[jl] + i : 3 * js[jl] + i + 1]
             src = w1p[i][:].rearrange("p t m -> p (t m)")
-            if on_scalar:
+            if on_scalar == "g":
+                nc.gpsimd.tensor_scalar(out=prods[u, x][:], in0=src, scalar1=late[u][:, x : x + 1], scalar2=0.0, op0=ALU.mult, op1=ALU.add)
+            elif on_scalar:
                 nc.scalar.activation(prods[u, x][:], src, ACT.Identity, scale=col)
             else:
                 nc.vector.tensor_scalar(out=prods[u, x][:], in0=src, scalar1=col, scalar2=None, op0=ALU.mult)
+
+        late = {}
+
+        def cast_rel(u):
+            a, js = UNITS[u]
+            late[u] = work.tile([128, 3 * len(js)], F32, name="late")
+            nc.vector.tensor_copy(out=late[u][:], in_=rel_raw[:, a, 3 * js[0] : 3 * js[-1] + 3])
 
         def turn_a(u, t):
             a_ps[u, t] = psum.tile([128, width(u)], F32, name="a_ps", bufs=3)
@@ -235,23 +243,37 @@ def tile_rangeviewmetakernelfourneighbour_x1_kernel(tc, rel, w1, b1, w2, b2, f, 
                 nc.vector.tensor_copy(out=w1p[i][:], in_=src)
         nc.scalar.activation(b1c[:], b1_raw[:], ACT.Identity)
         nc.scalar.activation(b2c[:], b2_raw[:], ACT.Identity)
-        products(0, (0, 2, 3, 5), False)
-        products(0, (1, 4), True)
-        prep = {0: [J], 1: [0, 1], 2: [2, 3]}
+        products(0, (0, 2, 3, 5, 6, 8, 9, 11), False)
+        products(0, (1, 4, 7, 10), True)
         last = n_units - 1
         for s in range(n_units + 4):
-            mine = (3 if s < 3 else 6)
-            on_v = (0, 3, 6, 9, 5, 11, 8)[:mine]
-            on_s = [x for x in (1, 4, 0, 2, 3, 5, 6, 7, 8, 9, 10, 11) if x not in on_v]
+            n_g = 3 if s >= 2 else 0
+            n_v = {0: 3, 1: 5, 6: 0, 7: 0}.get(s, 4)
+            count = 3 * len(UNITS[s + 1][1]) if s < last else 0
+            todo = list(range(count))
+            on_g = todo[2 : 2 + n_g]
+            todo = [x for x in todo if x not in on_g]
+            on_v = todo[:1][:n_v] + todo[1:][::-1][: max(n_v - 1, 0)][::-1]
+            on_s = [x for x in todo if x not in on_v]
             on(turn_a, s, 0)
             on(leaky, s - 1, 1)
+            if s == 0:
+                group_w(J)
+                group_w(0)
+                quant_w(J)
+                quant_w(0)
+            if s == 1:
+                quant_w(2)
             products(s + 1, on_v[:1], False)
-            products(s + 1, on_s[:2], True)
+            on(empty_k, s - 2, 3)
+            products(s + 1, on_s[:1], True)
+            if on_g:
+                cast_rel(s + 1)
             on(mx2, s - 3, 0)
             if s - 3 == last:
-                mx2(last, 1)
                 mx2_turned(last, 0)
                 mx2_turned(last, 1)
+                mx2(last, 1)
                 empty_turned(TILES - 1)
                 empty_o(TILES - 1)
                 quant_o(TILES - 2)
@@ -259,46 +281,48 @@ def tile_rangeviewmetakernelfourneighbour_x1_kernel(tc, rel, w1, b1, w2, b2, f, 
                 break
             on(turn_a, s, 1)
             on(join_m, s - 1)
+            products(s + 1, on_g, "g")
             on(empty_a, s, 0)
+            if s == 1:
+                group_w(3)
+            on(times_f, s - 2, 0)
             on(times_f, s - 2, 1)
             on(quant_m, s - 1)
             on_tile(turn_o, s - 4)
             on(mx2, s - 3, 1)
-            on(turn_f, s - 1, 0)
-            products(s + 1, on_s[2:3], True)
+            products(s + 1, on_s[1:3], True)
             on(empty_a, s, 1)
             on_tile(empty_t, s - 4)
             on(turn_a, s, 2)
+            on(turn_f, s - 1, 0)
             on(join_p, s - 2)
-            for x in prep.get(s, ()):
-                group_w(x)
+            if s == 0:
+                group_w(1)
+            if s == 1:
+                quant_w(3)
             on(leaky, s, 0)
             on_tile(empty_o, s - 3)
             on(mx1, s - 1, 0)
             on(mx1, s - 1, 1)
             on(turn_a, s, 3)
             on(quant_p, s - 2)
-            products(s + 1, on_v[1:2], False)
-            for x in prep.get(s, ()):
-                quant_w(x)
+            if s == 0:
+                quant_w(1)
+                group_w(2)
             products(s + 1, on_s[3:4], True)
             on(empty_a, s, 2)
+            products(s + 1, on_s[4:], True)
+            products(s + 1, on_v[1:], False)
             on(empty_k, s - 1, 0)
             on(empty_k, s - 1, 1)
             on(mx1, s - 1, 2)
             on(mx1, s - 1, 3)
             on(turn_f, s - 1, 1)
+            on_tile(round_o, s - 3)
             if s - 4 != last - 2:
                 on_tile(quant_o, s - 4)
-            products(s + 1, on_v[2:4], False)
-            on_tile(round_o, s - 3)
-            products(s + 1, on_v[4:], False)
-            products(s + 1, on_s[4:5], True)
             on(empty_a, s, 3)
-            products(s + 1, on_s[5:], True)
-            on(times_f, s - 1, 0)
             on(empty_k, s - 1, 2)
-            on(empty_k, s - 1, 3)
             if s == n_units:
                 store_scales(0, 512)
         store_scales(512, 1024)

@@ -106,15 +106,17 @@ def tile_rangeviewmetakernelfourneighbour_x1_kernel(tc, rel, w1, b1, w2, b2, f, 
                     nc.tensor.matmul(a_ps[u, t][:, jl * 128 : (jl + 1) * 128], lhsT=prods[u, 3 * jl + i][:, t * 128 : (t + 1) * 128], rhs=ident[:], start=(i == 0), stop=(i == 2), is_transpose=True)
 
         def empty_a(u, t):
-            if t % 2 == 0:
-                a_sb[u, t // 2] = work.tile([128, 2, width(u)], F32, name="a_sb", bufs=3)
-            nc.scalar.activation(a_sb[u, t // 2][:, t % 2, :], a_ps[u, t][:], ACT.Identity, bias=b1c[:, t : t + 1])
+            if t == 0:
+                a_sb[u] = work.tile([128, width(u) // 4, 4, 4], F32, name="a_sb")
+            nc.scalar.activation(a_sb[u][:, :, t, :], a_ps[u, t][:].rearrange("p (q n) -> p n q", q=4), ACT.Identity, bias=b1c[:, t : t + 1])
 
         def leaky(u, h):
             if h == 0:
-                m_w[u] = work.tile([128, 2, width(u), 2], BF16, name="m_w")
-            a = a_sb[u, h][:].rearrange("p e n -> p n e")
-            nc.vector.scalar_tensor_tensor(out=m_w[u][:, h], in0=a, scalar=SLOPE, in1=a, op0=ALU.mult, op1=ALU.max)
+                m_bf[u] = work.tile([128, 4 * width(u)], BF16, name="m_bf", align_bytes=64)
+            half = slice(h * width(u) // 2, (h + 1) * width(u) // 2)
+            a = a_sb[u][:].rearrange("p n t q -> p (n t) q")[:, half, :]
+            out = m_bf[u][:].rearrange("p (q x) -> p x q", q=4)[:, half, :]
+            nc.vector.scalar_tensor_tensor(out=out, in0=a, scalar=SLOPE, in1=a, op0=ALU.mult, op1=ALU.max)
 
         def join(dst, pairs, on_scalar):
             words = pairs[:].rearrange("p h n e -> p h (n e)").bitcast(F32).rearrange("p h n -> p n h")
@@ -139,8 +141,8 @@ def tile_rangeviewmetakernelfourneighbour_x1_kernel(tc, rel, w1, b1, w2, b2, f, 
 
         def empty_k(u, t):
             if t % 2 == 0:
-                k_sb[u, t // 2] = work.tile([128, 2, width(u)], F32, name="k_sb", bufs=3)
-            nc.scalar.activation(k_sb[u, t // 2][:, t % 2, :], k_ps[u, t][:], ACT.Identity, bias=b2c[:, t : t + 1])
+                k_sb[u, t // 2] = work.tile([128, width(u) // 4, 2, 4], F32, name="k_sb", bufs=3)
+            nc.scalar.activation(k_sb[u, t // 2][:, :, t % 2, :], k_ps[u, t][:].rearrange("p (q n) -> p n q", q=4), ACT.Identity, bias=b2c[:, t : t + 1])
 
         def turn_f(u, h):
             a, js = UNITS[u]
@@ -152,8 +154,9 @@ def tile_rangeviewmetakernelfourneighbour_x1_kernel(tc, rel, w1, b1, w2, b2, f, 
         def times_f(u, h):
             if h == 0:
                 p_w[u] = work.tile([128, 2, width(u), 2], BF16, name="p_w")
-            fv = f_ps[u, h][:].bitcast(BF16).rearrange("p (n e) -> p n e", e=2)
-            nc.vector.tensor_tensor(out=p_w[u][:, h], in0=fv, in1=k_sb[u, h][:].rearrange("p e n -> p n e"), op=ALU.mult)
+            fv = f_ps[u, h][:].bitcast(BF16).rearrange("p (q x) -> p x q", q=4)
+            out = p_w[u][:, h].rearrange("p n e -> p (n e)").rearrange("p (q x) -> p x q", q=4)
+            nc.vector.tensor_tensor(out=out, in0=fv, in1=k_sb[u, h][:].rearrange("p n e q -> p (n e) q"), op=ALU.mult)
 
         def join_p(u):
             p_bf[u] = work.tile([128, 4 * width(u)], BF16, name="p_bf", align_bytes=64)
@@ -246,29 +249,30 @@ def tile_rangeviewmetakernelfourneighbour_x1_kernel(tc, rel, w1, b1, w2, b2, f, 
         products(0, (0, 2, 3, 5, 6, 8, 9, 11), False)
         products(0, (1, 4, 7, 10), True)
         last = n_units - 1
+
+        def shares(u):
+            todo = list(range(3 * len(UNITS[u][1]))) if 0 < u <= last else []
+            early, on_g, on_v = {1: (3, 0, 1), 2: (2, 0, 4), 7: (1, 3, 0), 8: (0, 3, 0)}.get(u, (2, 3, 3))
+            return todo[:early], todo[early : early + on_g], todo[early + on_g : early + on_g + on_v], todo[early + on_g + on_v :]
+
+        products(1, shares(1)[0], False)
+        turn_a(0, 0)
         for s in range(n_units + 4):
-            n_g = 3 if s >= 2 else 0
-            n_v = {0: 3, 1: 5, 6: 0, 7: 0}.get(s, 4)
-            count = 3 * len(UNITS[s + 1][1]) if s < last else 0
-            todo = list(range(count))
-            on_g = todo[2 : 2 + n_g]
-            todo = [x for x in todo if x not in on_g]
-            on_v = todo[:1][:n_v] + todo[1:][::-1][: max(n_v - 1, 0)][::-1]
-            on_s = [x for x in todo if x not in on_v]
-            on(turn_a, s, 0)
+            early, on_g, on_v, on_s = shares(s + 1)
+            on(turn_a, s, 1)
+            on(leaky, s - 1, 0)
             on(leaky, s - 1, 1)
             if s == 0:
                 group_w(J)
                 group_w(0)
                 quant_w(J)
                 quant_w(0)
-            if s == 1:
-                quant_w(2)
+            on(empty_a, s, 0)
             products(s + 1, on_v[:1], False)
-            on(empty_k, s - 2, 3)
-            products(s + 1, on_s[:1], True)
+            on_tile(quant_o, s - 5)
             if on_g:
                 cast_rel(s + 1)
+            products(s + 1, on_s[:1], True)
             on(mx2, s - 3, 0)
             if s - 3 == last:
                 mx2_turned(last, 0)
@@ -276,53 +280,50 @@ def tile_rangeviewmetakernelfourneighbour_x1_kernel(tc, rel, w1, b1, w2, b2, f, 
                 mx2(last, 1)
                 empty_turned(TILES - 1)
                 empty_o(TILES - 1)
-                quant_o(TILES - 2)
                 quant_o(TILES - 1)
                 break
-            on(turn_a, s, 1)
-            on(join_m, s - 1)
+            on(empty_a, s, 1)
+            on(turn_a, s, 2)
+            on(quant_m, s - 1)
             products(s + 1, on_g, "g")
-            on(empty_a, s, 0)
             if s == 1:
                 group_w(3)
+                quant_w(2)
             on(times_f, s - 2, 0)
             on(times_f, s - 2, 1)
-            on(quant_m, s - 1)
             on_tile(turn_o, s - 4)
             on(mx2, s - 3, 1)
-            products(s + 1, on_s[1:3], True)
-            on(empty_a, s, 1)
+            on(mx1, s - 1, 0)
+            on(mx1, s - 1, 1)
+            products(s + 1, on_s[1:2], True)
+            on(empty_a, s, 2)
             on_tile(empty_t, s - 4)
-            on(turn_a, s, 2)
+            on(turn_a, s, 3)
             on(turn_f, s - 1, 0)
+            products(s + 1, on_v[1:2], False)
             on(join_p, s - 2)
             if s == 0:
                 group_w(1)
+                group_w(2)
+                quant_w(1)
             if s == 1:
                 quant_w(3)
-            on(leaky, s, 0)
-            on_tile(empty_o, s - 3)
-            on(mx1, s - 1, 0)
-            on(mx1, s - 1, 1)
-            on(turn_a, s, 3)
-            on(quant_p, s - 2)
-            if s == 0:
-                quant_w(1)
-                group_w(2)
-            products(s + 1, on_s[3:4], True)
-            on(empty_a, s, 2)
-            products(s + 1, on_s[4:], True)
-            products(s + 1, on_v[1:], False)
+            products(s + 1, on_s[2:3], True)
             on(empty_k, s - 1, 0)
             on(empty_k, s - 1, 1)
             on(mx1, s - 1, 2)
             on(mx1, s - 1, 3)
-            on(turn_f, s - 1, 1)
-            on_tile(round_o, s - 3)
-            if s - 4 != last - 2:
-                on_tile(quant_o, s - 4)
+            products(s + 1, on_v[2:], False)
+            on(quant_p, s - 2)
             on(empty_a, s, 3)
+            products(s + 1, on_s[3:], True)
+            on(turn_f, s - 1, 1)
+            on(turn_a, s + 1, 0)
+            on_tile(empty_o, s - 3)
+            products(s + 2, shares(s + 2)[0], False)
             on(empty_k, s - 1, 2)
+            on(empty_k, s - 1, 3)
+            on_tile(round_o, s - 3)
             if s == n_units:
                 store_scales(0, 512)
         store_scales(512, 1024)

@@ -16,7 +16,8 @@ N, J, H, C, O = 1024, 4, 512, 512, 512
 FLOPS = 2 * N * J * H * C + 2 * N * J * C * O
 SLOPE = 0.2
 TILES = N // 128
-UNITS = [(a, (0, 1, 2, 3)) for a in range(0, TILES - 1)] + [(TILES - 1, (0, 1)), (TILES - 1, (2, 3))]
+LAST = TILES - 1
+W2 = J
 
 
 def tile_rangeviewmetakernelfourneighbour_x1_kernel(tc, rel, w1, b1, w2, b2, f, wo, out_0, out_1, out_2):
@@ -31,17 +32,16 @@ def tile_rangeviewmetakernelfourneighbour_x1_kernel(tc, rel, w1, b1, w2, b2, f, 
         w1_raw = keep.tile([128, 3, 512], BF16, name="w1_raw")
         b1_raw = keep.tile([128, 4], BF16, name="b1_raw")
         b2_raw = keep.tile([128, 4], BF16, name="b2_raw")
-        w2_raw = keep.tile([128, 4, 512], BF16, name="w2_raw")
-        wo_raw = [keep.tile([128, 4, 512], BF16, name=f"wo_raw{j}") for j in range(J)]
+        w_raw = [keep.tile([128, 4, 512], BF16, name=f"w_raw{x}") for x in range(J + 1)]
         f_sb = [keep.tile([128, J, 512], BF16, name=f"f_sb{a}") for a in range(TILES)]
 
         nc.sync.dma_start(out=w1_raw[:], in_=w1.partition_broadcast(128))
         nc.sync.dma_start(out=rel_raw[:], in_=rel.rearrange("(a p) j i -> p a (j i)", p=128))
         nc.sync.dma_start(out=b1_raw[:], in_=b1.rearrange("(p t) -> p t", t=4))
         nc.sync.dma_start(out=b2_raw[:], in_=b2.rearrange("(p t) -> p t", t=4))
-        nc.sync.dma_start(out=w2_raw[:], in_=w2.rearrange("(p k) c -> p k c", k=4))
+        nc.sync.dma_start(out=w_raw[W2][:], in_=w2.rearrange("(p k) c -> p k c", k=4))
         for j in range(J):
-            nc.sync.dma_start(out=wo_raw[j][:], in_=wo[j].rearrange("(p k) c -> p k c", k=4))
+            nc.sync.dma_start(out=w_raw[j][:], in_=wo[j].rearrange("(p k) c -> p k c", k=4))
         for a in range(TILES):
             nc.sync.dma_start(out=f_sb[a][:], in_=f[a * 128 : (a + 1) * 128])
 
@@ -52,155 +52,133 @@ def tile_rangeviewmetakernelfourneighbour_x1_kernel(tc, rel, w1, b1, w2, b2, f, 
         b2c = keep.tile([128, 4], F32, name="b2c")
         relf = keep.tile([128, TILES, 12], F32, name="relf")
         w1p = [keep.tile([128, 4, 128], BF16, name=f"w1p{i}") for i in range(3)]
-
         w_q = [keep.tile([128, 512], U32, name=f"w_q{x}", align_bytes=64) for x in range(J + 1)]
         w_s = [keep.tile([128, 512], U8, name=f"w_s{x}", align_bytes=64) for x in range(J + 1)]
-        w_raw = wo_raw + [w2_raw]
-        w_grp = {}
+        o_q = keep.tile([128, N], U32, name="o_q", align_bytes=64)
+        o_s = keep.tile([128, N], U8, name="o_s", align_bytes=64)
+
+        w_grp, rel_g, prods, a_ps, a_sb, m_bf, m_q = {}, {}, {}, {}, {}, {}, {}
+        k_ps, k_sb, f_ps, p_w, p_bf, p_q = {}, {}, {}, {}, {}, {}
+        o_ps, r_sb, o_w, t_ps, o_bf = {}, {}, {}, {}, {}
 
         def group_w(x):
             w_grp[x] = work.tile([128, 2048], BF16, name="w_grp", align_bytes=64, bufs=3)
             dst = w_grp[x][:].rearrange("p (t m k) -> p t m k", t=4, k=4)
-            src = w_raw[x][:].rearrange("p k (m t) -> p t m k", t=4)
-            if x in ():
-                nc.scalar.copy(dst, src)
-            else:
-                nc.vector.tensor_copy(out=dst, in_=src)
+            nc.vector.tensor_copy(out=dst, in_=w_raw[x][:].rearrange("p k (m t) -> p t m k", t=4))
 
         def quant_w(x):
             nc.vector.quantize_mx(out=w_q[x][:].bitcast(FP8X4), scales=w_s[x][:], in_=w_grp[x][:])
 
-        prods, a_ps, a_sb, m_w, m_bf, m_q = {}, {}, {}, {}, {}, {}
-        k_ps, k_sb, f_ps, p_w, p_bf, p_q = {}, {}, {}, {}, {}, {}
-        o_ps, r_sb, o_w, t_ps, o_bf = {}, {}, {}, {}, {}
-        o_q = keep.tile([128, N], U32, name="o_q", align_bytes=64)
-        o_s = keep.tile([128, N], U8, name="o_s", align_bytes=64)
+        def cast_rel(a):
+            rel_g[a] = work.tile([128, 12], F32, name="rel_g")
+            nc.vector.tensor_copy(out=rel_g[a][:], in_=rel_raw[:, a, :])
 
-        def width(u):
-            return 128 * len(UNITS[u][1])
+        def products(a, xs, engine):
+            for x in xs:
+                prods[a, x] = work.tile([128, 512], F32, name="prod", bufs=24)
+                src = w1p[x % 3][:].rearrange("p t m -> p (t m)")
+                if engine == "gpsimd":
+                    nc.gpsimd.tensor_scalar(out=prods[a, x][:], in0=src, scalar1=rel_g[a][:, x : x + 1], scalar2=0.0, op0=ALU.mult, op1=ALU.add)
+                elif engine == "scalar":
+                    nc.scalar.activation(prods[a, x][:], src, ACT.Identity, scale=relf[:, a, x : x + 1])
+                else:
+                    nc.vector.tensor_scalar(out=prods[a, x][:], in0=src, scalar1=relf[:, a, x : x + 1], scalar2=None, op0=ALU.mult)
 
-        def product(u, x, on_scalar):
-            a, js = UNITS[u]
-            jl, i = divmod(x, 3)
-            prods[u, x] = work.tile([128, 512], F32, name="prod", bufs=24)
-            col = relf[:, a, 3 * js[jl] + i : 3 * js[jl] + i + 1]
-            src = w1p[i][:].rearrange("p t m -> p (t m)")
-            if on_scalar == "g":
-                nc.gpsimd.tensor_scalar(out=prods[u, x][:], in0=src, scalar1=late[u][:, x : x + 1], scalar2=0.0, op0=ALU.mult, op1=ALU.add)
-            elif on_scalar:
-                nc.scalar.activation(prods[u, x][:], src, ACT.Identity, scale=col)
-            else:
-                nc.vector.tensor_scalar(out=prods[u, x][:], in0=src, scalar1=col, scalar2=None, op0=ALU.mult)
-
-        late = {}
-
-        def cast_rel(u):
-            a, js = UNITS[u]
-            late[u] = work.tile([128, 3 * len(js)], F32, name="late")
-            nc.vector.tensor_copy(out=late[u][:], in_=rel_raw[:, a, 3 * js[0] : 3 * js[-1] + 3])
-
-        def turn_a(u, t):
-            a_ps[u, t] = psum.tile([128, width(u)], F32, name="a_ps", bufs=3)
-            for jl in range(len(UNITS[u][1])):
+        def turn_a(a, t):
+            a_ps[a, t] = psum.tile([128, 512], F32, name="a_ps", bufs=3)
+            for j in range(J):
                 for i in range(3):
-                    nc.tensor.matmul(a_ps[u, t][:, jl * 128 : (jl + 1) * 128], lhsT=prods[u, 3 * jl + i][:, t * 128 : (t + 1) * 128], rhs=ident[:], start=(i == 0), stop=(i == 2), is_transpose=True)
+                    nc.tensor.matmul(a_ps[a, t][:, j * 128 : (j + 1) * 128], lhsT=prods[a, 3 * j + i][:, t * 128 : (t + 1) * 128], rhs=ident[:], start=(i == 0), stop=(i == 2), is_transpose=True)
 
-        def empty_a(u, t):
+        def empty_a(a, t):
             if t == 0:
-                a_sb[u] = work.tile([128, width(u) // 4, 4, 4], F32, name="a_sb")
-            nc.scalar.activation(a_sb[u][:, :, t, :], a_ps[u, t][:].rearrange("p (q n) -> p n q", q=4), ACT.Identity, bias=b1c[:, t : t + 1])
+                a_sb[a] = work.tile([128, 128, 4, J], F32, name="a_sb")
+            nc.scalar.activation(a_sb[a][:, :, t, :], a_ps[a, t][:].rearrange("p (j n) -> p n j", j=J), ACT.Identity, bias=b1c[:, t : t + 1])
 
-        def leaky(u, h):
-            if h == 0:
-                m_bf[u] = work.tile([128, 4 * width(u)], BF16, name="m_bf", align_bytes=64)
-            half = slice(h * width(u) // 2, (h + 1) * width(u) // 2)
-            a = a_sb[u][:].rearrange("p n t q -> p (n t) q")[:, half, :]
-            out = m_bf[u][:].rearrange("p (q x) -> p x q", q=4)[:, half, :]
-            nc.vector.scalar_tensor_tensor(out=out, in0=a, scalar=SLOPE, in1=a, op0=ALU.mult, op1=ALU.max)
+        def leaky(a):
+            m_bf[a] = work.tile([128, 2048], BF16, name="m_bf", align_bytes=64)
+            src = a_sb[a][:].rearrange("p n t j -> p (n t) j")
+            nc.vector.scalar_tensor_tensor(out=m_bf[a][:].rearrange("p (j x) -> p x j", j=J), in0=src, scalar=SLOPE, in1=src, op0=ALU.mult, op1=ALU.max)
 
-        def join(dst, pairs, on_scalar):
-            words = pairs[:].rearrange("p h n e -> p h (n e)").bitcast(F32).rearrange("p h n -> p n h")
-            out = dst[:].bitcast(F32).rearrange("p (n h) -> p n h", h=2)
-            if on_scalar:
+        def quant_m(a):
+            m_q[a] = (work.tile([128, 512], U32, name="m_q", align_bytes=64), work.tile([128, 512], U8, name="m_s", align_bytes=64))
+            nc.vector.quantize_mx(out=m_q[a][0][:].bitcast(FP8X4), scales=m_q[a][1][:], in_=m_bf[a][:])
+
+        def mx1(a, t, tag="k_ps", bufs=2):
+            k_ps[a, t] = psum.tile([128, 512], F32, name=tag, bufs=bufs)
+            cols = slice(t * 128, (t + 1) * 128)
+            nc.tensor.matmul_mx(k_ps[a, t][:], lhsT=w_q[W2][:, cols].bitcast(FP8X4), lhsT_scale=w_s[W2][:, cols], rhs=m_q[a][0][:].bitcast(FP8X4), rhs_scale=m_q[a][1][:], start=True, stop=True)
+
+        def empty_k(a, t):
+            if t % 2 == 0:
+                k_sb[a, t // 2] = work.tile([128, 128, 2, 4], F32, name="k_sb", bufs=3)
+            nc.scalar.activation(k_sb[a, t // 2][:, :, t % 2, :], k_ps[a, t][:].rearrange("p (n i) -> p n i", i=4), ACT.Identity, bias=b2c[:, t : t + 1])
+
+        def turn_f(a, h):
+            f_ps[a, h] = psum.tile([128, 512], F32, name="f_ps", bufs=2)
+            for j in range(J):
+                words = f_sb[a][:, j, :].bitcast(F32)
+                nc.tensor.transpose(f_ps[a, h][:, j * 128 : (j + 1) * 128], words[:, h:256:2], ident[:])
+
+        def times_f(a, h, j0=0, j1=J):
+            if a not in p_w:
+                p_w[a] = work.tile([128, 2, 512, 2], BF16, name="p_w")
+            fv = f_ps[a, h][:, j0 * 128 : j1 * 128].bitcast(BF16).rearrange("p (n i e) -> p n e i", i=4, e=2)
+            out = p_w[a][:, h, j0 * 128 : j1 * 128, :].rearrange("p (n i) e -> p n e i", i=4)
+            nc.vector.tensor_tensor(out=out, in0=fv, in1=k_sb[a, h][:, j0 * 32 : j1 * 32], op=ALU.mult)
+
+        def join_p(a, engine, j0=0, j1=J):
+            if a not in p_bf:
+                p_bf[a] = work.tile([128, 2048], BF16, name="p_bf", align_bytes=64)
+            words = p_w[a][:].rearrange("p h n e -> p h (n e)").bitcast(F32)[:, :, j0 * 128 : j1 * 128].rearrange("p h n -> p n h")
+            out = p_bf[a][:, j0 * 512 : j1 * 512].bitcast(F32).rearrange("p (n h) -> p n h", h=2)
+            if engine == "scalar":
                 nc.scalar.copy(out, words)
             else:
                 nc.vector.tensor_copy(out=out, in_=words)
 
-        def join_m(u):
-            m_bf[u] = work.tile([128, 4 * width(u)], BF16, name="m_bf", align_bytes=64)
-            join(m_bf[u], m_w[u], u in ())
+        def quant_p(a, j0=0, j1=J):
+            if a not in p_q:
+                p_q[a] = (work.tile([128, 512], U32, name="p_q", align_bytes=64, bufs=3), work.tile([128, 512], U8, name="p_s", align_bytes=64, bufs=3))
+            cols = slice(j0 * 128, j1 * 128)
+            nc.vector.quantize_mx(out=p_q[a][0][:, cols].bitcast(FP8X4), scales=p_q[a][1][:, cols], in_=p_bf[a][:, j0 * 512 : j1 * 512])
 
-        def quant_m(u):
-            m_q[u] = (work.tile([128, width(u)], U32, name="m_q", align_bytes=64), work.tile([128, width(u)], U8, name="m_s", align_bytes=64))
-            nc.vector.quantize_mx(out=m_q[u][0][:].bitcast(FP8X4), scales=m_q[u][1][:], in_=m_bf[u][:])
-
-        def mx1(u, t):
-            k_ps[u, t] = psum.tile([128, width(u)], F32, name="k_ps", bufs=2)
-            cols = slice(t * 128, (t + 1) * 128)
-            nc.tensor.matmul_mx(k_ps[u, t][:], lhsT=w_q[J][:, cols].bitcast(FP8X4), lhsT_scale=w_s[J][:, cols], rhs=m_q[u][0][:].bitcast(FP8X4), rhs_scale=m_q[u][1][:], start=True, stop=True)
-
-        def empty_k(u, t):
-            if t % 2 == 0:
-                k_sb[u, t // 2] = work.tile([128, width(u) // 4, 2, 4], F32, name="k_sb", bufs=3)
-            nc.scalar.activation(k_sb[u, t // 2][:, :, t % 2, :], k_ps[u, t][:].rearrange("p (q n) -> p n q", q=4), ACT.Identity, bias=b2c[:, t : t + 1])
-
-        def turn_f(u, h):
-            a, js = UNITS[u]
-            f_ps[u, h] = psum.tile([128, width(u)], F32, name="f_ps", bufs=2)
-            for jl, j in enumerate(js):
-                words = f_sb[a][:, j, :].bitcast(F32)
-                nc.tensor.transpose(f_ps[u, h][:, jl * 128 : (jl + 1) * 128], words[:, h:256:2], ident[:])
-
-        def times_f(u, h):
-            if h == 0:
-                p_w[u] = work.tile([128, 2, width(u), 2], BF16, name="p_w")
-            fv = f_ps[u, h][:].bitcast(BF16).rearrange("p (q x) -> p x q", q=4)
-            out = p_w[u][:, h].rearrange("p n e -> p (n e)").rearrange("p (q x) -> p x q", q=4)
-            nc.vector.tensor_tensor(out=out, in0=fv, in1=k_sb[u, h][:].rearrange("p n e q -> p (n e) q"), op=ALU.mult)
-
-        def join_p(u):
-            p_bf[u] = work.tile([128, 4 * width(u)], BF16, name="p_bf", align_bytes=64)
-            join(p_bf[u], p_w[u], u in ())
-
-        def quant_p(u):
-            p_q[u] = (work.tile([128, width(u)], U32, name="p_q", align_bytes=64, bufs=3), work.tile([128, width(u)], U8, name="p_s", align_bytes=64, bufs=3))
-            nc.vector.quantize_mx(out=p_q[u][0][:].bitcast(FP8X4), scales=p_q[u][1][:], in_=p_bf[u][:])
-
-        def mx2(u, part):
-            a, js = UNITS[u]
-            half = len(js) // 2
-            for jl in range(part * half, (part + 1) * half):
-                j = js[jl]
+        def mx2(a, j0, j1):
+            for j in range(j0, j1):
                 if j == 0:
-                    o_ps[a] = psum.tile([128, 512], F32, name="o_ps")
-                cols = slice(jl * 128, (jl + 1) * 128)
-                nc.tensor.matmul_mx(o_ps[a][:], lhsT=p_q[u][0][:, cols].bitcast(FP8X4), lhsT_scale=p_q[u][1][:, cols], rhs=w_q[j][:].bitcast(FP8X4), rhs_scale=w_s[j][:], start=(j == 0), stop=(j == J - 1))
+                    o_ps[a] = psum.tile([128, 512], F32, name="k_ps", bufs=2) if a == LAST else psum.tile([128, 512], F32, name="o_ps")
+                cols = slice(j * 128, (j + 1) * 128)
+                nc.tensor.matmul_mx(o_ps[a][:], lhsT=p_q[a][0][:, cols].bitcast(FP8X4), lhsT_scale=p_q[a][1][:, cols], rhs=w_q[j][:].bitcast(FP8X4), rhs_scale=w_s[j][:], start=(j == 0), stop=(j == J - 1))
+
+        def mx2_turned(a, j0, j1):
+            for j in range(j0, j1):
+                if j == 0:
+                    t_ps[a] = psum.tile([128, 4, 128], F32, name="a_ps", bufs=3)
+                rows = slice(j * 128, (j + 1) * 128)
+                for t in range(4):
+                    cols = slice(t * 128, (t + 1) * 128)
+                    nc.tensor.matmul_mx(t_ps[a][:, t, :], lhsT=w_q[j][:, cols].bitcast(FP8X4), lhsT_scale=w_s[j][:, cols], rhs=p_q[a][0][:, rows].bitcast(FP8X4), rhs_scale=p_q[a][1][:, rows], start=(j == 0 and t == 0), stop=(j == J - 1 and t == 3))
+
+        def empty_turned(a, engine):
+            o_bf[a] = work.tile([128, 512], BF16, name="o_bf", align_bytes=64)
+            out, src = o_bf[a][:].rearrange("p (n t) -> p n t", t=4), t_ps[a][:].rearrange("p t n -> p n t")
+            if engine == "scalar":
+                nc.scalar.activation(out, src, ACT.Identity)
+            else:
+                nc.vector.tensor_copy(out=out, in_=src)
 
         def empty_o(a):
             r_sb[a] = work.tile([128, 512], F32, name="r_sb")
             nc.scalar.activation(r_sb[a][:].rearrange("n (m t) -> n m t", t=4), o_ps[a][:].rearrange("n (t m) -> n m t", t=4), ACT.Identity)
             nc.sync.dma_start(out=out_0[a * 128 : (a + 1) * 128, :], in_=r_sb[a][:])
 
-        def mx2_turned(u, part):
-            a = UNITS[u][0]
-            if UNITS[u][1][-1] != J - 1:
-                return
-            if part == 0:
-                t_ps[a] = psum.tile([128, 4, 128], F32, name="a_ps", bufs=3)
-            passes = [(v, jl, j) for v in range(len(UNITS)) if UNITS[v][0] == a for jl, j in enumerate(UNITS[v][1])]
-            for t in (2 * part, 2 * part + 1):
-                cols = slice(t * 128, (t + 1) * 128)
-                for v, jl, j in passes:
-                    rows = slice(jl * 128, (jl + 1) * 128)
-                    nc.tensor.matmul_mx(t_ps[a][:, t, :], lhsT=w_q[j][:, cols].bitcast(FP8X4), lhsT_scale=w_s[j][:, cols], rhs=p_q[v][0][:, rows].bitcast(FP8X4), rhs_scale=p_q[v][1][:, rows], start=(j == 0), stop=(j == J - 1))
-
-        def empty_turned(a):
-            o_bf[a] = work.tile([128, 512], BF16, name="o_bf", align_bytes=64)
-            nc.scalar.activation(o_bf[a][:].rearrange("p (n t) -> p n t", t=4), t_ps[a][:].rearrange("p t n -> p n t"), ACT.Identity)
-
-        def round_o(a):
+        def round_o(a, engine):
             o_w[a] = work.tile([128, 2, 128, 2], BF16, name="o_w")
-            nc.vector.tensor_copy(out=o_w[a][:], in_=r_sb[a][:].rearrange("n (m h e) -> n h m e", h=2, e=2))
+            src = r_sb[a][:].rearrange("n (m h e) -> n h m e", h=2, e=2)
+            if engine == "scalar":
+                nc.scalar.activation(o_w[a][:], src, ACT.Identity)
+            else:
+                nc.vector.tensor_copy(out=o_w[a][:], in_=src)
 
         def turn_o(a):
             t_ps[a] = psum.tile([128, 2, 128], F32, name="a_ps", bufs=3)
@@ -217,25 +195,18 @@ def tile_rangeviewmetakernelfourneighbour_x1_kernel(tc, rel, w1, b1, w2, b2, f, 
             nc.vector.quantize_mx(out=o_q[:, cols].bitcast(FP8X4), scales=o_s[:, cols], in_=o_bf[a][:])
             nc.sync.dma_start(out=out_1[0, :, cols, :].rearrange("p m t -> p (m t)").bitcast(I32), in_=o_q[:, cols].bitcast(I32))
 
-        def store_scales(c0, c1):
+        def store_scales(c0, c1, queue):
             for q in range(4):
-                nc.sync.dma_start(out=out_2[0, 4 * q : 4 * q + 4, c0:c1].bitcast(I32), in_=o_s[32 * q : 32 * q + 4, c0:c1].bitcast(I32))
+                queue.dma_start(out=out_2[0, 4 * q : 4 * q + 4, c0:c1].bitcast(I32), in_=o_s[32 * q : 32 * q + 4, c0:c1].bitcast(I32))
 
-        n_units = len(UNITS)
+        def on(fn, a, *args):
+            if a >= 0:
+                fn(a, *args)
 
-        def on(fn, u, *args):
-            if 0 <= u < n_units:
-                fn(u, *args)
-
-        def on_tile(fn, u):
-            if 0 <= u < n_units and UNITS[u][1][-1] == J - 1:
-                fn(UNITS[u][0])
-
-        def products(u, xs, on_scalar):
-            if 0 <= u < n_units:
-                for x in xs:
-                    if x < 3 * len(UNITS[u][1]):
-                        product(u, x, on_scalar)
+        def shares(a):
+            early, n_g, n_v = {1: (3, 0, 1), 2: (2, 0, 3)}.get(a, (1, 3, 3))
+            xs = list(range(12)) if a <= LAST else []
+            return xs[:early], xs[early : early + n_g], xs[early + n_g : early + n_g + n_v], xs[early + n_g + n_v :]
 
         nc.vector.tensor_copy(out=relf[:], in_=rel_raw[:])
         for i in range(3):
@@ -246,84 +217,140 @@ def tile_rangeviewmetakernelfourneighbour_x1_kernel(tc, rel, w1, b1, w2, b2, f, 
                 nc.vector.tensor_copy(out=w1p[i][:], in_=src)
         nc.scalar.activation(b1c[:], b1_raw[:], ACT.Identity)
         nc.scalar.activation(b2c[:], b2_raw[:], ACT.Identity)
-        products(0, (0, 2, 3, 5, 6, 8, 9, 11), False)
-        products(0, (1, 4, 7, 10), True)
-        last = n_units - 1
-
-        def shares(u):
-            todo = list(range(3 * len(UNITS[u][1]))) if 0 < u <= last else []
-            early, on_g, on_v = {1: (3, 0, 1), 2: (2, 0, 4), 7: (1, 3, 0), 8: (0, 3, 0)}.get(u, (2, 3, 3))
-            return todo[:early], todo[early : early + on_g], todo[early + on_g : early + on_g + on_v], todo[early + on_g + on_v :]
-
-        products(1, shares(1)[0], False)
+        products(0, (0, 2, 3, 5, 6, 8, 9, 11), "vector")
+        products(0, (1, 4, 7, 10), "scalar")
+        products(1, shares(1)[0], "vector")
         turn_a(0, 0)
-        for s in range(n_units + 4):
+        for s in range(LAST):
             early, on_g, on_v, on_s = shares(s + 1)
-            on(turn_a, s, 1)
-            on(leaky, s - 1, 0)
-            on(leaky, s - 1, 1)
+            turn_a(s, 1)
+            on(leaky, s - 1)
             if s == 0:
-                group_w(J)
+                group_w(W2)
                 group_w(0)
-                quant_w(J)
+                quant_w(W2)
                 quant_w(0)
-            on(empty_a, s, 0)
-            products(s + 1, on_v[:1], False)
-            on_tile(quant_o, s - 5)
+            empty_a(s, 0)
+            products(s + 1, on_v[:1], "vector")
+            on(quant_o, s - 5)
             if on_g:
                 cast_rel(s + 1)
-            products(s + 1, on_s[:1], True)
-            on(mx2, s - 3, 0)
-            if s - 3 == last:
-                mx2_turned(last, 0)
-                mx2_turned(last, 1)
-                mx2(last, 1)
-                empty_turned(TILES - 1)
-                empty_o(TILES - 1)
-                quant_o(TILES - 1)
-                break
-            on(empty_a, s, 1)
-            on(turn_a, s, 2)
+            products(s + 1, on_s[:1], "scalar")
+            on(mx2, s - 3, 0, 2)
+            empty_a(s, 1)
+            turn_a(s, 2)
             on(quant_m, s - 1)
-            products(s + 1, on_g, "g")
+            products(s + 1, on_g, "gpsimd")
             if s == 1:
                 group_w(3)
                 quant_w(2)
             on(times_f, s - 2, 0)
             on(times_f, s - 2, 1)
-            on_tile(turn_o, s - 4)
-            on(mx2, s - 3, 1)
+            on(turn_o, s - 4)
+            on(mx2, s - 3, 2, 4)
             on(mx1, s - 1, 0)
             on(mx1, s - 1, 1)
-            products(s + 1, on_s[1:2], True)
-            on(empty_a, s, 2)
-            on_tile(empty_t, s - 4)
-            on(turn_a, s, 3)
+            products(s + 1, on_s[1:3], "scalar")
+            empty_a(s, 2)
+            on(empty_t, s - 4)
+            turn_a(s, 3)
             on(turn_f, s - 1, 0)
-            products(s + 1, on_v[1:2], False)
-            on(join_p, s - 2)
+            products(s + 1, on_v[1:2], "vector")
+            on(join_p, s - 2, "vector")
             if s == 0:
                 group_w(1)
                 group_w(2)
                 quant_w(1)
             if s == 1:
                 quant_w(3)
-            products(s + 1, on_s[2:3], True)
+            products(s + 1, on_s[3:4], "scalar")
             on(empty_k, s - 1, 0)
             on(empty_k, s - 1, 1)
             on(mx1, s - 1, 2)
             on(mx1, s - 1, 3)
-            products(s + 1, on_v[2:], False)
+            products(s + 1, on_v[2:], "vector")
             on(quant_p, s - 2)
-            on(empty_a, s, 3)
-            products(s + 1, on_s[3:], True)
+            empty_a(s, 3)
+            products(s + 1, on_s[4:], "scalar")
             on(turn_f, s - 1, 1)
-            on(turn_a, s + 1, 0)
-            on_tile(empty_o, s - 3)
-            products(s + 2, shares(s + 2)[0], False)
+            turn_a(s + 1, 0)
+            on(empty_o, s - 3)
+            products(s + 2, shares(s + 2)[0], "vector")
             on(empty_k, s - 1, 2)
             on(empty_k, s - 1, 3)
-            on_tile(round_o, s - 3)
-            if s == n_units:
-                store_scales(0, 512)
-        store_scales(512, 1024)
+            on(round_o, s - 3, "vector")
+        a = LAST
+        turn_a(a, 1)
+        leaky(a - 1)
+        empty_a(a, 0)
+        turn_a(a, 2)
+        empty_a(a, 1)
+        turn_a(a, 3)
+        mx2(a - 3, 0, 4)
+        quant_o(a - 5)
+        quant_m(a - 1)
+        empty_a(a, 2)
+        times_f(a - 2, 0)
+        times_f(a - 2, 1)
+        mx1(a - 1, 0)
+        mx1(a - 1, 1)
+        empty_a(a, 3)
+        turn_o(a - 4)
+        turn_f(a - 1, 0)
+        empty_k(a - 1, 0)
+        empty_k(a - 1, 1)
+        mx1(a - 1, 2)
+        mx1(a - 1, 3)
+        turn_f(a - 1, 1)
+        leaky(a)
+        join_p(a - 2, "scalar")
+        empty_k(a - 1, 2)
+        empty_k(a - 1, 3)
+        empty_o(a - 3)
+        empty_t(a - 4)
+        quant_p(a - 2)
+        quant_m(a)
+        mx2_turned(a - 3, 0, 4)
+        mx2(a - 2, 0, 4)
+        mx1(a, 0)
+        mx1(a, 1)
+        mx1(a, 2, "a_ps", 3)
+        mx1(a, 3, "a_ps", 3)
+        times_f(a - 1, 0)
+        quant_o(a - 4)
+        times_f(a - 1, 1)
+        empty_turned(a - 3, "scalar")
+        empty_k(a, 0)
+        empty_k(a, 1)
+        turn_f(a, 0)
+        mx2_turned(a - 2, 0, 4)
+        empty_k(a, 2)
+        empty_k(a, 3)
+        turn_f(a, 1)
+        quant_o(a - 3)
+        join_p(a - 1, "vector")
+        empty_o(a - 2)
+        empty_turned(a - 2, "scalar")
+        times_f(a, 0)
+        store_scales(0, 512, nc.sync)
+        quant_p(a - 1)
+        times_f(a, 1, 0, 2)
+        mx2_turned(a - 1, 0, 4)
+        mx2(a - 1, 0, 4)
+        quant_o(a - 2)
+        join_p(a, "vector", 0, 2)
+        times_f(a, 1, 2, 4)
+        quant_p(a, 0, 2)
+        join_p(a, "vector", 2, 4)
+        empty_turned(a - 1, "scalar")
+        empty_o(a - 1)
+        mx2(a, 0, 2)
+        mx2_turned(a, 0, 2)
+        quant_o(a - 1)
+        quant_p(a, 2, 4)
+        mx2_turned(a, 2, 4)
+        mx2(a, 2, 4)
+        empty_turned(a, "vector")
+        empty_o(a)
+        quant_o(a)
+        store_scales(512, 1024, nc.scalar)

@@ -28,18 +28,23 @@ def tile_rangeviewmetakernelfourneighbour_x1_kernel(tc, rel, w1, b1, w2, b2, f, 
         psum = ctx.enter_context(tc.psum_pool(name="psum", bufs=1))
         ctx.enter_context(tc.manual_schedule())
 
-        rel_raw = keep.tile([128, TILES, 12], BF16, name="rel_raw")
-        w1_raw = keep.tile([128, 3, 512], BF16, name="w1_raw")
+        rel_0 = keep.tile([128, 12], BF16, name="rel_0")
+        rel_raw = keep.tile([128, TILES, 16], BF16, name="rel_raw")
+        w1_raw = [keep.tile([128, 512], BF16, name=f"w1_raw{i}") for i in range(3)]
         b1_raw = keep.tile([128, 4], BF16, name="b1_raw")
         b2_raw = keep.tile([128, 4], BF16, name="b2_raw")
         w_raw = [keep.tile([128, 4, 512], BF16, name=f"w_raw{x}") for x in range(J + 1)]
         f_sb = [keep.tile([128, J, 512], BF16, name=f"f_sb{a}") for a in range(TILES)]
 
-        nc.sync.dma_start(out=w1_raw[:], in_=w1.partition_broadcast(128))
-        nc.sync.dma_start(out=rel_raw[:], in_=rel.rearrange("(a p) j i -> p a (j i)", p=128))
+        rel_rows = rel.rearrange("(a p) j i -> p a (j i)", p=128)
+        nc.sync.dma_start(out=w1_raw[0][:], in_=w1[0].partition_broadcast(128))
+        nc.sync.dma_start(out=rel_0[:], in_=rel_rows[:, 0, :])
+        nc.sync.dma_start(out=w1_raw[1][:], in_=w1[1].partition_broadcast(128))
+        nc.sync.dma_start(out=w1_raw[2][:], in_=w1[2].partition_broadcast(128))
+        nc.sync.dma_start(out=rel_raw[:, 1:, 0:12], in_=rel_rows[:, 1:, :])
         nc.sync.dma_start(out=b1_raw[:], in_=b1.rearrange("(p t) -> p t", t=4))
-        nc.sync.dma_start(out=b2_raw[:], in_=b2.rearrange("(p t) -> p t", t=4))
         nc.sync.dma_start(out=w_raw[W2][:], in_=w2.rearrange("(p k) c -> p k c", k=4))
+        nc.sync.dma_start(out=b2_raw[:], in_=b2.rearrange("(p t) -> p t", t=4))
         for j in range(J):
             nc.sync.dma_start(out=w_raw[j][:], in_=wo[j].rearrange("(p k) c -> p k c", k=4))
         for a in range(TILES):
@@ -71,7 +76,7 @@ def tile_rangeviewmetakernelfourneighbour_x1_kernel(tc, rel, w1, b1, w2, b2, f, 
 
         def cast_rel(a):
             rel_g[a] = work.tile([128, 12], F32, name="rel_g")
-            nc.vector.tensor_copy(out=rel_g[a][:], in_=rel_raw[:, a, :])
+            nc.vector.tensor_copy(out=rel_g[a][:], in_=rel_raw[:, a, 0:12])
 
         def products(a, xs, engine):
             for x in xs:
@@ -204,32 +209,76 @@ def tile_rangeviewmetakernelfourneighbour_x1_kernel(tc, rel, w1, b1, w2, b2, f, 
                 fn(a, *args)
 
         def shares(a):
-            early, n_g, n_v = {1: (3, 0, 1), 2: (2, 0, 3)}.get(a, (1, 3, 3))
+            early, n_g, n_v = (2, 3, 3)
             xs = list(range(12)) if a <= LAST else []
             return xs[:early], xs[early : early + n_g], xs[early + n_g : early + n_g + n_v], xs[early + n_g + n_v :]
 
-        nc.vector.tensor_copy(out=relf[:], in_=rel_raw[:])
+        nc.vector.tensor_copy(out=relf[:, 0, :], in_=rel_0[:])
         for i in range(3):
-            src = w1_raw[:, i, :].rearrange("p (m t) -> p t m", t=4)
+            src = w1_raw[i][:].rearrange("p (m t) -> p t m", t=4)
             if i == 1:
                 nc.scalar.copy(w1p[i][:], src)
             else:
                 nc.vector.tensor_copy(out=w1p[i][:], in_=src)
-        nc.scalar.activation(b1c[:], b1_raw[:], ACT.Identity)
-        nc.scalar.activation(b2c[:], b2_raw[:], ACT.Identity)
         products(0, (0, 2, 3, 5, 6, 8, 9, 11), "vector")
         products(0, (1, 4, 7, 10), "scalar")
-        products(1, shares(1)[0], "vector")
+        nc.vector.tensor_copy(out=relf[:, 1:, :], in_=rel_raw[:, 1:, 0:12])
+        nc.scalar.activation(b1c[:], b1_raw[:], ACT.Identity)
         turn_a(0, 0)
-        for s in range(LAST):
+        turn_a(0, 1)
+        group_w(W2)
+        products(1, range(0, 1), "vector")
+        quant_w(W2)
+        products(1, range(1, 6), "vector")
+        products(1, range(6, 7), "scalar")
+        empty_a(0, 0)
+        products(1, range(7, 9), "scalar")
+        empty_a(0, 1)
+        turn_a(0, 2)
+        turn_a(0, 3)
+        products(1, range(9, 11), "scalar")
+        empty_a(0, 2)
+        products(1, range(11, 12), "scalar")
+        empty_a(0, 3)
+        nc.scalar.activation(b2c[:], b2_raw[:], ACT.Identity)
+        group_w(0)
+        group_w(1)
+        quant_w(0)
+        turn_a(1, 0)
+        turn_a(1, 1)
+        leaky(0)
+        quant_w(1)
+        quant_m(0)
+        empty_a(1, 0)
+        products(2, range(7, 8), "scalar")
+        empty_a(1, 1)
+        turn_a(1, 2)
+        products(2, range(8, 9), "scalar")
+        mx1(0, 0)
+        mx1(0, 1)
+        empty_a(1, 2)
+        turn_a(1, 3)
+        turn_f(0, 0)
+        products(2, range(0, 7), "vector")
+        group_w(2)
+        empty_k(0, 0)
+        empty_k(0, 1)
+        mx1(0, 2)
+        mx1(0, 3)
+        empty_a(1, 3)
+        products(2, range(9, 12), "scalar")
+        turn_f(0, 1)
+        turn_a(2, 0)
+        products(3, shares(3)[0], "vector")
+        quant_w(2)
+        empty_k(0, 2)
+        empty_k(0, 3)
+        for s in range(2, LAST):
             early, on_g, on_v, on_s = shares(s + 1)
             turn_a(s, 1)
             on(leaky, s - 1)
-            if s == 0:
-                group_w(W2)
-                group_w(0)
-                quant_w(W2)
-                quant_w(0)
+            if s == 2:
+                group_w(3)
             empty_a(s, 0)
             products(s + 1, on_v[:1], "vector")
             on(quant_o, s - 5)
@@ -241,29 +290,22 @@ def tile_rangeviewmetakernelfourneighbour_x1_kernel(tc, rel, w1, b1, w2, b2, f, 
             turn_a(s, 2)
             on(quant_m, s - 1)
             products(s + 1, on_g, "gpsimd")
-            if s == 1:
-                group_w(3)
-                quant_w(2)
             on(times_f, s - 2, 0)
             on(times_f, s - 2, 1)
             on(turn_o, s - 4)
             on(mx2, s - 3, 2, 4)
             on(mx1, s - 1, 0)
             on(mx1, s - 1, 1)
-            products(s + 1, on_s[1:3], "scalar")
+            products(s + 1, on_s[1:2], "scalar")
             empty_a(s, 2)
             on(empty_t, s - 4)
             turn_a(s, 3)
             on(turn_f, s - 1, 0)
             products(s + 1, on_v[1:2], "vector")
             on(join_p, s - 2, "vector")
-            if s == 0:
-                group_w(1)
-                group_w(2)
-                quant_w(1)
-            if s == 1:
+            if s == 2:
                 quant_w(3)
-            products(s + 1, on_s[3:4], "scalar")
+            products(s + 1, on_s[2:3], "scalar")
             on(empty_k, s - 1, 0)
             on(empty_k, s - 1, 1)
             on(mx1, s - 1, 2)
@@ -271,7 +313,7 @@ def tile_rangeviewmetakernelfourneighbour_x1_kernel(tc, rel, w1, b1, w2, b2, f, 
             products(s + 1, on_v[2:], "vector")
             on(quant_p, s - 2)
             empty_a(s, 3)
-            products(s + 1, on_s[4:], "scalar")
+            products(s + 1, on_s[3:], "scalar")
             on(turn_f, s - 1, 1)
             turn_a(s + 1, 0)
             on(empty_o, s - 3)

@@ -78,11 +78,16 @@ def tile_rangeviewmetakernelfourneighbour_x1_kernel(tc, rel, w1, b1, w2, b2, f, 
             rel_g[a] = work.tile([128, 12], F32, name="rel_g")
             nc.vector.tensor_copy(out=rel_g[a][:], in_=rel_raw[:, a, 0:12])
 
+        def fused(a):
+            return (5, 8) if a > 2 else ()
+
         def products(a, xs, engine):
             for x in xs:
                 prods[a, x] = work.tile([128, 512], F32, name="prod", bufs=24)
                 src = w1p[x % 3][:].rearrange("p t m -> p (t m)")
-                if engine == "gpsimd":
+                if x in fused(a):
+                    nc.vector.scalar_tensor_tensor(out=prods[a, x][:], in0=src, scalar=relf[:, a, x : x + 1], in1=prods[a, x - 1][:], op0=ALU.mult, op1=ALU.add)
+                elif engine == "gpsimd":
                     nc.gpsimd.tensor_scalar(out=prods[a, x][:], in0=src, scalar1=rel_g[a][:, x : x + 1], scalar2=0.0, op0=ALU.mult, op1=ALU.add)
                 elif engine == "scalar":
                     nc.scalar.activation(prods[a, x][:], src, ACT.Identity, scale=relf[:, a, x : x + 1])
@@ -92,7 +97,7 @@ def tile_rangeviewmetakernelfourneighbour_x1_kernel(tc, rel, w1, b1, w2, b2, f, 
         def turn_a(a, t):
             a_ps[a, t] = psum.tile([128, 512], F32, name="a_ps", bufs=3)
             for j in range(J):
-                for i in range(3):
+                for i in (0, 2) if 3 * j + 2 in fused(a) else (0, 1, 2):
                     nc.tensor.matmul(a_ps[a, t][:, j * 128 : (j + 1) * 128], lhsT=prods[a, 3 * j + i][:, t * 128 : (t + 1) * 128], rhs=ident[:], start=(i == 0), stop=(i == 2), is_transpose=True)
 
         def empty_a(a, t):
@@ -209,8 +214,8 @@ def tile_rangeviewmetakernelfourneighbour_x1_kernel(tc, rel, w1, b1, w2, b2, f, 
                 fn(a, *args)
 
         def shares(a):
-            early, n_g, n_v = (2, 3, 3)
-            xs = list(range(12)) if a <= LAST else []
+            early, n_g, n_v = (1, 3, 3)
+            xs = list((0, 1, 4, 7, 2, 5, 8, 3, 6, 9, 10, 11)) if a <= LAST else []
             return xs[:early], xs[early : early + n_g], xs[early + n_g : early + n_g + n_v], xs[early + n_g + n_v :]
 
         nc.vector.tensor_copy(out=relf[:, 0, :], in_=rel_0[:])
@@ -220,25 +225,25 @@ def tile_rangeviewmetakernelfourneighbour_x1_kernel(tc, rel, w1, b1, w2, b2, f, 
                 nc.scalar.copy(w1p[i][:], src)
             else:
                 nc.vector.tensor_copy(out=w1p[i][:], in_=src)
-        products(0, (0, 2, 3, 5, 6, 8, 9, 11), "vector")
         products(0, (1, 4, 7, 10), "scalar")
+        products(0, (0, 2, 3, 5, 6, 8, 9, 11), "vector")
         nc.vector.tensor_copy(out=relf[:, 1:, :], in_=rel_raw[:, 1:, 0:12])
         nc.scalar.activation(b1c[:], b1_raw[:], ACT.Identity)
         turn_a(0, 0)
         turn_a(0, 1)
         group_w(W2)
-        products(1, range(0, 1), "vector")
+        products(1, (0, 1, 2, 3, 4, 5)[:1], "vector")
         quant_w(W2)
-        products(1, range(1, 6), "vector")
-        products(1, range(6, 7), "scalar")
+        products(1, (0, 1, 2, 3, 4, 5)[1:], "vector")
+        products(1, (6, 7, 8, 9, 10, 11)[:1], "scalar")
         empty_a(0, 0)
-        products(1, range(7, 9), "scalar")
+        products(1, (6, 7, 8, 9, 10, 11)[1:3], "scalar")
         empty_a(0, 1)
         turn_a(0, 2)
         turn_a(0, 3)
-        products(1, range(9, 11), "scalar")
+        products(1, (6, 7, 8, 9, 10, 11)[3:5], "scalar")
         empty_a(0, 2)
-        products(1, range(11, 12), "scalar")
+        products(1, (6, 7, 8, 9, 10, 11)[5:], "scalar")
         empty_a(0, 3)
         nc.scalar.activation(b2c[:], b2_raw[:], ACT.Identity)
         group_w(0)
@@ -250,23 +255,23 @@ def tile_rangeviewmetakernelfourneighbour_x1_kernel(tc, rel, w1, b1, w2, b2, f, 
         quant_w(1)
         quant_m(0)
         empty_a(1, 0)
-        products(2, range(7, 8), "scalar")
+        products(2, (7, 8, 9, 10, 11)[:1], "scalar")
         empty_a(1, 1)
         turn_a(1, 2)
-        products(2, range(8, 9), "scalar")
+        products(2, (7, 8, 9, 10, 11)[1:2], "scalar")
         mx1(0, 0)
         mx1(0, 1)
         empty_a(1, 2)
         turn_a(1, 3)
         turn_f(0, 0)
-        products(2, range(0, 7), "vector")
+        products(2, (0, 1, 2, 3, 4, 5, 6), "vector")
         group_w(2)
         empty_k(0, 0)
         empty_k(0, 1)
         mx1(0, 2)
         mx1(0, 3)
         empty_a(1, 3)
-        products(2, range(9, 12), "scalar")
+        products(2, (7, 8, 9, 10, 11)[2:], "scalar")
         turn_f(0, 1)
         turn_a(2, 0)
         products(3, shares(3)[0], "vector")
@@ -296,7 +301,7 @@ def tile_rangeviewmetakernelfourneighbour_x1_kernel(tc, rel, w1, b1, w2, b2, f, 
             on(mx2, s - 3, 2, 4)
             on(mx1, s - 1, 0)
             on(mx1, s - 1, 1)
-            products(s + 1, on_s[1:2], "scalar")
+            products(s + 1, on_s[1:3], "scalar")
             empty_a(s, 2)
             on(empty_t, s - 4)
             turn_a(s, 3)
@@ -305,7 +310,7 @@ def tile_rangeviewmetakernelfourneighbour_x1_kernel(tc, rel, w1, b1, w2, b2, f, 
             on(join_p, s - 2, "vector")
             if s == 2:
                 quant_w(3)
-            products(s + 1, on_s[2:3], "scalar")
+            products(s + 1, on_s[3:4], "scalar")
             on(empty_k, s - 1, 0)
             on(empty_k, s - 1, 1)
             on(mx1, s - 1, 2)
@@ -313,7 +318,7 @@ def tile_rangeviewmetakernelfourneighbour_x1_kernel(tc, rel, w1, b1, w2, b2, f, 
             products(s + 1, on_v[2:], "vector")
             on(quant_p, s - 2)
             empty_a(s, 3)
-            products(s + 1, on_s[3:], "scalar")
+            products(s + 1, on_s[4:], "scalar")
             on(turn_f, s - 1, 1)
             turn_a(s + 1, 0)
             on(empty_o, s - 3)

@@ -30,26 +30,26 @@ def tile_rangeviewmetakernelfourneighbour_x1_kernel(tc, rel, w1, b1, w2, b2, f, 
 
         rel_0 = keep.tile([128, 12], BF16, name="rel_0")
         rel_raw = keep.tile([128, TILES, 16], BF16, name="rel_raw")
-        w1_raw = [keep.tile([128, 512], BF16, name=f"w1_raw{i}") for i in range(3)]
+        w1_col = keep.tile([128, 3, 4], BF16, name="w1_col")
         b1_raw = keep.tile([128, 4], BF16, name="b1_raw")
         b2_raw = keep.tile([128, 4], BF16, name="b2_raw")
         w_raw = [keep.tile([128, 4, 512], BF16, name=f"w_raw{x}") for x in range(J + 1)]
         f_sb = [keep.tile([128, J, 512], BF16, name=f"f_sb{a}") for a in range(TILES)]
 
         rel_rows = rel.rearrange("(a p) j i -> p a (j i)", p=128)
-        nc.sync.dma_start(out=w1_raw[0][:], in_=w1[0].partition_broadcast(128))
+        nc.sync.dma_start(out=w1_col[:], in_=w1.rearrange("i (p t) -> p i t", t=4))
         nc.sync.dma_start(out=rel_0[:], in_=rel_rows[:, 0, :])
-        nc.sync.dma_start(out=w1_raw[1][:], in_=w1[1].partition_broadcast(128))
-        nc.sync.dma_start(out=w1_raw[2][:], in_=w1[2].partition_broadcast(128))
-        nc.sync.dma_start(out=rel_raw[:, 1:, 0:12], in_=rel_rows[:, 1:, :])
-        nc.sync.dma_start(out=b1_raw[:], in_=b1.rearrange("(p t) -> p t", t=4))
         nc.sync.dma_start(out=w_raw[W2][:], in_=w2.rearrange("(p k) c -> p k c", k=4))
+        nc.sync.dma_start(out=b1_raw[:], in_=b1.rearrange("(p t) -> p t", t=4))
+        nc.sync.dma_start(out=rel_raw[:, 1:, 0:12], in_=rel_rows[:, 1:, :])
         nc.sync.dma_start(out=b2_raw[:], in_=b2.rearrange("(p t) -> p t", t=4))
         for j in range(J):
             nc.sync.dma_start(out=w_raw[j][:], in_=wo[j].rearrange("(p k) c -> p k c", k=4))
         for a in range(TILES):
             nc.sync.dma_start(out=f_sb[a][:], in_=f[a * 128 : (a + 1) * 128])
 
+        ident_bf = keep.tile([128, 128], BF16, name="ident_bf")
+        make_identity(nc, ident_bf[:])
         ident = keep.tile([128, 128], F32, name="ident")
         make_identity(nc, ident[:])
 
@@ -220,11 +220,13 @@ def tile_rangeviewmetakernelfourneighbour_x1_kernel(tc, rel, w1, b1, w2, b2, f, 
 
         nc.vector.tensor_copy(out=relf[:, 0, :], in_=rel_0[:])
         for i in range(3):
-            src = w1_raw[i][:].rearrange("p (m t) -> p t m", t=4)
+            bank = psum.tile([128, 4, 128], BF16, name="a_ps", bufs=3)
+            for t in range(4):
+                nc.tensor.transpose(bank[:, t, :], w1_col[:, i, t : t + 1].to_broadcast([128, 128]), ident_bf[:])
             if i == 1:
-                nc.scalar.copy(w1p[i][:], src)
+                nc.scalar.copy(w1p[i][:], bank[:])
             else:
-                nc.vector.tensor_copy(out=w1p[i][:], in_=src)
+                nc.vector.tensor_copy(out=w1p[i][:], in_=bank[:])
         products(0, (1, 4, 7, 10), "scalar")
         products(0, (0, 2, 3, 5, 6, 8, 9, 11), "vector")
         nc.vector.tensor_copy(out=relf[:, 1:, :], in_=rel_raw[:, 1:, 0:12])

@@ -68,8 +68,8 @@ def tile_rangeviewmetakernelfourneighbour_x1_kernel(tc, rel, w1, b1, w2, b2, f, 
 
         def group_w(x):
             w_grp[x] = work.tile([128, 2048], BF16, name="w_grp", align_bytes=64, bufs=3)
-            dst = w_grp[x][:].rearrange("p (t m k) -> p t m k", t=4, k=4)
-            nc.vector.tensor_copy(out=dst, in_=w_raw[x][:].rearrange("p k (m t) -> p t m k", t=4))
+            dst = w_grp[x][:].rearrange("p (t m k) -> p m k t", t=4, k=4)
+            nc.vector.tensor_copy(out=dst, in_=w_raw[x][:].rearrange("p k (m t) -> p m k t", t=4))
 
         def quant_w(x):
             nc.vector.quantize_mx(out=w_q[x][:].bitcast(FP8X4), scales=w_s[x][:], in_=w_grp[x][:])
@@ -79,7 +79,7 @@ def tile_rangeviewmetakernelfourneighbour_x1_kernel(tc, rel, w1, b1, w2, b2, f, 
             nc.vector.tensor_copy(out=rel_g[a][:], in_=rel_raw[:, a, 0:12])
 
         def fused(a):
-            return (5, 8) if a > 2 else ()
+            return (5, 8) if a > 2 else (2, 5) if a == 1 else ()
 
         def products(a, xs, engine):
             for x in xs:
@@ -223,29 +223,29 @@ def tile_rangeviewmetakernelfourneighbour_x1_kernel(tc, rel, w1, b1, w2, b2, f, 
             bank = psum.tile([128, 4, 128], BF16, name="a_ps", bufs=3)
             for t in range(4):
                 nc.tensor.transpose(bank[:, t, :], w1_col[:, i, t : t + 1].to_broadcast([128, 128]), ident_bf[:])
-            if i == 1:
+            if i > 0:
                 nc.scalar.copy(w1p[i][:], bank[:])
             else:
                 nc.vector.tensor_copy(out=w1p[i][:], in_=bank[:])
+        products(0, (0, 3, 6, 9, 2, 5, 8, 11), "vector")
         products(0, (1, 4, 7, 10), "scalar")
-        products(0, (0, 2, 3, 5, 6, 8, 9, 11), "vector")
         nc.vector.tensor_copy(out=relf[:, 1:, :], in_=rel_raw[:, 1:, 0:12])
         nc.scalar.activation(b1c[:], b1_raw[:], ACT.Identity)
         turn_a(0, 0)
         turn_a(0, 1)
         group_w(W2)
-        products(1, (0, 1, 2, 3, 4, 5)[:1], "vector")
+        products(1, (1,), "vector")
         quant_w(W2)
-        products(1, (0, 1, 2, 3, 4, 5)[1:], "vector")
-        products(1, (6, 7, 8, 9, 10, 11)[:1], "scalar")
+        products(1, (4, 0, 3, 2, 5), "vector")
+        products(1, range(6, 7), "scalar")
         empty_a(0, 0)
-        products(1, (6, 7, 8, 9, 10, 11)[1:3], "scalar")
+        products(1, range(7, 9), "scalar")
         empty_a(0, 1)
         turn_a(0, 2)
         turn_a(0, 3)
-        products(1, (6, 7, 8, 9, 10, 11)[3:5], "scalar")
+        products(1, range(9, 11), "scalar")
         empty_a(0, 2)
-        products(1, (6, 7, 8, 9, 10, 11)[5:], "scalar")
+        products(1, range(11, 12), "scalar")
         empty_a(0, 3)
         nc.scalar.activation(b2c[:], b2_raw[:], ACT.Identity)
         group_w(0)
@@ -253,39 +253,39 @@ def tile_rangeviewmetakernelfourneighbour_x1_kernel(tc, rel, w1, b1, w2, b2, f, 
         quant_w(0)
         turn_a(1, 0)
         turn_a(1, 1)
-        leaky(0)
         quant_w(1)
+        leaky(0)
+        products(2, (1,), "vector")
         quant_m(0)
         empty_a(1, 0)
-        products(2, (7, 8, 9, 10, 11)[:1], "scalar")
+        products(2, range(7, 8), "scalar")
         empty_a(1, 1)
         turn_a(1, 2)
-        products(2, (7, 8, 9, 10, 11)[1:2], "scalar")
         mx1(0, 0)
         mx1(0, 1)
+        products(2, range(8, 9), "scalar")
         empty_a(1, 2)
         turn_a(1, 3)
         turn_f(0, 0)
-        products(2, (0, 1, 2, 3, 4, 5, 6), "vector")
+        products(2, [x for x in range(7) if x != 1], "vector")
         group_w(2)
         empty_k(0, 0)
         empty_k(0, 1)
         mx1(0, 2)
         mx1(0, 3)
         empty_a(1, 3)
-        products(2, (7, 8, 9, 10, 11)[2:], "scalar")
+        products(2, range(9, 12), "scalar")
         turn_f(0, 1)
         turn_a(2, 0)
         products(3, shares(3)[0], "vector")
         quant_w(2)
+        group_w(3)
         empty_k(0, 2)
         empty_k(0, 3)
         for s in range(2, LAST):
             early, on_g, on_v, on_s = shares(s + 1)
             turn_a(s, 1)
             on(leaky, s - 1)
-            if s == 2:
-                group_w(3)
             empty_a(s, 0)
             products(s + 1, on_v[:1], "vector")
             on(quant_o, s - 5)

@@ -71,6 +71,13 @@ def tile_rangeviewmetakernelfourneighbour_x1_kernel(tc, rel, w1, b1, w2, b2, f, 
             dst = w_grp[x][:].rearrange("p (t m k) -> p m k t", t=4, k=4)
             nc.vector.tensor_copy(out=dst, in_=w_raw[x][:].rearrange("p k (m t) -> p m k t", t=4))
 
+        def group_w_part(x, part):
+            if part == 0:
+                w_grp[x] = work.tile([128, 2048], BF16, name="w_grp", align_bytes=64, bufs=3)
+            ms = slice(part * 32, (part + 1) * 32)
+            dst = w_grp[x][:].rearrange("p (t m k) -> p m k t", t=4, k=4)[:, ms]
+            nc.scalar.copy(dst, w_raw[x][:].rearrange("p k (m t) -> p m k t", t=4)[:, ms])
+
         def quant_w(x):
             nc.vector.quantize_mx(out=w_q[x][:].bitcast(FP8X4), scales=w_s[x][:], in_=w_grp[x][:])
 
@@ -140,8 +147,8 @@ def tile_rangeviewmetakernelfourneighbour_x1_kernel(tc, rel, w1, b1, w2, b2, f, 
         def join_p(a, engine, j0=0, j1=J):
             if a not in p_bf:
                 p_bf[a] = work.tile([128, 2048], BF16, name="p_bf", align_bytes=64)
-            words = p_w[a][:].rearrange("p h n e -> p h (n e)").bitcast(F32)[:, :, j0 * 128 : j1 * 128].rearrange("p h n -> p n h")
-            out = p_bf[a][:, j0 * 512 : j1 * 512].bitcast(F32).rearrange("p (n h) -> p n h", h=2)
+            words = p_w[a][:].rearrange("p h n e -> p h (n e)").bitcast(F32)[:, :, j0 * 128 : j1 * 128].rearrange("p h (n i) -> p n h i", i=4)
+            out = p_bf[a][:, j0 * 512 : j1 * 512].bitcast(F32).rearrange("p (n i h) -> p n h i", i=4, h=2)
             if engine == "scalar":
                 nc.scalar.copy(out, words)
             else:
@@ -184,11 +191,12 @@ def tile_rangeviewmetakernelfourneighbour_x1_kernel(tc, rel, w1, b1, w2, b2, f, 
 
         def round_o(a, engine):
             o_w[a] = work.tile([128, 2, 128, 2], BF16, name="o_w")
-            src = r_sb[a][:].rearrange("n (m h e) -> n h m e", h=2, e=2)
+            src = r_sb[a][:].rearrange("n (m h e) -> n m h e", h=2, e=2)
+            out = o_w[a][:].rearrange("n h m e -> n m h e")
             if engine == "scalar":
-                nc.scalar.activation(o_w[a][:], src, ACT.Identity)
+                nc.scalar.activation(out, src, ACT.Identity)
             else:
-                nc.vector.tensor_copy(out=o_w[a][:], in_=src)
+                nc.vector.tensor_copy(out=out, in_=src)
 
         def turn_o(a):
             t_ps[a] = psum.tile([128, 2, 128], F32, name="a_ps", bufs=3)
@@ -227,8 +235,8 @@ def tile_rangeviewmetakernelfourneighbour_x1_kernel(tc, rel, w1, b1, w2, b2, f, 
                 nc.scalar.copy(w1p[i][:], bank[:])
             else:
                 nc.vector.tensor_copy(out=w1p[i][:], in_=bank[:])
-        products(0, (0, 3, 6, 9, 2, 5, 8, 11), "vector")
-        products(0, (1, 4, 7, 10), "scalar")
+        products(0, (0, 3, 6, 1, 2, 5, 9, 8, 11), "vector")
+        products(0, (4, 7, 10), "scalar")
         nc.vector.tensor_copy(out=relf[:, 1:, :], in_=rel_raw[:, 1:, 0:12])
         nc.scalar.activation(b1c[:], b1_raw[:], ACT.Identity)
         turn_a(0, 0)
@@ -255,26 +263,29 @@ def tile_rangeviewmetakernelfourneighbour_x1_kernel(tc, rel, w1, b1, w2, b2, f, 
         turn_a(1, 1)
         quant_w(1)
         leaky(0)
-        products(2, (1,), "vector")
+        products(2, (0,), "vector")
         quant_m(0)
+        group_w_part(2, 0)
+        group_w_part(2, 1)
         empty_a(1, 0)
-        products(2, range(7, 8), "scalar")
+        group_w_part(2, 2)
+        products(2, range(8, 9), "scalar")
         empty_a(1, 1)
         turn_a(1, 2)
         mx1(0, 0)
         mx1(0, 1)
-        products(2, range(8, 9), "scalar")
+        group_w_part(2, 3)
+        products(2, range(9, 10), "scalar")
         empty_a(1, 2)
         turn_a(1, 3)
         turn_f(0, 0)
-        products(2, [x for x in range(7) if x != 1], "vector")
-        group_w(2)
+        products(2, range(1, 8), "vector")
         empty_k(0, 0)
         empty_k(0, 1)
         mx1(0, 2)
         mx1(0, 3)
         empty_a(1, 3)
-        products(2, range(9, 12), "scalar")
+        products(2, range(10, 12), "scalar")
         turn_f(0, 1)
         turn_a(2, 0)
         products(3, shares(3)[0], "vector")
@@ -376,16 +387,16 @@ def tile_rangeviewmetakernelfourneighbour_x1_kernel(tc, rel, w1, b1, w2, b2, f, 
         empty_k(a, 2)
         empty_k(a, 3)
         turn_f(a, 1)
-        quant_o(a - 3)
         join_p(a - 1, "vector")
+        quant_o(a - 3)
+        quant_p(a - 1)
         empty_o(a - 2)
         empty_turned(a - 2, "scalar")
-        times_f(a, 0)
         store_scales(0, 512, nc.sync)
-        quant_p(a - 1)
-        times_f(a, 1, 0, 2)
         mx2_turned(a - 1, 0, 4)
         mx2(a - 1, 0, 4)
+        times_f(a, 0)
+        times_f(a, 1, 0, 2)
         quant_o(a - 2)
         join_p(a, "vector", 0, 2)
         times_f(a, 1, 2, 4)

@@ -63,20 +63,21 @@ def tile_rangeviewmetakernelfourneighbour_x1_kernel(tc, rel, w1, b1, w2, b2, f, 
         o_s = keep.tile([128, N], U8, name="o_s", align_bytes=64)
 
         w_grp, rel_g, prods, a_ps, a_sb, m_bf, m_q = {}, {}, {}, {}, {}, {}, {}
-        k_ps, k_sb, f_ps, p_w, p_bf, p_q = {}, {}, {}, {}, {}, {}
+        k_ps, k_sb, f_ps, p_bf, p_q = {}, {}, {}, {}, {}
         o_ps, r_sb, o_w, t_ps, o_bf = {}, {}, {}, {}, {}
 
         def group_w(x):
             w_grp[x] = work.tile([128, 2048], BF16, name="w_grp", align_bytes=64, bufs=3)
-            dst = w_grp[x][:].rearrange("p (t m k) -> p m k t", t=4, k=4)
-            nc.vector.tensor_copy(out=dst, in_=w_raw[x][:].rearrange("p k (m t) -> p m k t", t=4))
+            slots = "g e" if x == W2 else "e g"
+            dst = w_grp[x][:].rearrange(f"p (t m {slots}) -> p m g e t", t=4, e=2, g=2)
+            nc.vector.tensor_copy(out=dst, in_=w_raw[x][:].rearrange("p (g e) (m t) -> p m g e t", t=4, e=2))
 
         def group_w_part(x, part):
             if part == 0:
                 w_grp[x] = work.tile([128, 2048], BF16, name="w_grp", align_bytes=64, bufs=3)
             ms = slice(part * 32, (part + 1) * 32)
-            dst = w_grp[x][:].rearrange("p (t m k) -> p m k t", t=4, k=4)[:, ms]
-            nc.scalar.copy(dst, w_raw[x][:].rearrange("p k (m t) -> p m k t", t=4)[:, ms])
+            dst = w_grp[x][:].rearrange("p (t m e g) -> p m g e t", t=4, e=2, g=2)[:, ms]
+            nc.scalar.copy(dst, w_raw[x][:].rearrange("p (g e) (m t) -> p m g e t", t=4, e=2)[:, ms])
 
         def quant_w(x):
             nc.vector.quantize_mx(out=w_q[x][:].bitcast(FP8X4), scales=w_s[x][:], in_=w_grp[x][:])
@@ -127,32 +128,25 @@ def tile_rangeviewmetakernelfourneighbour_x1_kernel(tc, rel, w1, b1, w2, b2, f, 
             nc.tensor.matmul_mx(k_ps[a, t][:], lhsT=w_q[W2][:, cols].bitcast(FP8X4), lhsT_scale=w_s[W2][:, cols], rhs=m_q[a][0][:].bitcast(FP8X4), rhs_scale=m_q[a][1][:], start=True, stop=True)
 
         def empty_k(a, t):
-            if t % 2 == 0:
-                k_sb[a, t // 2] = work.tile([128, 128, 2, 4], F32, name="k_sb", bufs=3)
-            nc.scalar.activation(k_sb[a, t // 2][:, :, t % 2, :], k_ps[a, t][:].rearrange("p (n i) -> p n i", i=4), ACT.Identity, bias=b2c[:, t : t + 1])
+            if t == 0:
+                k_sb[a] = work.tile([128, 128, 2, 2, 4], F32, name="k_sb")
+            nc.scalar.activation(k_sb[a][:, :, t % 2, t // 2, :], k_ps[a, t][:].rearrange("p (n i) -> p n i", i=4), ACT.Identity, bias=b2c[:, t : t + 1])
 
         def turn_f(a, h):
-            f_ps[a, h] = psum.tile([128, 512], F32, name="f_ps", bufs=2)
-            for j in range(J):
-                words = f_sb[a][:, j, :].bitcast(F32)
-                nc.tensor.transpose(f_ps[a, h][:, j * 128 : (j + 1) * 128], words[:, h:256:2], ident[:])
+            f_ps[a, h] = psum.tile([128, 2, 256], F32, name="f_ps", bufs=2)
+            for jj in range(2):
+                words = f_sb[a][:, 2 * h + jj, :].bitcast(F32)
+                for g in range(2):
+                    nc.tensor.transpose(f_ps[a, h][:, g, jj * 128 : (jj + 1) * 128], words[:, g:256:2], ident[:])
 
-        def times_f(a, h, j0=0, j1=J):
-            if a not in p_w:
-                p_w[a] = work.tile([128, 2, 512, 2], BF16, name="p_w")
-            fv = f_ps[a, h][:, j0 * 128 : j1 * 128].bitcast(BF16).rearrange("p (n i e) -> p n e i", i=4, e=2)
-            out = p_w[a][:, h, j0 * 128 : j1 * 128, :].rearrange("p (n i) e -> p n e i", i=4)
-            nc.vector.tensor_tensor(out=out, in0=fv, in1=k_sb[a, h][:, j0 * 32 : j1 * 32], op=ALU.mult)
-
-        def join_p(a, engine, j0=0, j1=J):
+        def times_f(a, j0, j1):
             if a not in p_bf:
                 p_bf[a] = work.tile([128, 2048], BF16, name="p_bf", align_bytes=64)
-            words = p_w[a][:].rearrange("p h n e -> p h (n e)").bitcast(F32)[:, :, j0 * 128 : j1 * 128].rearrange("p h (n i) -> p n h i", i=4)
-            out = p_bf[a][:, j0 * 512 : j1 * 512].bitcast(F32).rearrange("p (n i h) -> p n h i", i=4, h=2)
-            if engine == "scalar":
-                nc.scalar.copy(out, words)
-            else:
-                nc.vector.tensor_copy(out=out, in_=words)
+            words = f_ps[a, j0 // 2][:, :, j0 % 2 * 128 : (j0 % 2 + j1 - j0) * 128]
+            fv = words.bitcast(BF16).rearrange("p g (n i e) -> p n g i e", i=4, e=2)
+            kv = k_sb[a][:, j0 * 32 : j1 * 32].rearrange("p n e g i -> p n g i e")
+            out = p_bf[a][:, j0 * 512 : j1 * 512].rearrange("p (n i e g) -> p n g i e", i=4, e=2, g=2)
+            nc.vector.tensor_tensor(out=out, in0=fv, in1=kv, op=ALU.mult)
 
         def quant_p(a, j0=0, j1=J):
             if a not in p_q:
@@ -222,8 +216,8 @@ def tile_rangeviewmetakernelfourneighbour_x1_kernel(tc, rel, w1, b1, w2, b2, f, 
                 fn(a, *args)
 
         def shares(a):
-            early, n_g, n_v = (1, 3, 3)
-            xs = list((0, 1, 4, 7, 2, 5, 8, 3, 6, 9, 10, 11)) if a <= LAST else []
+            early, n_g, n_v = (2, 3, 3)
+            xs = list((0, 3, 1, 4, 7, 2, 5, 8, 6, 9, 10, 11)) if a <= LAST else []
             return xs[:early], xs[early : early + n_g], xs[early + n_g : early + n_g + n_v], xs[early + n_g + n_v :]
 
         nc.vector.tensor_copy(out=relf[:, 0, :], in_=rel_0[:])
@@ -308,22 +302,21 @@ def tile_rangeviewmetakernelfourneighbour_x1_kernel(tc, rel, w1, b1, w2, b2, f, 
             turn_a(s, 2)
             on(quant_m, s - 1)
             products(s + 1, on_g, "gpsimd")
-            on(times_f, s - 2, 0)
-            on(times_f, s - 2, 1)
+            on(times_f, s - 2, 0, 2)
+            on(times_f, s - 2, 2, 4)
             on(turn_o, s - 4)
             on(mx2, s - 3, 2, 4)
             on(mx1, s - 1, 0)
             on(mx1, s - 1, 1)
-            products(s + 1, on_s[1:3], "scalar")
+            products(s + 1, on_s[1:2], "scalar")
             empty_a(s, 2)
             on(empty_t, s - 4)
             turn_a(s, 3)
             on(turn_f, s - 1, 0)
             products(s + 1, on_v[1:2], "vector")
-            on(join_p, s - 2, "vector")
             if s == 2:
                 quant_w(3)
-            products(s + 1, on_s[3:4], "scalar")
+            products(s + 1, on_s[2:3], "scalar")
             on(empty_k, s - 1, 0)
             on(empty_k, s - 1, 1)
             on(mx1, s - 1, 2)
@@ -331,7 +324,7 @@ def tile_rangeviewmetakernelfourneighbour_x1_kernel(tc, rel, w1, b1, w2, b2, f, 
             products(s + 1, on_v[2:], "vector")
             on(quant_p, s - 2)
             empty_a(s, 3)
-            products(s + 1, on_s[4:], "scalar")
+            products(s + 1, on_s[3:], "scalar")
             on(turn_f, s - 1, 1)
             turn_a(s + 1, 0)
             on(empty_o, s - 3)
@@ -350,8 +343,8 @@ def tile_rangeviewmetakernelfourneighbour_x1_kernel(tc, rel, w1, b1, w2, b2, f, 
         quant_o(a - 5)
         quant_m(a - 1)
         empty_a(a, 2)
-        times_f(a - 2, 0)
-        times_f(a - 2, 1)
+        times_f(a - 2, 0, 2)
+        times_f(a - 2, 2, 4)
         mx1(a - 1, 0)
         mx1(a - 1, 1)
         empty_a(a, 3)
@@ -363,7 +356,6 @@ def tile_rangeviewmetakernelfourneighbour_x1_kernel(tc, rel, w1, b1, w2, b2, f, 
         mx1(a - 1, 3)
         turn_f(a - 1, 1)
         leaky(a)
-        join_p(a - 2, "scalar")
         empty_k(a - 1, 2)
         empty_k(a - 1, 3)
         empty_o(a - 3)
@@ -371,45 +363,44 @@ def tile_rangeviewmetakernelfourneighbour_x1_kernel(tc, rel, w1, b1, w2, b2, f, 
         quant_p(a - 2)
         quant_m(a)
         mx2_turned(a - 3, 0, 4)
+        for t in range(2):
+            mx1(a, t)
+        for t in range(2, 4):
+            mx1(a, t, "a_ps", 3)
         mx2(a - 2, 0, 4)
-        mx1(a, 0)
-        mx1(a, 1)
-        mx1(a, 2, "a_ps", 3)
-        mx1(a, 3, "a_ps", 3)
-        times_f(a - 1, 0)
+        times_f(a - 1, 0, 2)
         quant_o(a - 4)
-        times_f(a - 1, 1)
+        times_f(a - 1, 2, 4)
         empty_turned(a - 3, "scalar")
-        empty_k(a, 0)
-        empty_k(a, 1)
+        for t in range(4):
+            empty_k(a, t)
         turn_f(a, 0)
-        mx2_turned(a - 2, 0, 4)
-        empty_k(a, 2)
-        empty_k(a, 3)
         turn_f(a, 1)
-        join_p(a - 1, "vector")
         quant_o(a - 3)
         quant_p(a - 1)
         empty_o(a - 2)
-        empty_turned(a - 2, "scalar")
+        round_o(a - 2, "scalar")
         store_scales(0, 512, nc.sync)
-        mx2_turned(a - 1, 0, 4)
         mx2(a - 1, 0, 4)
-        times_f(a, 0)
-        times_f(a, 1, 0, 2)
-        quant_o(a - 2)
-        join_p(a, "vector", 0, 2)
-        times_f(a, 1, 2, 4)
+        turn_o(a - 2)
+        times_f(a, 0, 2)
+        times_f(a, 2, 3)
         quant_p(a, 0, 2)
-        join_p(a, "vector", 2, 4)
-        empty_turned(a - 1, "scalar")
         empty_o(a - 1)
+        empty_t(a - 2)
+        round_o(a - 1, "scalar")
         mx2(a, 0, 2)
         mx2_turned(a, 0, 2)
-        quant_o(a - 1)
-        quant_p(a, 2, 4)
+        turn_o(a - 1)
+        times_f(a, 3, 4)
+        quant_p(a, 2, 3)
+        quant_p(a, 3, 4)
+        quant_o(a - 2)
+        empty_t(a - 1)
+        mx2(a, 2, 3)
         mx2_turned(a, 2, 4)
-        mx2(a, 2, 4)
+        mx2(a, 3, 4)
+        quant_o(a - 1)
         empty_turned(a, "vector")
         empty_o(a)
         quant_o(a)

@@ -61,10 +61,11 @@ def tile_rangeviewmetakernelfourneighbour_x1_kernel(tc, rel, w1, b1, w2, b2, f, 
         w_s = [keep.tile([128, 512], U8, name=f"w_s{x}", align_bytes=64) for x in range(J + 1)]
         o_q = keep.tile([128, N], U32, name="o_q", align_bytes=64)
         o_s = keep.tile([128, N], U8, name="o_s", align_bytes=64)
+        o_bf = keep.tile([128, 4 * N], BF16, name="o_bf", align_bytes=64)
 
         w_grp, rel_g, prods, a_ps, a_sb, m_bf, m_q = {}, {}, {}, {}, {}, {}, {}
         k_ps, k_sb, f_ps, p_bf, p_q = {}, {}, {}, {}, {}
-        o_ps, r_sb, o_w, t_ps, o_bf = {}, {}, {}, {}, {}
+        o_ps, r_sb, o_w, t_ps = {}, {}, {}, {}
 
         def group_w(x):
             w_grp[x] = work.tile([128, 2048], BF16, name="w_grp", align_bytes=64, bufs=3)
@@ -87,7 +88,7 @@ def tile_rangeviewmetakernelfourneighbour_x1_kernel(tc, rel, w1, b1, w2, b2, f, 
             nc.vector.tensor_copy(out=rel_g[a][:], in_=rel_raw[:, a, 0:12])
 
         def fused(a):
-            return (5, 8) if a > 2 else (2, 5) if a == 1 else ()
+            return (8,) if a > 2 else (2, 5) if a == 1 else ()
 
         def products(a, xs, engine):
             for x in xs:
@@ -113,8 +114,12 @@ def tile_rangeviewmetakernelfourneighbour_x1_kernel(tc, rel, w1, b1, w2, b2, f, 
                 a_sb[a] = work.tile([128, 128, 4, J], F32, name="a_sb")
             nc.scalar.activation(a_sb[a][:, :, t, :], a_ps[a, t][:].rearrange("p (j n) -> p n j", j=J), ACT.Identity, bias=b1c[:, t : t + 1])
 
-        def leaky(a):
+        def take_m(a):
             m_bf[a] = work.tile([128, 2048], BF16, name="m_bf", align_bytes=64)
+
+        def leaky(a):
+            if a not in m_bf:
+                take_m(a)
             src = a_sb[a][:].rearrange("p n t j -> p (n t) j")
             nc.vector.scalar_tensor_tensor(out=m_bf[a][:].rearrange("p (j x) -> p x j", j=J), in0=src, scalar=SLOPE, in1=src, op0=ALU.mult, op1=ALU.max)
 
@@ -132,8 +137,8 @@ def tile_rangeviewmetakernelfourneighbour_x1_kernel(tc, rel, w1, b1, w2, b2, f, 
                 k_sb[a] = work.tile([128, 128, 2, 2, 4], F32, name="k_sb")
             nc.scalar.activation(k_sb[a][:, :, t % 2, t // 2, :], k_ps[a, t][:].rearrange("p (n i) -> p n i", i=4), ACT.Identity, bias=b2c[:, t : t + 1])
 
-        def turn_f(a, h):
-            f_ps[a, h] = psum.tile([128, 2, 256], F32, name="f_ps", bufs=2)
+        def turn_f(a, h, tag="f_ps", bufs=2):
+            f_ps[a, h] = psum.tile([128, 2, 256], F32, name=tag, bufs=bufs)
             for jj in range(2):
                 words = f_sb[a][:, 2 * h + jj, :].bitcast(F32)
                 for g in range(2):
@@ -154,10 +159,10 @@ def tile_rangeviewmetakernelfourneighbour_x1_kernel(tc, rel, w1, b1, w2, b2, f, 
             cols = slice(j0 * 128, j1 * 128)
             nc.vector.quantize_mx(out=p_q[a][0][:, cols].bitcast(FP8X4), scales=p_q[a][1][:, cols], in_=p_bf[a][:, j0 * 512 : j1 * 512])
 
-        def mx2(a, j0, j1):
+        def mx2(a, j0, j1, tag="o_ps", bufs=1):
             for j in range(j0, j1):
                 if j == 0:
-                    o_ps[a] = psum.tile([128, 512], F32, name="k_ps", bufs=2) if a == LAST else psum.tile([128, 512], F32, name="o_ps")
+                    o_ps[a] = psum.tile([128, 512], F32, name=tag, bufs=bufs)
                 cols = slice(j * 128, (j + 1) * 128)
                 nc.tensor.matmul_mx(o_ps[a][:], lhsT=p_q[a][0][:, cols].bitcast(FP8X4), lhsT_scale=p_q[a][1][:, cols], rhs=w_q[j][:].bitcast(FP8X4), rhs_scale=w_s[j][:], start=(j == 0), stop=(j == J - 1))
 
@@ -170,46 +175,47 @@ def tile_rangeviewmetakernelfourneighbour_x1_kernel(tc, rel, w1, b1, w2, b2, f, 
                     cols = slice(t * 128, (t + 1) * 128)
                     nc.tensor.matmul_mx(t_ps[a][:, t, :], lhsT=w_q[j][:, cols].bitcast(FP8X4), lhsT_scale=w_s[j][:, cols], rhs=p_q[a][0][:, rows].bitcast(FP8X4), rhs_scale=p_q[a][1][:, rows], start=(j == 0 and t == 0), stop=(j == J - 1 and t == 3))
 
-        def empty_turned(a, engine):
-            o_bf[a] = work.tile([128, 512], BF16, name="o_bf", align_bytes=64)
-            out, src = o_bf[a][:].rearrange("p (n t) -> p n t", t=4), t_ps[a][:].rearrange("p t n -> p n t")
-            if engine == "scalar":
-                nc.scalar.activation(out, src, ACT.Identity)
-            else:
-                nc.vector.tensor_copy(out=out, in_=src)
+        def empty_turned(a):
+            out = o_bf[:, a * 512 : (a + 1) * 512].rearrange("p (n t) -> p n t", t=4)
+            nc.vector.tensor_copy(out=out, in_=t_ps[a][:].rearrange("p t n -> p n t"))
 
         def empty_o(a):
-            r_sb[a] = work.tile([128, 512], F32, name="r_sb")
+            r_sb[a] = work.tile([128, 512], F32, name="r_sb", bufs=TILES)
             nc.scalar.activation(r_sb[a][:].rearrange("n (m t) -> n m t", t=4), o_ps[a][:].rearrange("n (t m) -> n m t", t=4), ACT.Identity)
             nc.sync.dma_start(out=out_0[a * 128 : (a + 1) * 128, :], in_=r_sb[a][:])
 
-        def round_o(a, engine):
-            o_w[a] = work.tile([128, 2, 128, 2], BF16, name="o_w")
-            src = r_sb[a][:].rearrange("n (m h e) -> n m h e", h=2, e=2)
-            out = o_w[a][:].rearrange("n h m e -> n m h e")
-            if engine == "scalar":
-                nc.scalar.activation(out, src, ACT.Identity)
-            else:
-                nc.vector.tensor_copy(out=out, in_=src)
+        def round_o(tiles, engine):
+            tag = "m_bf" if engine == "gpsimd" else "o_w"
+            words = work.tile([128, 4, 2, 128, 2], BF16, name=tag, align_bytes=64)
+            for x, a in enumerate(tiles):
+                o_w[a] = words[:, x]
+                src = r_sb[a][:].rearrange("n (m h e) -> n h m e", h=2, e=2)
+                if engine == "gpsimd":
+                    nc.gpsimd.tensor_scalar(out=o_w[a], in0=src, scalar1=1.0, scalar2=0.0, op0=ALU.mult, op1=ALU.add)
+                elif engine == "scalar":
+                    nc.scalar.activation(o_w[a], src, ACT.Identity)
+                else:
+                    nc.vector.tensor_copy(out=o_w[a], in_=src)
 
-        def turn_o(a):
-            t_ps[a] = psum.tile([128, 2, 128], F32, name="a_ps", bufs=3)
-            words = o_w[a][:].rearrange("n h m e -> n h (m e)").bitcast(F32)
-            for h in range(2):
-                nc.tensor.transpose(t_ps[a][:, h, :], words[:, h, :], ident[:])
+        def turn_o(a0, a1, tag="a_ps", bufs=3):
+            t_ps[a0] = psum.tile([128, 2, 2, 128], F32, name=tag, bufs=bufs)
+            for a in range(a0, a1):
+                words = o_w[a].rearrange("n h m e -> n h (m e)").bitcast(F32)
+                for h in range(2):
+                    nc.tensor.transpose(t_ps[a0][:, a - a0, h, :], words[:, h, :], ident[:])
 
-        def empty_t(a):
-            o_bf[a] = work.tile([128, 512], BF16, name="o_bf", align_bytes=64)
-            nc.scalar.copy(o_bf[a][:].bitcast(F32).rearrange("p (n h) -> p n h", h=2), t_ps[a][:].rearrange("p h n -> p n h"))
+        def empty_t(a0, a1):
+            out = o_bf[:, a0 * 512 : a1 * 512].bitcast(F32).rearrange("p (a n h) -> p a n h", n=128, h=2)
+            nc.scalar.copy(out, t_ps[a0][:, 0 : a1 - a0].rearrange("p a h n -> p a n h"))
 
-        def quant_o(a):
-            cols = slice(a * 128, (a + 1) * 128)
-            nc.vector.quantize_mx(out=o_q[:, cols].bitcast(FP8X4), scales=o_s[:, cols], in_=o_bf[a][:])
+        def quant_o(a0, a1):
+            cols = slice(a0 * 128, a1 * 128)
+            nc.vector.quantize_mx(out=o_q[:, cols].bitcast(FP8X4), scales=o_s[:, cols], in_=o_bf[:, a0 * 512 : a1 * 512])
             nc.sync.dma_start(out=out_1[0, :, cols, :].rearrange("p m t -> p (m t)").bitcast(I32), in_=o_q[:, cols].bitcast(I32))
 
-        def store_scales(c0, c1, queue):
+        def store_scales(c0, c1, queues):
             for q in range(4):
-                queue.dma_start(out=out_2[0, 4 * q : 4 * q + 4, c0:c1].bitcast(I32), in_=o_s[32 * q : 32 * q + 4, c0:c1].bitcast(I32))
+                queues[q].dma_start(out=out_2[0, 4 * q : 4 * q + 4, c0:c1].bitcast(I32), in_=o_s[32 * q : 32 * q + 4, c0:c1].bitcast(I32))
 
         def on(fn, a, *args):
             if a >= 0:
@@ -293,24 +299,20 @@ def tile_rangeviewmetakernelfourneighbour_x1_kernel(tc, rel, w1, b1, w2, b2, f, 
             on(leaky, s - 1)
             empty_a(s, 0)
             products(s + 1, on_v[:1], "vector")
-            on(quant_o, s - 5)
-            if on_g:
-                cast_rel(s + 1)
+            cast_rel(s + 1)
             products(s + 1, on_s[:1], "scalar")
-            on(mx2, s - 3, 0, 2)
             empty_a(s, 1)
             turn_a(s, 2)
             on(quant_m, s - 1)
             products(s + 1, on_g, "gpsimd")
             on(times_f, s - 2, 0, 2)
             on(times_f, s - 2, 2, 4)
-            on(turn_o, s - 4)
-            on(mx2, s - 3, 2, 4)
+            on(mx2, s - 3, 0, 4)
             on(mx1, s - 1, 0)
             on(mx1, s - 1, 1)
             products(s + 1, on_s[1:2], "scalar")
             empty_a(s, 2)
-            on(empty_t, s - 4)
+            on(empty_o, s - 3)
             turn_a(s, 3)
             on(turn_f, s - 1, 0)
             products(s + 1, on_v[1:2], "vector")
@@ -322,16 +324,15 @@ def tile_rangeviewmetakernelfourneighbour_x1_kernel(tc, rel, w1, b1, w2, b2, f, 
             on(mx1, s - 1, 2)
             on(mx1, s - 1, 3)
             products(s + 1, on_v[2:], "vector")
-            on(quant_p, s - 2)
+            if s < LAST - 1:
+                quant_p(s - 2)
             empty_a(s, 3)
             products(s + 1, on_s[3:], "scalar")
             on(turn_f, s - 1, 1)
             turn_a(s + 1, 0)
-            on(empty_o, s - 3)
             products(s + 2, shares(s + 2)[0], "vector")
             on(empty_k, s - 1, 2)
             on(empty_k, s - 1, 3)
-            on(round_o, s - 3, "vector")
         a = LAST
         turn_a(a, 1)
         leaky(a - 1)
@@ -339,69 +340,73 @@ def tile_rangeviewmetakernelfourneighbour_x1_kernel(tc, rel, w1, b1, w2, b2, f, 
         turn_a(a, 2)
         empty_a(a, 1)
         turn_a(a, 3)
-        mx2(a - 3, 0, 4)
-        quant_o(a - 5)
+        quant_p(a - 3)
         quant_m(a - 1)
-        empty_a(a, 2)
+        take_m(a)
+        round_o((0, 1, 2), "gpsimd")
         times_f(a - 2, 0, 2)
         times_f(a - 2, 2, 4)
+        empty_a(a, 2)
         mx1(a - 1, 0)
         mx1(a - 1, 1)
+        mx2(a - 3, 0, 4)
         empty_a(a, 3)
-        turn_o(a - 4)
-        turn_f(a - 1, 0)
         empty_k(a - 1, 0)
         empty_k(a - 1, 1)
         mx1(a - 1, 2)
         mx1(a - 1, 3)
+        turn_f(a - 1, 0)
         turn_f(a - 1, 1)
+        turn_o(0, 2)
         leaky(a)
         empty_k(a - 1, 2)
         empty_k(a - 1, 3)
+        round_o((3,), "scalar")
         empty_o(a - 3)
-        empty_t(a - 4)
+        turn_o(2, 4)
+        empty_t(0, 2)
+        turn_f(a, 0, "a_ps", 3)
+        empty_t(2, 4)
         quant_p(a - 2)
         quant_m(a)
-        mx2_turned(a - 3, 0, 4)
+        round_o((4,), "gpsimd")
         for t in range(2):
             mx1(a, t)
-        for t in range(2, 4):
-            mx1(a, t, "a_ps", 3)
+        mx1(a, 2, "a_ps", 3)
+        mx1(a, 3, "a_ps", 3)
         mx2(a - 2, 0, 4)
         times_f(a - 1, 0, 2)
-        quant_o(a - 4)
         times_f(a - 1, 2, 4)
-        empty_turned(a - 3, "scalar")
         for t in range(4):
             empty_k(a, t)
-        turn_f(a, 0)
-        turn_f(a, 1)
-        quant_o(a - 3)
-        quant_p(a - 1)
         empty_o(a - 2)
-        round_o(a - 2, "scalar")
-        store_scales(0, 512, nc.sync)
-        mx2(a - 1, 0, 4)
-        turn_o(a - 2)
-        times_f(a, 0, 2)
-        times_f(a, 2, 3)
-        quant_p(a, 0, 2)
+        turn_f(a, 1)
+        quant_o(0, 2)
+        quant_p(a - 1)
+        mx2(a - 1, 0, 4, "k_ps", 2)
+        round_o((5,), "gpsimd")
         empty_o(a - 1)
-        empty_t(a - 2)
-        round_o(a - 1, "scalar")
-        mx2(a, 0, 2)
-        mx2_turned(a, 0, 2)
-        turn_o(a - 1)
+        round_o((6,), "scalar")
+        times_f(a, 0, 1)
+        times_f(a, 1, 2)
+        quant_p(a, 0, 1)
+        times_f(a, 2, 3)
+        quant_p(a, 1, 2)
+        turn_o(4, 6, "f_ps", 2)
+        empty_t(4, 6)
+        mx2_turned(a, 0, 1)
+        mx2(a, 0, 1)
+        mx2_turned(a, 1, 2)
+        mx2(a, 1, 2)
+        turn_o(6, 7, "k_ps", 2)
         times_f(a, 3, 4)
         quant_p(a, 2, 3)
         quant_p(a, 3, 4)
-        quant_o(a - 2)
-        empty_t(a - 1)
-        mx2(a, 2, 3)
+        empty_t(6, 7)
         mx2_turned(a, 2, 4)
-        mx2(a, 3, 4)
-        quant_o(a - 1)
-        empty_turned(a, "vector")
+        mx2(a, 2, 4)
+        quant_o(2, 6)
+        empty_turned(a)
         empty_o(a)
-        quant_o(a)
-        store_scales(512, 1024, nc.scalar)
+        quant_o(6, 8)
+        store_scales(0, 1024, [nc.scalar, nc.scalar, nc.sync, nc.sync])

@@ -48,8 +48,6 @@ def tile_rangeviewmetakernelfourneighbour_x1_kernel(tc, rel, w1, b1, w2, b2, f, 
         for a in range(TILES):
             nc.sync.dma_start(out=f_sb[a][:], in_=f[a * 128 : (a + 1) * 128])
 
-        ident_bf = keep.tile([128, 128], BF16, name="ident_bf")
-        make_identity(nc, ident_bf[:])
         ident = keep.tile([128, 128], F32, name="ident")
         make_identity(nc, ident[:])
 
@@ -88,7 +86,7 @@ def tile_rangeviewmetakernelfourneighbour_x1_kernel(tc, rel, w1, b1, w2, b2, f, 
             nc.vector.tensor_copy(out=rel_g[a][:], in_=rel_raw[:, a, 0:12])
 
         def fused(a):
-            return (8,) if a > 2 else (2, 5) if a == 1 else ()
+            return (2, 5) if a == 1 else (2,) if a > 5 else ()
 
         def products(a, xs, engine):
             for x in xs:
@@ -132,10 +130,11 @@ def tile_rangeviewmetakernelfourneighbour_x1_kernel(tc, rel, w1, b1, w2, b2, f, 
             cols = slice(t * 128, (t + 1) * 128)
             nc.tensor.matmul_mx(k_ps[a, t][:], lhsT=w_q[W2][:, cols].bitcast(FP8X4), lhsT_scale=w_s[W2][:, cols], rhs=m_q[a][0][:].bitcast(FP8X4), rhs_scale=m_q[a][1][:], start=True, stop=True)
 
-        def empty_k(a, t):
-            if t == 0:
+        def empty_k(a, t, j0=0, j1=J):
+            if a not in k_sb:
                 k_sb[a] = work.tile([128, 128, 2, 2, 4], F32, name="k_sb")
-            nc.scalar.activation(k_sb[a][:, :, t % 2, t // 2, :], k_ps[a, t][:].rearrange("p (n i) -> p n i", i=4), ACT.Identity, bias=b2c[:, t : t + 1])
+            src = k_ps[a, t][:, j0 * 128 : j1 * 128].rearrange("p (n i) -> p n i", i=4)
+            nc.scalar.activation(k_sb[a][:, j0 * 32 : j1 * 32, t % 2, t // 2, :], src, ACT.Identity, bias=b2c[:, t : t + 1])
 
         def turn_f(a, h, tag="f_ps", bufs=2):
             f_ps[a, h] = psum.tile([128, 2, 256], F32, name=tag, bufs=bufs)
@@ -197,6 +196,11 @@ def tile_rangeviewmetakernelfourneighbour_x1_kernel(tc, rel, w1, b1, w2, b2, f, 
                 else:
                     nc.vector.tensor_copy(out=o_w[a], in_=src)
 
+        def round_from_bank(a):
+            words = work.tile([128, 4, 2, 128, 2], BF16, name="o_w", align_bytes=64)
+            o_w[a] = words[:, 0]
+            nc.scalar.activation(o_w[a], o_ps[a][:].rearrange("n (h e m) -> n h m e", h=2, e=2), ACT.Identity)
+
         def turn_o(a0, a1, tag="a_ps", bufs=3):
             t_ps[a0] = psum.tile([128, 2, 2, 128], F32, name=tag, bufs=bufs)
             for a in range(a0, a1):
@@ -221,23 +225,30 @@ def tile_rangeviewmetakernelfourneighbour_x1_kernel(tc, rel, w1, b1, w2, b2, f, 
             if a >= 0:
                 fn(a, *args)
 
-        def shares(a):
-            early, n_g, n_v = (2, 3, 3)
-            xs = list((0, 3, 1, 4, 7, 2, 5, 8, 6, 9, 10, 11)) if a <= LAST else []
-            return xs[:early], xs[early : early + n_g], xs[early + n_g : early + n_g + n_v], xs[early + n_g + n_v :]
+        def first_stage(a):
+            mx1(a, 0)
+            mx1(a, 1)
+            mx1(a, 2, "a_ps", 3)
+            mx1(a, 3, "a_ps", 3)
 
-        nc.vector.tensor_copy(out=relf[:, 0, :], in_=rel_0[:])
+        def shares(a):
+            xs = [1, 0, 2, *range(3, 12)] if a <= LAST else []
+            return xs[:4], xs[9:], xs[4:5], xs[5:9]
+
+        nc.scalar.activation(relf[:, 0, :], rel_0[:], ACT.Identity)
         for i in range(3):
-            bank = psum.tile([128, 4, 128], BF16, name="a_ps", bufs=3)
-            for t in range(4):
-                nc.tensor.transpose(bank[:, t, :], w1_col[:, i, t : t + 1].to_broadcast([128, 128]), ident_bf[:])
+            bank = psum.tile([128, 2, 128], F32, name="a_ps", bufs=3)
+            for u in range(2):
+                nc.tensor.transpose(bank[:, u, :], w1_col[:, i, :].bitcast(F32)[:, u : u + 1].to_broadcast([128, 128]), ident[:])
+            src = bank[:].bitcast(BF16).rearrange("p u (m e) -> p u e m", e=2)
+            dst = w1p[i][:].rearrange("p (u e) m -> p u e m", e=2)
             if i > 0:
-                nc.scalar.copy(w1p[i][:], bank[:])
+                nc.scalar.copy(dst, src)
             else:
-                nc.vector.tensor_copy(out=w1p[i][:], in_=bank[:])
-        products(0, (0, 3, 6, 1, 2, 5, 9, 8, 11), "vector")
-        products(0, (4, 7, 10), "scalar")
-        nc.vector.tensor_copy(out=relf[:, 1:, :], in_=rel_raw[:, 1:, 0:12])
+                nc.vector.tensor_copy(out=dst, in_=src)
+        products(0, (0, 3, 1, 2, 4, 5, 6, 8, 11), "vector")
+        nc.scalar.activation(relf[:, 1:, :], rel_raw[:, 1:, 0:12], ACT.Identity)
+        products(0, (7, 9, 10), "scalar")
         nc.scalar.activation(b1c[:], b1_raw[:], ACT.Identity)
         turn_a(0, 0)
         turn_a(0, 1)
@@ -254,6 +265,7 @@ def tile_rangeviewmetakernelfourneighbour_x1_kernel(tc, rel, w1, b1, w2, b2, f, 
         products(1, range(9, 11), "scalar")
         empty_a(0, 2)
         products(1, range(11, 12), "scalar")
+        products(2, range(7, 8), "scalar")
         empty_a(0, 3)
         nc.scalar.activation(b2c[:], b2_raw[:], ACT.Identity)
         group_w(0)
@@ -261,10 +273,10 @@ def tile_rangeviewmetakernelfourneighbour_x1_kernel(tc, rel, w1, b1, w2, b2, f, 
         quant_w(0)
         turn_a(1, 0)
         turn_a(1, 1)
-        quant_w(1)
         leaky(0)
         products(2, (0,), "vector")
         quant_m(0)
+        quant_w(1)
         group_w_part(2, 0)
         group_w_part(2, 1)
         empty_a(1, 0)
@@ -272,73 +284,67 @@ def tile_rangeviewmetakernelfourneighbour_x1_kernel(tc, rel, w1, b1, w2, b2, f, 
         products(2, range(8, 9), "scalar")
         empty_a(1, 1)
         turn_a(1, 2)
-        mx1(0, 0)
-        mx1(0, 1)
+        first_stage(0)
         group_w_part(2, 3)
         products(2, range(9, 10), "scalar")
         empty_a(1, 2)
         turn_a(1, 3)
         turn_f(0, 0)
-        products(2, range(1, 8), "vector")
-        empty_k(0, 0)
-        empty_k(0, 1)
-        mx1(0, 2)
-        mx1(0, 3)
-        empty_a(1, 3)
+        products(2, range(1, 7), "vector")
         products(2, range(10, 12), "scalar")
-        turn_f(0, 1)
-        turn_a(2, 0)
-        products(3, shares(3)[0], "vector")
-        quant_w(2)
-        group_w(3)
         empty_k(0, 2)
         empty_k(0, 3)
+        empty_a(1, 3)
+        turn_a(2, 0)
+        turn_a(2, 1)
+        turn_f(0, 1)
+        quant_w(2)
+        group_w(3)
+        products(3, shares(3)[0], "vector")
+        empty_k(0, 0)
+        empty_k(0, 1)
         for s in range(2, LAST):
             early, on_g, on_v, on_s = shares(s + 1)
-            turn_a(s, 1)
-            on(leaky, s - 1)
-            empty_a(s, 0)
-            products(s + 1, on_v[:1], "vector")
-            cast_rel(s + 1)
+            leaky(s - 1)
             products(s + 1, on_s[:1], "scalar")
+            empty_a(s, 0)
+            products(s + 1, on_v, "vector")
+            cast_rel(s + 1)
+            products(s + 1, on_s[1:2], "scalar")
             empty_a(s, 1)
             turn_a(s, 2)
-            on(quant_m, s - 1)
-            products(s + 1, on_g, "gpsimd")
-            on(times_f, s - 2, 0, 2)
-            on(times_f, s - 2, 2, 4)
-            on(mx2, s - 3, 0, 4)
-            on(mx1, s - 1, 0)
-            on(mx1, s - 1, 1)
-            products(s + 1, on_s[1:2], "scalar")
-            empty_a(s, 2)
-            on(empty_o, s - 3)
             turn_a(s, 3)
-            on(turn_f, s - 1, 0)
-            products(s + 1, on_v[1:2], "vector")
+            quant_m(s - 1)
+            products(s + 1, on_g, "gpsimd")
+            times_f(s - 2, 0, 2)
+            times_f(s - 2, 2, 4)
+            products(s + 1, on_s[2:3], "scalar")
+            empty_a(s, 2)
+            on(mx2, s - 3, 0, 4)
+            first_stage(s - 1)
+            products(s + 1, on_s[3:], "scalar")
+            empty_a(s, 3)
+            on(empty_o, s - 3)
+            turn_f(s - 1, 0)
+            products(s + 2, shares(s + 2)[0][:1], "vector")
             if s == 2:
                 quant_w(3)
-            products(s + 1, on_s[2:3], "scalar")
-            on(empty_k, s - 1, 0)
-            on(empty_k, s - 1, 1)
-            on(mx1, s - 1, 2)
-            on(mx1, s - 1, 3)
-            products(s + 1, on_v[2:], "vector")
+            empty_k(s - 1, 2)
+            empty_k(s - 1, 3)
             if s < LAST - 1:
                 quant_p(s - 2)
-            empty_a(s, 3)
-            products(s + 1, on_s[3:], "scalar")
-            on(turn_f, s - 1, 1)
             turn_a(s + 1, 0)
-            products(s + 2, shares(s + 2)[0], "vector")
-            on(empty_k, s - 1, 2)
-            on(empty_k, s - 1, 3)
+            turn_a(s + 1, 1)
+            turn_f(s - 1, 1)
+            products(s + 2, shares(s + 2)[0][1:], "vector")
+            empty_k(s - 1, 0)
+            empty_k(s - 1, 1)
         a = LAST
-        turn_a(a, 1)
         leaky(a - 1)
         empty_a(a, 0)
-        turn_a(a, 2)
         empty_a(a, 1)
+        round_o((3,), "scalar")
+        turn_a(a, 2)
         turn_a(a, 3)
         quant_p(a - 3)
         quant_m(a - 1)
@@ -347,65 +353,59 @@ def tile_rangeviewmetakernelfourneighbour_x1_kernel(tc, rel, w1, b1, w2, b2, f, 
         times_f(a - 2, 0, 2)
         times_f(a - 2, 2, 4)
         empty_a(a, 2)
-        mx1(a - 1, 0)
-        mx1(a - 1, 1)
+        first_stage(a - 1)
         mx2(a - 3, 0, 4)
         empty_a(a, 3)
-        empty_k(a - 1, 0)
-        empty_k(a - 1, 1)
-        mx1(a - 1, 2)
-        mx1(a - 1, 3)
         turn_f(a - 1, 0)
         turn_f(a - 1, 1)
-        turn_o(0, 2)
         leaky(a)
-        empty_k(a - 1, 2)
-        empty_k(a - 1, 3)
-        round_o((3,), "scalar")
+        for t in (2, 3, 0, 1):
+            empty_k(a - 1, t)
         empty_o(a - 3)
+        turn_o(0, 2)
         turn_o(2, 4)
-        empty_t(0, 2)
         turn_f(a, 0, "a_ps", 3)
+        empty_t(0, 2)
         empty_t(2, 4)
         quant_p(a - 2)
         quant_m(a)
         round_o((4,), "gpsimd")
-        for t in range(2):
-            mx1(a, t)
-        mx1(a, 2, "a_ps", 3)
-        mx1(a, 3, "a_ps", 3)
+        first_stage(a)
         mx2(a - 2, 0, 4)
         times_f(a - 1, 0, 2)
         times_f(a - 1, 2, 4)
         for t in range(4):
-            empty_k(a, t)
+            empty_k(a, t, 0, 2)
+        for t in range(4):
+            empty_k(a, t, 2, 4)
         empty_o(a - 2)
         turn_f(a, 1)
         quant_o(0, 2)
         quant_p(a - 1)
         mx2(a - 1, 0, 4, "k_ps", 2)
-        round_o((5,), "gpsimd")
+        round_o((5,), "scalar")
+        round_from_bank(a - 1)
         empty_o(a - 1)
-        round_o((6,), "scalar")
         times_f(a, 0, 1)
         times_f(a, 1, 2)
         quant_p(a, 0, 1)
         times_f(a, 2, 3)
         quant_p(a, 1, 2)
-        turn_o(4, 6, "f_ps", 2)
-        empty_t(4, 6)
         mx2_turned(a, 0, 1)
         mx2(a, 0, 1)
+        turn_o(4, 6)
+        turn_o(6, 7, "k_ps", 2)
         mx2_turned(a, 1, 2)
         mx2(a, 1, 2)
-        turn_o(6, 7, "k_ps", 2)
+        empty_t(4, 6)
         times_f(a, 3, 4)
         quant_p(a, 2, 3)
         quant_p(a, 3, 4)
         empty_t(6, 7)
         mx2_turned(a, 2, 4)
         mx2(a, 2, 4)
-        quant_o(2, 6)
+        quant_o(2, 4)
+        quant_o(4, 6)
         empty_turned(a)
         empty_o(a)
         quant_o(6, 8)

@@ -51,9 +51,9 @@ def tile_rangeviewmetakernelfourneighbour_x1_kernel(tc, rel, w1, b1, w2, b2, f, 
         ident = keep.tile([128, 128], F32, name="ident")
         make_identity(nc, ident[:])
 
-        b1c = keep.tile([128, 4], F32, name="b1c")
-        b2c = keep.tile([128, 4], F32, name="b2c")
         relf = keep.tile([128, TILES, 12], F32, name="relf")
+        rel_last = keep.tile([128, TILES, J], BF16, name="rel_last")
+        w1c = keep.tile([128, 4], F32, name="w1c")
         w1p = [keep.tile([128, 4, 128], BF16, name=f"w1p{i}") for i in range(3)]
         w_q = [keep.tile([128, 512], U32, name=f"w_q{x}", align_bytes=64) for x in range(J + 1)]
         w_s = [keep.tile([128, 512], U8, name=f"w_s{x}", align_bytes=64) for x in range(J + 1)]
@@ -61,7 +61,7 @@ def tile_rangeviewmetakernelfourneighbour_x1_kernel(tc, rel, w1, b1, w2, b2, f, 
         o_s = keep.tile([128, N], U8, name="o_s", align_bytes=64)
         o_bf = keep.tile([128, 4 * N], BF16, name="o_bf", align_bytes=64)
 
-        w_grp, rel_g, prods, a_ps, a_sb, m_bf, m_q = {}, {}, {}, {}, {}, {}, {}
+        w_grp, rel_g, prods, a_ps, r_ps, u_sb, a_sb, m_bf, m_q = {}, {}, {}, {}, {}, {}, {}, {}, {}
         k_ps, k_sb, f_ps, p_bf, p_q = {}, {}, {}, {}, {}
         o_ps, r_sb, o_w, t_ps = {}, {}, {}, {}
 
@@ -85,16 +85,12 @@ def tile_rangeviewmetakernelfourneighbour_x1_kernel(tc, rel, w1, b1, w2, b2, f, 
             rel_g[a] = work.tile([128, 12], F32, name="rel_g")
             nc.vector.tensor_copy(out=rel_g[a][:], in_=rel_raw[:, a, 0:12])
 
-        def fused(a):
-            return (2, 5) if a == 1 else (2,) if a > 5 else ()
-
         def products(a, xs, engine):
             for x in xs:
-                prods[a, x] = work.tile([128, 512], F32, name="prod", bufs=24)
-                src = w1p[x % 3][:].rearrange("p t m -> p (t m)")
-                if x in fused(a):
-                    nc.vector.scalar_tensor_tensor(out=prods[a, x][:], in0=src, scalar=relf[:, a, x : x + 1], in1=prods[a, x - 1][:], op0=ALU.mult, op1=ALU.add)
-                elif engine == "gpsimd":
+                width = 256 if x % 3 == 2 and a < LAST else 512
+                prods[a, x] = work.tile([128, width], F32, name="prod", bufs=24)
+                src = w1p[x % 3][:].rearrange("p t m -> p (t m)")[:, :width]
+                if engine == "gpsimd":
                     nc.gpsimd.tensor_scalar(out=prods[a, x][:], in0=src, scalar1=rel_g[a][:, x : x + 1], scalar2=0.0, op0=ALU.mult, op1=ALU.add)
                 elif engine == "scalar":
                     nc.scalar.activation(prods[a, x][:], src, ACT.Identity, scale=relf[:, a, x : x + 1])
@@ -103,14 +99,29 @@ def tile_rangeviewmetakernelfourneighbour_x1_kernel(tc, rel, w1, b1, w2, b2, f, 
 
         def turn_a(a, t):
             a_ps[a, t] = psum.tile([128, 512], F32, name="a_ps", bufs=3)
+            terms = 3 if t < 2 or a == LAST else 2
             for j in range(J):
-                for i in (0, 2) if 3 * j + 2 in fused(a) else (0, 1, 2):
-                    nc.tensor.matmul(a_ps[a, t][:, j * 128 : (j + 1) * 128], lhsT=prods[a, 3 * j + i][:, t * 128 : (t + 1) * 128], rhs=ident[:], start=(i == 0), stop=(i == 2), is_transpose=True)
+                for i in range(terms):
+                    nc.tensor.matmul(a_ps[a, t][:, j * 128 : (j + 1) * 128], lhsT=prods[a, 3 * j + i][:, t * 128 : (t + 1) * 128], rhs=ident[:], start=(i == 0), stop=(i == terms - 1), is_transpose=True)
+
+        def spread_rel(a):
+            r_ps[a] = psum.tile([128, 2, 128], F32, name="o_ps")
+            words = rel_last[:, a, :].bitcast(F32)
+            for u in range(2):
+                nc.tensor.transpose(r_ps[a][:, u, :], words[:, u : u + 1].to_broadcast([128, 128]), ident[:])
+
+        def last_term(a, t):
+            u_sb[a, t] = work.tile([128, 128, J], F32, name="u_sb", bufs=4)
+            src = r_ps[a][:].bitcast(BF16).rearrange("p u (n e) -> p n u e", e=2)
+            nc.scalar.activation(u_sb[a, t][:].rearrange("p n (u e) -> p n u e", e=2), src, ACT.Identity, scale=w1c[:, t : t + 1], bias=b1_raw[:, t : t + 1])
+
+        def add_a(a, t):
+            nc.vector.tensor_tensor(out=a_sb[a][:, :, t, :], in0=a_ps[a, t][:].rearrange("p (j n) -> p n j", j=J), in1=u_sb[a, t][:], op=ALU.add)
 
         def empty_a(a, t):
             if t == 0:
                 a_sb[a] = work.tile([128, 128, 4, J], F32, name="a_sb")
-            nc.scalar.activation(a_sb[a][:, :, t, :], a_ps[a, t][:].rearrange("p (j n) -> p n j", j=J), ACT.Identity, bias=b1c[:, t : t + 1])
+            nc.scalar.activation(a_sb[a][:, :, t, :], a_ps[a, t][:].rearrange("p (j n) -> p n j", j=J), ACT.Identity, bias=b1_raw[:, t : t + 1])
 
         def take_m(a):
             m_bf[a] = work.tile([128, 2048], BF16, name="m_bf", align_bytes=64)
@@ -126,7 +137,8 @@ def tile_rangeviewmetakernelfourneighbour_x1_kernel(tc, rel, w1, b1, w2, b2, f, 
             nc.vector.quantize_mx(out=m_q[a][0][:].bitcast(FP8X4), scales=m_q[a][1][:], in_=m_bf[a][:])
 
         def mx1(a, t, tag="k_ps", bufs=2):
-            k_ps[a, t] = psum.tile([128, 512], F32, name=tag, bufs=bufs)
+            if (a, t) not in k_ps:
+                k_ps[a, t] = psum.tile([128, 512], F32, name=tag, bufs=bufs)
             cols = slice(t * 128, (t + 1) * 128)
             nc.tensor.matmul_mx(k_ps[a, t][:], lhsT=w_q[W2][:, cols].bitcast(FP8X4), lhsT_scale=w_s[W2][:, cols], rhs=m_q[a][0][:].bitcast(FP8X4), rhs_scale=m_q[a][1][:], start=True, stop=True)
 
@@ -134,7 +146,7 @@ def tile_rangeviewmetakernelfourneighbour_x1_kernel(tc, rel, w1, b1, w2, b2, f, 
             if a not in k_sb:
                 k_sb[a] = work.tile([128, 128, 2, 2, 4], F32, name="k_sb")
             src = k_ps[a, t][:, j0 * 128 : j1 * 128].rearrange("p (n i) -> p n i", i=4)
-            nc.scalar.activation(k_sb[a][:, j0 * 32 : j1 * 32, t % 2, t // 2, :], src, ACT.Identity, bias=b2c[:, t : t + 1])
+            nc.scalar.activation(k_sb[a][:, j0 * 32 : j1 * 32, t % 2, t // 2, :], src, ACT.Identity, bias=b2_raw[:, t : t + 1])
 
         def turn_f(a, h, tag="f_ps", bufs=2):
             f_ps[a, h] = psum.tile([128, 2, 256], F32, name=tag, bufs=bufs)
@@ -228,14 +240,13 @@ def tile_rangeviewmetakernelfourneighbour_x1_kernel(tc, rel, w1, b1, w2, b2, f, 
         def first_stage(a):
             mx1(a, 0)
             mx1(a, 1)
+            k_ps[a, 3] = psum.tile([128, 512], F32, name="a_ps", bufs=3)
             mx1(a, 2, "a_ps", 3)
             mx1(a, 3, "a_ps", 3)
 
-        def shares(a):
-            xs = [1, 0, 2, *range(3, 12)] if a <= LAST else []
-            return xs[:4], xs[9:], xs[4:5], xs[5:9]
-
+        nc.vector.tensor_copy(out=rel_last[:, 0, :], in_=rel_0[:, 2:12:3])
         nc.scalar.activation(relf[:, 0, :], rel_0[:], ACT.Identity)
+        nc.scalar.activation(w1c[:], w1_col[:, 2, :], ACT.Identity)
         for i in range(3):
             bank = psum.tile([128, 2, 128], F32, name="a_ps", bufs=3)
             for u in range(2):
@@ -246,101 +257,126 @@ def tile_rangeviewmetakernelfourneighbour_x1_kernel(tc, rel, w1, b1, w2, b2, f, 
                 nc.scalar.copy(dst, src)
             else:
                 nc.vector.tensor_copy(out=dst, in_=src)
+        spread_rel(0)
         products(0, (0, 3, 1, 2, 4, 5, 6, 8, 11), "vector")
         nc.scalar.activation(relf[:, 1:, :], rel_raw[:, 1:, 0:12], ACT.Identity)
         products(0, (7, 9, 10), "scalar")
-        nc.scalar.activation(b1c[:], b1_raw[:], ACT.Identity)
+        nc.vector.tensor_copy(out=rel_last[:, 1:, :], in_=rel_raw[:, 1:, 2:12:3])
         turn_a(0, 0)
         turn_a(0, 1)
-        group_w(W2)
-        products(1, (1,), "vector")
-        quant_w(W2)
-        products(1, (4, 0, 3, 2, 5), "vector")
-        products(1, range(6, 7), "scalar")
-        empty_a(0, 0)
-        products(1, range(7, 9), "scalar")
-        empty_a(0, 1)
         turn_a(0, 2)
+        group_w(W2)
+        products(1, (0,), "vector")
+        quant_w(W2)
+        products(1, (1, 2, 3, 4, 5), "vector")
+        last_term(0, 2)
+        empty_a(0, 0)
+        last_term(0, 3)
         turn_a(0, 3)
-        products(1, range(9, 11), "scalar")
-        empty_a(0, 2)
-        products(1, range(11, 12), "scalar")
-        products(2, range(7, 8), "scalar")
-        empty_a(0, 3)
-        nc.scalar.activation(b2c[:], b2_raw[:], ACT.Identity)
+        spread_rel(1)
+        products(1, (6, 7), "scalar")
+        empty_a(0, 1)
+        products(1, (8, 9, 10, 11), "scalar")
         group_w(0)
-        group_w(1)
-        quant_w(0)
+        cast_rel(2)
+        products(2, (0, 1), "vector")
+        products(2, (2, 3), "gpsimd")
+        add_a(0, 2)
         turn_a(1, 0)
+        add_a(0, 3)
+        quant_w(0)
         turn_a(1, 1)
         leaky(0)
-        products(2, (0,), "vector")
+        products(2, (4,), "vector")
         quant_m(0)
-        quant_w(1)
-        group_w_part(2, 0)
-        group_w_part(2, 1)
+        last_term(1, 2)
+        last_term(1, 3)
+        group_w_part(1, 0)
         empty_a(1, 0)
-        group_w_part(2, 2)
-        products(2, range(8, 9), "scalar")
-        empty_a(1, 1)
+        group_w_part(1, 1)
+        group_w_part(1, 2)
         turn_a(1, 2)
-        first_stage(0)
-        group_w_part(2, 3)
-        products(2, range(9, 10), "scalar")
-        empty_a(1, 2)
+        mx1(0, 0)
+        mx1(0, 1)
+        mx1(0, 2, "a_ps", 3)
+        mx1(0, 3, "o_ps", 1)
+        empty_a(1, 1)
         turn_a(1, 3)
-        turn_f(0, 0)
-        products(2, range(1, 7), "vector")
-        products(2, range(10, 12), "scalar")
-        empty_k(0, 2)
+        group_w_part(1, 3)
+        group_w_part(2, 0)
+        products(2, (5, 6, 7, 8), "vector")
+        products(2, (9,), "scalar")
+        group_w(3)
+        group_w_part(2, 1)
         empty_k(0, 3)
-        empty_a(1, 3)
+        empty_k(0, 2)
+        turn_f(0, 0)
+        spread_rel(2)
+        cast_rel(2)
+        quant_w(1)
+        products(2, (10, 11), "gpsimd")
+        add_a(1, 2)
+        add_a(1, 3)
         turn_a(2, 0)
         turn_a(2, 1)
         turn_f(0, 1)
-        quant_w(2)
-        group_w(3)
-        products(3, shares(3)[0], "vector")
+        quant_w(3)
+        group_w_part(2, 2)
         empty_k(0, 0)
         empty_k(0, 1)
         for s in range(2, LAST):
-            early, on_g, on_v, on_s = shares(s + 1)
+            on_v, on_s = {2: ((0,), (1, 2, 3, 4, 5)), 3: ((5,), (0, 1, 3, 4)), 4: ((5,), (0, 1, 3, 4)), 6: ((0, 1), (3, 4, 5, 8))}.get(s, ((0,), (1, 3, 4, 5)))
             leaky(s - 1)
-            products(s + 1, on_s[:1], "scalar")
-            empty_a(s, 0)
+            if s == 2:
+                empty_a(s, 0)
+            last_term(s, 2)
+            last_term(s, 3)
+            if s > 2:
+                empty_a(s, 0)
             products(s + 1, on_v, "vector")
+            if s == 2:
+                group_w_part(2, 3)
             cast_rel(s + 1)
-            products(s + 1, on_s[1:2], "scalar")
-            empty_a(s, 1)
             turn_a(s, 2)
             turn_a(s, 3)
             quant_m(s - 1)
-            products(s + 1, on_g, "gpsimd")
+            products(s + 1, (6, 7, 8, 9, 10, 11) if s < LAST - 1 else (6, 7, 9, 10, 11), "gpsimd")
+            if s > 2:
+                empty_k(s - 2, 0)
+                empty_k(s - 2, 1)
+            empty_a(s, 1)
             times_f(s - 2, 0, 2)
+            add_a(s, 2)
+            add_a(s, 3)
             times_f(s - 2, 2, 4)
-            products(s + 1, on_s[2:3], "scalar")
-            empty_a(s, 2)
+            products(s + 1, on_s[:2], "scalar")
             on(mx2, s - 3, 0, 4)
-            first_stage(s - 1)
-            products(s + 1, on_s[3:], "scalar")
-            empty_a(s, 3)
-            on(empty_o, s - 3)
-            turn_f(s - 1, 0)
-            products(s + 2, shares(s + 2)[0][:1], "vector")
-            if s == 2:
-                quant_w(3)
-            empty_k(s - 1, 2)
-            empty_k(s - 1, 3)
             if s < LAST - 1:
+                first_stage(s - 1)
+                on(empty_o, s - 3)
+            else:
+                mx1(s - 1, 0)
+                mx1(s - 1, 1)
+                mx1(s - 1, 2, "a_ps", 3)
+                empty_o(s - 3)
+                mx1(s - 1, 3, "o_ps", 1)
+            products(s + 1, on_s[2:], "scalar")
+            turn_f(s - 1, 0)
+            if s < LAST - 1:
+                spread_rel(s + 1)
+                if s == 2:
+                    quant_w(2)
+                products(s + 2, (2,), "vector")
                 quant_p(s - 2)
+            empty_k(s - 1, 3)
+            empty_k(s - 1, 2)
             turn_a(s + 1, 0)
             turn_a(s + 1, 1)
             turn_f(s - 1, 1)
-            products(s + 2, shares(s + 2)[0][1:], "vector")
-            empty_k(s - 1, 0)
-            empty_k(s - 1, 1)
         a = LAST
         leaky(a - 1)
+        empty_k(a - 2, 0)
+        empty_k(a - 2, 1)
         empty_a(a, 0)
         empty_a(a, 1)
         round_o((3,), "scalar")
@@ -354,10 +390,10 @@ def tile_rangeviewmetakernelfourneighbour_x1_kernel(tc, rel, w1, b1, w2, b2, f, 
         times_f(a - 2, 2, 4)
         empty_a(a, 2)
         first_stage(a - 1)
-        mx2(a - 3, 0, 4)
         empty_a(a, 3)
         turn_f(a - 1, 0)
         turn_f(a - 1, 1)
+        mx2(a - 3, 0, 4)
         leaky(a)
         for t in (2, 3, 0, 1):
             empty_k(a - 1, t)

@@ -33,13 +33,15 @@ def tile_rangeviewmetakernelfourneighbour_x1_kernel(tc, rel, w1, b1, w2, b2, f, 
         w1_col = keep.tile([128, 3, 4], BF16, name="w1_col")
         b1_raw = keep.tile([128, 4], BF16, name="b1_raw")
         b2_raw = keep.tile([128, 4], BF16, name="b2_raw")
-        w_raw = [keep.tile([128, 4, 512], BF16, name=f"w_raw{x}") for x in range(J + 1)]
+        w_raw = [keep.tile([128, 4, 512], BF16, name=f"w_raw{x}") for x in range(J)]
+        w2_raw = [keep.tile([128, 4, 128], BF16, name=f"w2_raw{u}") for u in range(4)]
         f_sb = [keep.tile([128, J, 512], BF16, name=f"f_sb{a}") for a in range(TILES)]
 
         rel_rows = rel.rearrange("(a p) j i -> p a (j i)", p=128)
         nc.sync.dma_start(out=w1_col[:], in_=w1.rearrange("i (p t) -> p i t", t=4))
         nc.sync.dma_start(out=rel_0[:], in_=rel_rows[:, 0, :])
-        nc.sync.dma_start(out=w_raw[W2][:], in_=w2.rearrange("(p k) c -> p k c", k=4))
+        for u in range(4):
+            nc.sync.dma_start(out=w2_raw[u][:], in_=w2.rearrange("(p k) c -> p k c", k=4)[:, :, u * 128 : (u + 1) * 128])
         nc.sync.dma_start(out=b1_raw[:], in_=b1.rearrange("(p t) -> p t", t=4))
         nc.sync.dma_start(out=rel_raw[:, 1:, 0:12], in_=rel_rows[:, 1:, :])
         nc.sync.dma_start(out=b2_raw[:], in_=b2.rearrange("(p t) -> p t", t=4))
@@ -62,13 +64,18 @@ def tile_rangeviewmetakernelfourneighbour_x1_kernel(tc, rel, w1, b1, w2, b2, f, 
         o_bf = keep.tile([128, 4 * N], BF16, name="o_bf", align_bytes=64)
 
         w_grp, rel_g, prods, a_ps, r_ps, u_sb, a_sb, m_bf, m_q = {}, {}, {}, {}, {}, {}, {}, {}, {}
-        k_ps, k_sb, f_ps, p_bf, p_q = {}, {}, {}, {}, {}
+        k_ps, k_sb, f_ps, f_w, p_bf, p_q = {}, {}, {}, {}, {}, {}
         o_ps, r_sb, o_w, t_ps = {}, {}, {}, {}
+
+        def group_w2(u):
+            if u == 0:
+                w_grp[W2] = work.tile([128, 2048], BF16, name="w_grp", align_bytes=64, bufs=3)
+            dst = w_grp[W2][:].rearrange("p (t m k) -> p m k t", t=4, k=4)[:, u * 32 : (u + 1) * 32]
+            nc.vector.tensor_copy(out=dst, in_=w2_raw[u][:].rearrange("p k (m t) -> p m k t", t=4))
 
         def group_w(x):
             w_grp[x] = work.tile([128, 2048], BF16, name="w_grp", align_bytes=64, bufs=3)
-            slots = "g e" if x == W2 else "e g"
-            dst = w_grp[x][:].rearrange(f"p (t m {slots}) -> p m g e t", t=4, e=2, g=2)
+            dst = w_grp[x][:].rearrange("p (t m e g) -> p m g e t", t=4, e=2, g=2)
             nc.vector.tensor_copy(out=dst, in_=w_raw[x][:].rearrange("p (g e) (m t) -> p m g e t", t=4, e=2))
 
         def group_w_part(x, part):
@@ -88,7 +95,7 @@ def tile_rangeviewmetakernelfourneighbour_x1_kernel(tc, rel, w1, b1, w2, b2, f, 
         def products(a, xs, engine):
             for x in xs:
                 width = 256 if x % 3 == 2 and a < LAST else 512
-                prods[a, x] = work.tile([128, width], F32, name="prod", bufs=24)
+                prods[a, x] = work.tile([128, width], F32, name="prod", bufs=28)
                 src = w1p[x % 3][:].rearrange("p t m -> p (t m)")[:, :width]
                 if engine == "gpsimd":
                     nc.gpsimd.tensor_scalar(out=prods[a, x][:], in0=src, scalar1=rel_g[a][:, x : x + 1], scalar2=0.0, op0=ALU.mult, op1=ALU.add)
@@ -97,10 +104,11 @@ def tile_rangeviewmetakernelfourneighbour_x1_kernel(tc, rel, w1, b1, w2, b2, f, 
                 else:
                     nc.vector.tensor_scalar(out=prods[a, x][:], in0=src, scalar1=relf[:, a, x : x + 1], scalar2=None, op0=ALU.mult)
 
-        def turn_a(a, t):
-            a_ps[a, t] = psum.tile([128, 512], F32, name="a_ps", bufs=3)
+        def turn_a(a, t, js=range(J)):
+            if (a, t) not in a_ps:
+                a_ps[a, t] = psum.tile([128, 512], F32, name="a_ps", bufs=3)
             terms = 3 if t < 2 or a == LAST else 2
-            for j in range(J):
+            for j in js:
                 for i in range(terms):
                     nc.tensor.matmul(a_ps[a, t][:, j * 128 : (j + 1) * 128], lhsT=prods[a, 3 * j + i][:, t * 128 : (t + 1) * 128], rhs=ident[:], start=(i == 0), stop=(i == terms - 1), is_transpose=True)
 
@@ -115,12 +123,16 @@ def tile_rangeviewmetakernelfourneighbour_x1_kernel(tc, rel, w1, b1, w2, b2, f, 
             src = r_ps[a][:].bitcast(BF16).rearrange("p u (n e) -> p n u e", e=2)
             nc.scalar.activation(u_sb[a, t][:].rearrange("p n (u e) -> p n u e", e=2), src, ACT.Identity, scale=w1c[:, t : t + 1], bias=b1_raw[:, t : t + 1])
 
+        def take_a(a):
+            if a not in a_sb:
+                a_sb[a] = work.tile([128, 128, 4, J], F32, name="a_sb")
+
         def add_a(a, t):
+            take_a(a)
             nc.vector.tensor_tensor(out=a_sb[a][:, :, t, :], in0=a_ps[a, t][:].rearrange("p (j n) -> p n j", j=J), in1=u_sb[a, t][:], op=ALU.add)
 
         def empty_a(a, t):
-            if t == 0:
-                a_sb[a] = work.tile([128, 128, 4, J], F32, name="a_sb")
+            take_a(a)
             nc.scalar.activation(a_sb[a][:, :, t, :], a_ps[a, t][:].rearrange("p (j n) -> p n j", j=J), ACT.Identity, bias=b1_raw[:, t : t + 1])
 
         def take_m(a):
@@ -164,6 +176,18 @@ def tile_rangeviewmetakernelfourneighbour_x1_kernel(tc, rel, w1, b1, w2, b2, f, 
             out = p_bf[a][:, j0 * 512 : j1 * 512].rearrange("p (n i e g) -> p n g i e", i=4, e=2, g=2)
             nc.vector.tensor_tensor(out=out, in0=fv, in1=kv, op=ALU.mult)
 
+        def empty_f(a, j):
+            f_w[a] = work.tile([128, 32, 2, 4], F32, name="f_w")
+            src = f_ps[a, j // 2][:, :, j % 2 * 128 : (j % 2 + 1) * 128].rearrange("p g (n i) -> p g n i", i=4)
+            nc.scalar.copy(f_w[a][:].rearrange("p n g i -> p g n i"), src)
+
+        def times_f_gpsimd(a, j):
+            if a not in p_bf:
+                p_bf[a] = work.tile([128, 2048], BF16, name="p_bf", align_bytes=64)
+            fv = f_w[a][:].rearrange("p n g i -> p n (g i)").bitcast(BF16).rearrange("p n (g i e) -> p n e g i", g=2, e=2)
+            out = p_bf[a][:, j * 512 : (j + 1) * 512].rearrange("p (n i e g) -> p n e g i", i=4, e=2, g=2)
+            nc.gpsimd.tensor_tensor(out=out, in0=k_sb[a][:, j * 32 : (j + 1) * 32], in1=fv, op=ALU.mult)
+
         def quant_p(a, j0=0, j1=J):
             if a not in p_q:
                 p_q[a] = (work.tile([128, 512], U32, name="p_q", align_bytes=64, bufs=3), work.tile([128, 512], U8, name="p_s", align_bytes=64, bufs=3))
@@ -197,7 +221,7 @@ def tile_rangeviewmetakernelfourneighbour_x1_kernel(tc, rel, w1, b1, w2, b2, f, 
 
         def round_o(tiles, engine):
             tag = "m_bf" if engine == "gpsimd" else "o_w"
-            words = work.tile([128, 4, 2, 128, 2], BF16, name=tag, align_bytes=64)
+            words = work.tile([128, len(tiles), 2, 128, 2], BF16, name=tag, align_bytes=64)
             for x, a in enumerate(tiles):
                 o_w[a] = words[:, x]
                 src = r_sb[a][:].rearrange("n (m h e) -> n h m e", h=2, e=2)
@@ -209,7 +233,7 @@ def tile_rangeviewmetakernelfourneighbour_x1_kernel(tc, rel, w1, b1, w2, b2, f, 
                     nc.vector.tensor_copy(out=o_w[a], in_=src)
 
         def round_from_bank(a):
-            words = work.tile([128, 4, 2, 128, 2], BF16, name="o_w", align_bytes=64)
+            words = work.tile([128, 1, 2, 128, 2], BF16, name="o_w", align_bytes=64)
             o_w[a] = words[:, 0]
             nc.scalar.activation(o_w[a], o_ps[a][:].rearrange("n (h e m) -> n h m e", h=2, e=2), ACT.Identity)
 
@@ -247,6 +271,7 @@ def tile_rangeviewmetakernelfourneighbour_x1_kernel(tc, rel, w1, b1, w2, b2, f, 
         nc.vector.tensor_copy(out=rel_last[:, 0, :], in_=rel_0[:, 2:12:3])
         nc.scalar.activation(relf[:, 0, :], rel_0[:], ACT.Identity)
         nc.scalar.activation(w1c[:], w1_col[:, 2, :], ACT.Identity)
+        group_w2(0)
         for i in range(3):
             bank = psum.tile([128, 2, 128], F32, name="a_ps", bufs=3)
             for u in range(2):
@@ -258,36 +283,41 @@ def tile_rangeviewmetakernelfourneighbour_x1_kernel(tc, rel, w1, b1, w2, b2, f, 
             else:
                 nc.vector.tensor_copy(out=dst, in_=src)
         spread_rel(0)
-        products(0, (0, 3, 1, 2, 4, 5, 6, 8, 11), "vector")
+        group_w2(1)
+        products(0, (0, 1, 3, 4, 6, 9), "vector")
         nc.scalar.activation(relf[:, 1:, :], rel_raw[:, 1:, 0:12], ACT.Identity)
-        products(0, (7, 9, 10), "scalar")
+        products(0, (7, 10), "scalar")
+        products(0, (2, 5, 8, 11), "vector")
         nc.vector.tensor_copy(out=rel_last[:, 1:, :], in_=rel_raw[:, 1:, 2:12:3])
+        for j in range(J):
+            turn_a(0, 2, (j,))
+            turn_a(0, 3, (j,))
         turn_a(0, 0)
-        turn_a(0, 1)
-        turn_a(0, 2)
-        group_w(W2)
-        products(1, (0,), "vector")
-        quant_w(W2)
-        products(1, (1, 2, 3, 4, 5), "vector")
         last_term(0, 2)
-        empty_a(0, 0)
         last_term(0, 3)
-        turn_a(0, 3)
-        spread_rel(1)
-        products(1, (6, 7), "scalar")
-        empty_a(0, 1)
-        products(1, (8, 9, 10, 11), "scalar")
-        group_w(0)
-        cast_rel(2)
-        products(2, (0, 1), "vector")
-        products(2, (2, 3), "gpsimd")
+        group_w2(2)
+        group_w2(3)
+        products(1, (0,), "vector")
+        cast_rel(1)
+        quant_w(W2)
+        products(1, (10, 11), "gpsimd")
         add_a(0, 2)
-        turn_a(1, 0)
         add_a(0, 3)
-        quant_w(0)
+        turn_a(0, 1)
+        spread_rel(1)
+        products(1, (1, 2, 3, 5), "vector")
+        products(1, (4, 6, 7, 8), "scalar")
+        products(2, (4,), "scalar")
+        empty_a(0, 0)
+        products(1, (9,), "scalar")
+        products(2, (9,), "scalar")
+        empty_a(0, 1)
+        group_w(0)
+        turn_a(1, 0)
         turn_a(1, 1)
+        products(2, (0, 1), "vector")
         leaky(0)
-        products(2, (4,), "vector")
+        quant_w(0)
         quant_m(0)
         last_term(1, 2)
         last_term(1, 3)
@@ -304,28 +334,28 @@ def tile_rangeviewmetakernelfourneighbour_x1_kernel(tc, rel, w1, b1, w2, b2, f, 
         turn_a(1, 3)
         group_w_part(1, 3)
         group_w_part(2, 0)
-        products(2, (5, 6, 7, 8), "vector")
-        products(2, (9,), "scalar")
+        products(2, (2, 3, 5, 6, 8, 11), "vector")
+        products(2, (7,), "scalar")
         group_w(3)
         group_w_part(2, 1)
         empty_k(0, 3)
         empty_k(0, 2)
         turn_f(0, 0)
         spread_rel(2)
-        cast_rel(2)
         quant_w(1)
-        products(2, (10, 11), "gpsimd")
+        cast_rel(2)
+        products(2, (10,), "gpsimd")
         add_a(1, 2)
         add_a(1, 3)
+        quant_w(3)
         turn_a(2, 0)
         turn_a(2, 1)
         turn_f(0, 1)
-        quant_w(3)
         group_w_part(2, 2)
         empty_k(0, 0)
         empty_k(0, 1)
         for s in range(2, LAST):
-            on_v, on_s = {2: ((0,), (1, 2, 3, 4, 5)), 3: ((5,), (0, 1, 3, 4)), 4: ((5,), (0, 1, 3, 4)), 6: ((0, 1), (3, 4, 5, 8))}.get(s, ((0,), (1, 3, 4, 5)))
+            on_v, on_s = {2: ((0,), (1, 2, 3, 4, 5, 8)), 3: ((5,), (0, 1, 3, 4, 8)), 4: ((5,), (0, 1, 3, 4, 8)), 5: ((0,), (1, 3, 4, 5, 8)), 6: ((0, 1, 3), (4, 5, 6, 7))}.get(s, ((0,), (1, 3, 4, 5)))
             leaky(s - 1)
             if s == 2:
                 empty_a(s, 0)
@@ -340,7 +370,7 @@ def tile_rangeviewmetakernelfourneighbour_x1_kernel(tc, rel, w1, b1, w2, b2, f, 
             turn_a(s, 2)
             turn_a(s, 3)
             quant_m(s - 1)
-            products(s + 1, (6, 7, 8, 9, 10, 11) if s < LAST - 1 else (6, 7, 9, 10, 11), "gpsimd")
+            products(s + 1, (6, 7, 9, 10, 11) if s < LAST - 1 else (8, 9, 10, 11), "gpsimd")
             if s > 2:
                 empty_k(s - 2, 0)
                 empty_k(s - 2, 1)
@@ -379,13 +409,13 @@ def tile_rangeviewmetakernelfourneighbour_x1_kernel(tc, rel, w1, b1, w2, b2, f, 
         empty_k(a - 2, 1)
         empty_a(a, 0)
         empty_a(a, 1)
-        round_o((3,), "scalar")
+        round_o((2, 3), "scalar")
         turn_a(a, 2)
         turn_a(a, 3)
         quant_p(a - 3)
         quant_m(a - 1)
         take_m(a)
-        round_o((0, 1, 2), "gpsimd")
+        round_o((0, 1), "gpsimd")
         times_f(a - 2, 0, 2)
         times_f(a - 2, 2, 4)
         empty_a(a, 2)
@@ -416,9 +446,11 @@ def tile_rangeviewmetakernelfourneighbour_x1_kernel(tc, rel, w1, b1, w2, b2, f, 
             empty_k(a, t, 2, 4)
         empty_o(a - 2)
         turn_f(a, 1)
-        quant_o(0, 2)
-        quant_p(a - 1)
+        turn_o(4, 5, "f_ps", 2)
+        quant_p(a - 1, 0, 2)
+        quant_p(a - 1, 2, 4)
         mx2(a - 1, 0, 4, "k_ps", 2)
+        empty_t(4, 5)
         round_o((5,), "scalar")
         round_from_bank(a - 1)
         empty_o(a - 1)
@@ -429,18 +461,16 @@ def tile_rangeviewmetakernelfourneighbour_x1_kernel(tc, rel, w1, b1, w2, b2, f, 
         quant_p(a, 1, 2)
         mx2_turned(a, 0, 1)
         mx2(a, 0, 1)
-        turn_o(4, 6)
-        turn_o(6, 7, "k_ps", 2)
         mx2_turned(a, 1, 2)
         mx2(a, 1, 2)
-        empty_t(4, 6)
+        turn_o(5, 7)
+        empty_t(5, 7)
         times_f(a, 3, 4)
         quant_p(a, 2, 3)
         quant_p(a, 3, 4)
-        empty_t(6, 7)
         mx2_turned(a, 2, 4)
         mx2(a, 2, 4)
-        quant_o(2, 4)
+        quant_o(0, 4)
         quant_o(4, 6)
         empty_turned(a)
         empty_o(a)

@@ -355,7 +355,7 @@ def tile_rangeviewmetakernelfourneighbour_x1_kernel(tc, rel, w1, b1, w2, b2, f, 
         empty_k(0, 0)
         empty_k(0, 1)
         for s in range(2, LAST):
-            on_v, on_s = {2: ((0,), (1, 2, 3, 4, 5, 8)), 3: ((5,), (0, 1, 3, 4, 8)), 4: ((5,), (0, 1, 3, 4, 8)), 5: ((0,), (1, 3, 4, 5, 8)), 6: ((0, 1, 3), (4, 5, 6, 7))}.get(s, ((0,), (1, 3, 4, 5)))
+            on_v, on_s = {2: ((0,), (1, 2, 3, 4, 5, 8, 11)), 3: ((5, 8), (0, 1, 3, 4, 11)), 4: ((0, 5), (1, 3, 4, 8, 11)), 5: ((0, 5), (1, 3, 4, 8, 11)), 6: ((0, 1, 3), (4, 5, 6, 7))}.get(s, ((0,), (1, 3, 4, 5)))
             leaky(s - 1)
             if s == 2:
                 empty_a(s, 0)
@@ -370,7 +370,7 @@ def tile_rangeviewmetakernelfourneighbour_x1_kernel(tc, rel, w1, b1, w2, b2, f, 
             turn_a(s, 2)
             turn_a(s, 3)
             quant_m(s - 1)
-            products(s + 1, (6, 7, 9, 10, 11) if s < LAST - 1 else (8, 9, 10, 11), "gpsimd")
+            products(s + 1, (6, 7, 9, 10) if s < LAST - 1 else (8, 9, 10, 11), "gpsimd")
             if s > 2:
                 empty_k(s - 2, 0)
                 empty_k(s - 2, 1)
@@ -400,8 +400,14 @@ def tile_rangeviewmetakernelfourneighbour_x1_kernel(tc, rel, w1, b1, w2, b2, f, 
                 quant_p(s - 2)
             empty_k(s - 1, 3)
             empty_k(s - 1, 2)
-            turn_a(s + 1, 0)
-            turn_a(s + 1, 1)
+            if s == LAST - 1:
+                turn_a(s + 1, 0, range(3))
+                turn_a(s + 1, 1, range(3))
+                turn_a(s + 1, 0, (3,))
+                turn_a(s + 1, 1, (3,))
+            else:
+                turn_a(s + 1, 0)
+                turn_a(s + 1, 1)
             turn_f(s - 1, 1)
         a = LAST
         leaky(a - 1)
@@ -471,8 +477,9 @@ def tile_rangeviewmetakernelfourneighbour_x1_kernel(tc, rel, w1, b1, w2, b2, f, 
         mx2_turned(a, 2, 4)
         mx2(a, 2, 4)
         quant_o(0, 4)
-        quant_o(4, 6)
+        quant_o(4, 5)
         empty_turned(a)
         empty_o(a)
-        quant_o(6, 8)
+        quant_o(5, 7)
+        quant_o(7, 8)
         store_scales(0, 1024, [nc.scalar, nc.scalar, nc.sync, nc.sync])

@@ -119,9 +119,9 @@ def tile_rangeviewmetakernelfourneighbour_x1_kernel(tc, rel, w1, b1, w2, b2, f, 
                 nc.tensor.transpose(r_ps[a][:, u, :], words[:, u : u + 1].to_broadcast([128, 128]), ident[:])
 
         def last_term(a, t):
-            u_sb[a, t] = work.tile([128, 128, J], F32, name="u_sb", bufs=4)
-            src = r_ps[a][:].bitcast(BF16).rearrange("p u (n e) -> p n u e", e=2)
-            nc.scalar.activation(u_sb[a, t][:].rearrange("p n (u e) -> p n u e", e=2), src, ACT.Identity, scale=w1c[:, t : t + 1], bias=b1_raw[:, t : t + 1])
+            u_sb[a, t] = work.tile([128, 512], F32, name="u_sb", bufs=4)
+            src = r_ps[a][:].bitcast(BF16).rearrange("p u x -> p (u x)")
+            nc.scalar.activation(u_sb[a, t][:], src, ACT.Identity, scale=w1c[:, t : t + 1], bias=b1_raw[:, t : t + 1])
 
         def take_a(a):
             if a not in a_sb:
@@ -129,7 +129,9 @@ def tile_rangeviewmetakernelfourneighbour_x1_kernel(tc, rel, w1, b1, w2, b2, f, 
 
         def add_a(a, t):
             take_a(a)
-            nc.vector.tensor_tensor(out=a_sb[a][:, :, t, :], in0=a_ps[a, t][:].rearrange("p (j n) -> p n j", j=J), in1=u_sb[a, t][:], op=ALU.add)
+            out = a_sb[a][:, :, t, :].rearrange("p n (u e) -> p n u e", e=2)
+            sums = a_ps[a, t][:].rearrange("p (u e n) -> p n u e", u=2, e=2)
+            nc.vector.tensor_tensor(out=out, in0=sums, in1=u_sb[a, t][:].rearrange("p (u n e) -> p n u e", u=2, e=2), op=ALU.add)
 
         def empty_a(a, t):
             take_a(a)
@@ -138,15 +140,18 @@ def tile_rangeviewmetakernelfourneighbour_x1_kernel(tc, rel, w1, b1, w2, b2, f, 
         def take_m(a):
             m_bf[a] = work.tile([128, 2048], BF16, name="m_bf", align_bytes=64)
 
-        def leaky(a):
+        def leaky(a, j0=0, j1=J):
             if a not in m_bf:
                 take_m(a)
-            src = a_sb[a][:].rearrange("p n t j -> p (n t) j")
-            nc.vector.scalar_tensor_tensor(out=m_bf[a][:].rearrange("p (j x) -> p x j", j=J), in0=src, scalar=SLOPE, in1=src, op0=ALU.mult, op1=ALU.max)
+            src = a_sb[a][:].rearrange("p n t j -> p (n t) j")[:, :, j0:j1]
+            out = m_bf[a][:].rearrange("p (j x) -> p x j", j=J)[:, :, j0:j1]
+            nc.vector.scalar_tensor_tensor(out=out, in0=src, scalar=SLOPE, in1=src, op0=ALU.mult, op1=ALU.max)
 
-        def quant_m(a):
-            m_q[a] = (work.tile([128, 512], U32, name="m_q", align_bytes=64), work.tile([128, 512], U8, name="m_s", align_bytes=64))
-            nc.vector.quantize_mx(out=m_q[a][0][:].bitcast(FP8X4), scales=m_q[a][1][:], in_=m_bf[a][:])
+        def quant_m(a, j0=0, j1=J):
+            if a not in m_q:
+                m_q[a] = (work.tile([128, 512], U32, name="m_q", align_bytes=64), work.tile([128, 512], U8, name="m_s", align_bytes=64))
+            cols = slice(j0 * 128, j1 * 128)
+            nc.vector.quantize_mx(out=m_q[a][0][:, cols].bitcast(FP8X4), scales=m_q[a][1][:, cols], in_=m_bf[a][:, j0 * 512 : j1 * 512])
 
         def mx1(a, t, tag="k_ps", bufs=2):
             if (a, t) not in k_ps:
@@ -326,21 +331,22 @@ def tile_rangeviewmetakernelfourneighbour_x1_kernel(tc, rel, w1, b1, w2, b2, f, 
         group_w_part(1, 1)
         group_w_part(1, 2)
         turn_a(1, 2)
+        turn_a(1, 3)
         mx1(0, 0)
         mx1(0, 1)
-        mx1(0, 2, "a_ps", 3)
-        mx1(0, 3, "o_ps", 1)
+        turn_f(0, 0)
+        turn_f(0, 1)
         empty_a(1, 1)
-        turn_a(1, 3)
         group_w_part(1, 3)
         group_w_part(2, 0)
         products(2, (2, 3, 5, 6, 8, 11), "vector")
         products(2, (7,), "scalar")
         group_w(3)
         group_w_part(2, 1)
-        empty_k(0, 3)
-        empty_k(0, 2)
-        turn_f(0, 0)
+        empty_k(0, 0)
+        empty_k(0, 1)
+        mx1(0, 2)
+        mx1(0, 3)
         spread_rel(2)
         quant_w(1)
         cast_rel(2)
@@ -350,76 +356,59 @@ def tile_rangeviewmetakernelfourneighbour_x1_kernel(tc, rel, w1, b1, w2, b2, f, 
         quant_w(3)
         turn_a(2, 0)
         turn_a(2, 1)
-        turn_f(0, 1)
         group_w_part(2, 2)
-        empty_k(0, 0)
-        empty_k(0, 1)
+        empty_k(0, 2)
+        empty_k(0, 3)
+        group_w_part(2, 3)
         for s in range(2, LAST):
-            on_v, on_s = {2: ((0,), (1, 2, 3, 4, 5, 8, 11)), 3: ((5, 8), (0, 1, 3, 4, 11)), 4: ((0, 5), (1, 3, 4, 8, 11)), 5: ((0, 5), (1, 3, 4, 8, 11)), 6: ((0, 1, 3), (4, 5, 6, 7))}.get(s, ((0,), (1, 3, 4, 5)))
+            on_v, on_s = {2: ((0, 5, 8), (1, 2, 3, 10, 11)), 3: ((5, 8), (0, 1, 3, 10, 11)), 4: ((0, 5), (1, 3, 8, 10, 11)), 5: ((0, 5), (1, 3, 8, 10, 11)), 6: ((0, 1, 3), (4, 5, 10, 11))}[s]
             leaky(s - 1)
-            if s == 2:
-                empty_a(s, 0)
+            empty_a(s, 0)
             last_term(s, 2)
             last_term(s, 3)
-            if s > 2:
-                empty_a(s, 0)
             products(s + 1, on_v, "vector")
-            if s == 2:
-                group_w_part(2, 3)
             cast_rel(s + 1)
+            empty_a(s, 1)
             turn_a(s, 2)
             turn_a(s, 3)
             quant_m(s - 1)
-            products(s + 1, (6, 7, 9, 10) if s < LAST - 1 else (8, 9, 10, 11), "gpsimd")
-            if s > 2:
-                empty_k(s - 2, 0)
-                empty_k(s - 2, 1)
-            empty_a(s, 1)
+            products(s + 1, (4, 6, 7, 9) if s < LAST - 1 else (6, 7, 8, 9), "gpsimd")
             times_f(s - 2, 0, 2)
+            times_f(s - 2, 2, 4)
             add_a(s, 2)
             add_a(s, 3)
-            times_f(s - 2, 2, 4)
             products(s + 1, on_s[:2], "scalar")
             on(mx2, s - 3, 0, 4)
-            if s < LAST - 1:
-                first_stage(s - 1)
-                on(empty_o, s - 3)
-            else:
-                mx1(s - 1, 0)
-                mx1(s - 1, 1)
-                mx1(s - 1, 2, "a_ps", 3)
-                empty_o(s - 3)
-                mx1(s - 1, 3, "o_ps", 1)
-            products(s + 1, on_s[2:], "scalar")
+            mx1(s - 1, 0)
+            mx1(s - 1, 1)
+            on(empty_o, s - 3)
+            empty_k(s - 1, 0)
+            empty_k(s - 1, 1)
             turn_f(s - 1, 0)
-            if s < LAST - 1:
-                spread_rel(s + 1)
-                if s == 2:
-                    quant_w(2)
-                products(s + 2, (2,), "vector")
-                quant_p(s - 2)
-            empty_k(s - 1, 3)
-            empty_k(s - 1, 2)
-            if s == LAST - 1:
-                turn_a(s + 1, 0, range(3))
-                turn_a(s + 1, 1, range(3))
-                turn_a(s + 1, 0, (3,))
-                turn_a(s + 1, 1, (3,))
-            else:
-                turn_a(s + 1, 0)
-                turn_a(s + 1, 1)
             turn_f(s - 1, 1)
+            mx1(s - 1, 2)
+            mx1(s - 1, 3)
+            products(s + 1, on_s[2:], "scalar")
+            if s == 2:
+                quant_w(2)
+            if s < LAST - 1:
+                products(s + 2, (2,), "vector")
+                spread_rel(s + 1)
+            quant_p(s - 2)
+            turn_a(s + 1, 0)
+            turn_a(s + 1, 1)
+            empty_k(s - 1, 2)
+            empty_k(s - 1, 3)
         a = LAST
-        leaky(a - 1)
-        empty_k(a - 2, 0)
-        empty_k(a - 2, 1)
+        leaky(a - 1, 0, 2)
+        leaky(a - 1, 2, 4)
         empty_a(a, 0)
         empty_a(a, 1)
         round_o((2, 3), "scalar")
         turn_a(a, 2)
         turn_a(a, 3)
-        quant_p(a - 3)
-        quant_m(a - 1)
+        quant_m(a - 1, 0, 2)
+        quant_m(a - 1, 2, 4)
         take_m(a)
         round_o((0, 1), "gpsimd")
         times_f(a - 2, 0, 2)

@@ -18,6 +18,7 @@ SLOPE = 0.2
 TILES = N // 128
 LAST = TILES - 1
 W2 = J
+PLAIN = (LAST,)
 
 
 def tile_rangeviewmetakernelfourneighbour_x1_kernel(tc, rel, w1, b1, w2, b2, f, wo, out_0, out_1, out_2):
@@ -94,7 +95,7 @@ def tile_rangeviewmetakernelfourneighbour_x1_kernel(tc, rel, w1, b1, w2, b2, f, 
 
         def products(a, xs, engine):
             for x in xs:
-                width = 256 if x % 3 == 2 and a < LAST else 512
+                width = 256 if x % 3 == 2 and a not in PLAIN else 512
                 prods[a, x] = work.tile([128, width], F32, name="prod", bufs=28)
                 src = w1p[x % 3][:].rearrange("p t m -> p (t m)")[:, :width]
                 if engine == "gpsimd":
@@ -107,10 +108,10 @@ def tile_rangeviewmetakernelfourneighbour_x1_kernel(tc, rel, w1, b1, w2, b2, f, 
         def turn_a(a, t, js=range(J)):
             if (a, t) not in a_ps:
                 a_ps[a, t] = psum.tile([128, 512], F32, name="a_ps", bufs=3)
-            terms = 3 if t < 2 or a == LAST else 2
             for j in js:
-                for i in range(terms):
-                    nc.tensor.matmul(a_ps[a, t][:, j * 128 : (j + 1) * 128], lhsT=prods[a, 3 * j + i][:, t * 128 : (t + 1) * 128], rhs=ident[:], start=(i == 0), stop=(i == terms - 1), is_transpose=True)
+                terms = range(3 * j, 3 * j + (3 if t < 2 or a in PLAIN else 2))
+                for x in terms:
+                    nc.tensor.matmul(a_ps[a, t][:, j * 128 : (j + 1) * 128], lhsT=prods[a, x][:, t * 128 : (t + 1) * 128], rhs=ident[:], start=(x == terms[0]), stop=(x == terms[-1]), is_transpose=True)
 
         def spread_rel(a):
             r_ps[a] = psum.tile([128, 2, 128], F32, name="o_ps")
@@ -339,7 +340,7 @@ def tile_rangeviewmetakernelfourneighbour_x1_kernel(tc, rel, w1, b1, w2, b2, f, 
         empty_a(1, 1)
         group_w_part(1, 3)
         group_w_part(2, 0)
-        products(2, (2, 3, 5, 6, 8, 11), "vector")
+        products(2, (2, 3, 5, 6, 8), "vector")
         products(2, (7,), "scalar")
         group_w(3)
         group_w_part(2, 1)
@@ -348,9 +349,9 @@ def tile_rangeviewmetakernelfourneighbour_x1_kernel(tc, rel, w1, b1, w2, b2, f, 
         mx1(0, 2)
         mx1(0, 3)
         spread_rel(2)
-        quant_w(1)
         cast_rel(2)
-        products(2, (10,), "gpsimd")
+        quant_w(1)
+        products(2, (10, 11), "gpsimd")
         add_a(1, 2)
         add_a(1, 3)
         quant_w(3)
@@ -361,7 +362,7 @@ def tile_rangeviewmetakernelfourneighbour_x1_kernel(tc, rel, w1, b1, w2, b2, f, 
         empty_k(0, 3)
         group_w_part(2, 3)
         for s in range(2, LAST):
-            on_v, on_s = {2: ((0, 5, 8), (1, 2, 3, 10, 11)), 3: ((5, 8), (0, 1, 3, 10, 11)), 4: ((0, 5), (1, 3, 8, 10, 11)), 5: ((0, 5), (1, 3, 8, 10, 11)), 6: ((0, 1, 3), (4, 5, 10, 11))}[s]
+            on_v, on_s, late = {2: ((0,), (1, 2, 3, 5, 10), (8, 11)), 3: ((5,), (0, 1, 3, 10, 11), (8,)), 4: ((0,), (1, 3, 5, 10, 11), (8,)), 5: ((0,), (1, 3, 5, 10, 11), (8,)), 6: ((0,), (6, 7, 8, 9), (10, 11))}[s]
             leaky(s - 1)
             empty_a(s, 0)
             last_term(s, 2)
@@ -372,7 +373,7 @@ def tile_rangeviewmetakernelfourneighbour_x1_kernel(tc, rel, w1, b1, w2, b2, f, 
             turn_a(s, 2)
             turn_a(s, 3)
             quant_m(s - 1)
-            products(s + 1, (4, 6, 7, 9) if s < LAST - 1 else (6, 7, 8, 9), "gpsimd")
+            products(s + 1, (4, 6, 7, 9) if s < LAST - 1 else (1, 3, 4, 5), "gpsimd")
             times_f(s - 2, 0, 2)
             times_f(s - 2, 2, 4)
             add_a(s, 2)
@@ -389,14 +390,21 @@ def tile_rangeviewmetakernelfourneighbour_x1_kernel(tc, rel, w1, b1, w2, b2, f, 
             mx1(s - 1, 2)
             mx1(s - 1, 3)
             products(s + 1, on_s[2:], "scalar")
+            products(s + 1, late, "vector")
             if s == 2:
                 quant_w(2)
             if s < LAST - 1:
                 products(s + 2, (2,), "vector")
                 spread_rel(s + 1)
             quant_p(s - 2)
-            turn_a(s + 1, 0)
-            turn_a(s + 1, 1)
+            if s < LAST - 1:
+                turn_a(s + 1, 0)
+                turn_a(s + 1, 1)
+            else:
+                turn_a(s + 1, 0, range(3))
+                turn_a(s + 1, 1, range(3))
+                turn_a(s + 1, 0, (3,))
+                turn_a(s + 1, 1, (3,))
             empty_k(s - 1, 2)
             empty_k(s - 1, 3)
         a = LAST
@@ -418,16 +426,16 @@ def tile_rangeviewmetakernelfourneighbour_x1_kernel(tc, rel, w1, b1, w2, b2, f, 
         empty_a(a, 3)
         turn_f(a - 1, 0)
         turn_f(a - 1, 1)
-        mx2(a - 3, 0, 4)
         leaky(a)
-        for t in (2, 3, 0, 1):
-            empty_k(a - 1, t)
-        empty_o(a - 3)
         turn_o(0, 2)
+        for t in (3, 2, 0, 1):
+            empty_k(a - 1, t)
         turn_o(2, 4)
+        mx2(a - 3, 0, 4)
         turn_f(a, 0, "a_ps", 3)
         empty_t(0, 2)
         empty_t(2, 4)
+        empty_o(a - 3)
         quant_p(a - 2)
         quant_m(a)
         round_o((4,), "gpsimd")

@@ -18,7 +18,6 @@ SLOPE = 0.2
 TILES = N // 128
 LAST = TILES - 1
 W2 = J
-PLAIN = (LAST,)
 
 
 def tile_rangeviewmetakernelfourneighbour_x1_kernel(tc, rel, w1, b1, w2, b2, f, wo, out_0, out_1, out_2):
@@ -65,7 +64,7 @@ def tile_rangeviewmetakernelfourneighbour_x1_kernel(tc, rel, w1, b1, w2, b2, f, 
         o_bf = keep.tile([128, 4 * N], BF16, name="o_bf", align_bytes=64)
 
         w_grp, rel_g, prods, a_ps, r_ps, u_sb, a_sb, m_bf, m_q = {}, {}, {}, {}, {}, {}, {}, {}, {}
-        k_ps, k_sb, f_ps, f_w, p_bf, p_q = {}, {}, {}, {}, {}, {}
+        k_ps, k_sb, f_ps, p_bf, p_q = {}, {}, {}, {}, {}
         o_ps, r_sb, o_w, t_ps = {}, {}, {}, {}
 
         def group_w2(u):
@@ -95,7 +94,7 @@ def tile_rangeviewmetakernelfourneighbour_x1_kernel(tc, rel, w1, b1, w2, b2, f, 
 
         def products(a, xs, engine):
             for x in xs:
-                width = 256 if x % 3 == 2 and a not in PLAIN else 512
+                width = 256 if x % 3 == 2 and a < LAST else 512
                 prods[a, x] = work.tile([128, width], F32, name="prod", bufs=28)
                 src = w1p[x % 3][:].rearrange("p t m -> p (t m)")[:, :width]
                 if engine == "gpsimd":
@@ -109,7 +108,7 @@ def tile_rangeviewmetakernelfourneighbour_x1_kernel(tc, rel, w1, b1, w2, b2, f, 
             if (a, t) not in a_ps:
                 a_ps[a, t] = psum.tile([128, 512], F32, name="a_ps", bufs=3)
             for j in js:
-                terms = range(3 * j, 3 * j + (3 if t < 2 or a in PLAIN else 2))
+                terms = range(3 * j, 3 * j + (3 if t < 2 or a == LAST else 2))
                 for x in terms:
                     nc.tensor.matmul(a_ps[a, t][:, j * 128 : (j + 1) * 128], lhsT=prods[a, x][:, t * 128 : (t + 1) * 128], rhs=ident[:], start=(x == terms[0]), stop=(x == terms[-1]), is_transpose=True)
 
@@ -182,18 +181,6 @@ def tile_rangeviewmetakernelfourneighbour_x1_kernel(tc, rel, w1, b1, w2, b2, f, 
             out = p_bf[a][:, j0 * 512 : j1 * 512].rearrange("p (n i e g) -> p n g i e", i=4, e=2, g=2)
             nc.vector.tensor_tensor(out=out, in0=fv, in1=kv, op=ALU.mult)
 
-        def empty_f(a, j):
-            f_w[a] = work.tile([128, 32, 2, 4], F32, name="f_w")
-            src = f_ps[a, j // 2][:, :, j % 2 * 128 : (j % 2 + 1) * 128].rearrange("p g (n i) -> p g n i", i=4)
-            nc.scalar.copy(f_w[a][:].rearrange("p n g i -> p g n i"), src)
-
-        def times_f_gpsimd(a, j):
-            if a not in p_bf:
-                p_bf[a] = work.tile([128, 2048], BF16, name="p_bf", align_bytes=64)
-            fv = f_w[a][:].rearrange("p n g i -> p n (g i)").bitcast(BF16).rearrange("p n (g i e) -> p n e g i", g=2, e=2)
-            out = p_bf[a][:, j * 512 : (j + 1) * 512].rearrange("p (n i e g) -> p n e g i", i=4, e=2, g=2)
-            nc.gpsimd.tensor_tensor(out=out, in0=k_sb[a][:, j * 32 : (j + 1) * 32], in1=fv, op=ALU.mult)
-
         def quant_p(a, j0=0, j1=J):
             if a not in p_q:
                 p_q[a] = (work.tile([128, 512], U32, name="p_q", align_bytes=64, bufs=3), work.tile([128, 512], U8, name="p_s", align_bytes=64, bufs=3))
@@ -233,10 +220,8 @@ def tile_rangeviewmetakernelfourneighbour_x1_kernel(tc, rel, w1, b1, w2, b2, f, 
                 src = r_sb[a][:].rearrange("n (m h e) -> n h m e", h=2, e=2)
                 if engine == "gpsimd":
                     nc.gpsimd.tensor_scalar(out=o_w[a], in0=src, scalar1=1.0, scalar2=0.0, op0=ALU.mult, op1=ALU.add)
-                elif engine == "scalar":
-                    nc.scalar.activation(o_w[a], src, ACT.Identity)
                 else:
-                    nc.vector.tensor_copy(out=o_w[a], in_=src)
+                    nc.scalar.activation(o_w[a], src, ACT.Identity)
 
         def round_from_bank(a):
             words = work.tile([128, 1, 2, 128, 2], BF16, name="o_w", align_bytes=64)
@@ -258,14 +243,6 @@ def tile_rangeviewmetakernelfourneighbour_x1_kernel(tc, rel, w1, b1, w2, b2, f, 
             cols = slice(a0 * 128, a1 * 128)
             nc.vector.quantize_mx(out=o_q[:, cols].bitcast(FP8X4), scales=o_s[:, cols], in_=o_bf[:, a0 * 512 : a1 * 512])
             nc.sync.dma_start(out=out_1[0, :, cols, :].rearrange("p m t -> p (m t)").bitcast(I32), in_=o_q[:, cols].bitcast(I32))
-
-        def store_scales(c0, c1, queues):
-            for q in range(4):
-                queues[q].dma_start(out=out_2[0, 4 * q : 4 * q + 4, c0:c1].bitcast(I32), in_=o_s[32 * q : 32 * q + 4, c0:c1].bitcast(I32))
-
-        def on(fn, a, *args):
-            if a >= 0:
-                fn(a, *args)
 
         def first_stage(a):
             mx1(a, 0)
@@ -355,34 +332,41 @@ def tile_rangeviewmetakernelfourneighbour_x1_kernel(tc, rel, w1, b1, w2, b2, f, 
         add_a(1, 2)
         add_a(1, 3)
         quant_w(3)
+        products(3, (2,), "vector")
         turn_a(2, 0)
         turn_a(2, 1)
         group_w_part(2, 2)
         empty_k(0, 2)
         empty_k(0, 3)
         group_w_part(2, 3)
+
         for s in range(2, LAST):
-            on_v, on_s, late = {2: ((0,), (1, 2, 3, 5, 10), (8, 11)), 3: ((5,), (0, 1, 3, 10, 11), (8,)), 4: ((0,), (1, 3, 5, 10, 11), (8,)), 5: ((0,), (1, 3, 5, 10, 11), (8,)), 6: ((0,), (6, 7, 8, 9), (10, 11))}[s]
+            short = s + 1 < LAST
+            on_g = (4, 6, 7, 9) if short else (1, 3, 4, 5)
+            on_s = (1, 3, 5, 10, 11) if short else (6, 7, 8, 9)
+            late = (8,) if short else (10, 11)
             leaky(s - 1)
             empty_a(s, 0)
             last_term(s, 2)
             last_term(s, 3)
-            products(s + 1, on_v, "vector")
+            products(s + 1, (0,), "vector")
             cast_rel(s + 1)
             empty_a(s, 1)
             turn_a(s, 2)
             turn_a(s, 3)
             quant_m(s - 1)
-            products(s + 1, (4, 6, 7, 9) if s < LAST - 1 else (1, 3, 4, 5), "gpsimd")
+            products(s + 1, on_g, "gpsimd")
             times_f(s - 2, 0, 2)
             times_f(s - 2, 2, 4)
             add_a(s, 2)
             add_a(s, 3)
             products(s + 1, on_s[:2], "scalar")
-            on(mx2, s - 3, 0, 4)
+            if s > 2:
+                mx2(s - 3, 0, 4)
             mx1(s - 1, 0)
             mx1(s - 1, 1)
-            on(empty_o, s - 3)
+            if s > 2:
+                empty_o(s - 3)
             empty_k(s - 1, 0)
             empty_k(s - 1, 1)
             turn_f(s - 1, 0)
@@ -393,20 +377,16 @@ def tile_rangeviewmetakernelfourneighbour_x1_kernel(tc, rel, w1, b1, w2, b2, f, 
             products(s + 1, late, "vector")
             if s == 2:
                 quant_w(2)
-            if s < LAST - 1:
+            if short:
                 products(s + 2, (2,), "vector")
                 spread_rel(s + 1)
             quant_p(s - 2)
-            if s < LAST - 1:
-                turn_a(s + 1, 0)
-                turn_a(s + 1, 1)
-            else:
-                turn_a(s + 1, 0, range(3))
-                turn_a(s + 1, 1, range(3))
-                turn_a(s + 1, 0, (3,))
-                turn_a(s + 1, 1, (3,))
+            for js in (range(J),) if short else (range(J - 1), (J - 1,)):
+                turn_a(s + 1, 0, js)
+                turn_a(s + 1, 1, js)
             empty_k(s - 1, 2)
             empty_k(s - 1, 3)
+
         a = LAST
         leaky(a - 1, 0, 2)
         leaky(a - 1, 2, 4)
@@ -479,4 +459,5 @@ def tile_rangeviewmetakernelfourneighbour_x1_kernel(tc, rel, w1, b1, w2, b2, f, 
         empty_o(a)
         quant_o(5, 7)
         quant_o(7, 8)
-        store_scales(0, 1024, [nc.scalar, nc.scalar, nc.sync, nc.sync])
+        for q, queue in enumerate((nc.scalar, nc.scalar, nc.sync, nc.sync)):
+            queue.dma_start(out=out_2[0, 4 * q : 4 * q + 4, :].bitcast(I32), in_=o_s[32 * q : 32 * q + 4, :].bitcast(I32))

@@ -18,6 +18,9 @@ SLOPE = 0.2
 TILES = N // 128
 LAST = TILES - 1
 W2 = J
+GUARD = (1.0 + 2.0**-10) * 2.0**-48
+FLOOR = 2.0**-70
+PRODS = 26
 
 
 def tile_rangeviewmetakernelfourneighbour_x1_kernel(tc, rel, w1, b1, w2, b2, f, wo, out_0, out_1, out_2):
@@ -30,18 +33,17 @@ def tile_rangeviewmetakernelfourneighbour_x1_kernel(tc, rel, w1, b1, w2, b2, f, 
 
         rel_0 = keep.tile([128, 12], BF16, name="rel_0")
         rel_raw = keep.tile([128, TILES, 16], BF16, name="rel_raw")
-        w1_col = keep.tile([128, 3, 4], BF16, name="w1_col")
+        w1_pad = keep.tile([128, 20], BF16, name="w1_pad")
+        w1_col = w1_pad[:, 8:20].rearrange("p (i t) -> p i t", t=4)
         b1_raw = keep.tile([128, 4], BF16, name="b1_raw")
         b2_raw = keep.tile([128, 4], BF16, name="b2_raw")
-        w_raw = [keep.tile([128, 4, 512], BF16, name=f"w_raw{x}") for x in range(J)]
-        w2_raw = [keep.tile([128, 4, 128], BF16, name=f"w2_raw{u}") for u in range(4)]
+        w_raw = [keep.tile([128, 4, 512], BF16, name=f"w_raw{x}") for x in range(J + 1)]
         f_sb = [keep.tile([128, J, 512], BF16, name=f"f_sb{a}") for a in range(TILES)]
 
         rel_rows = rel.rearrange("(a p) j i -> p a (j i)", p=128)
-        nc.sync.dma_start(out=w1_col[:], in_=w1.rearrange("i (p t) -> p i t", t=4))
+        nc.sync.dma_start(out=w1_col, in_=w1.rearrange("i (p t) -> p i t", t=4))
         nc.sync.dma_start(out=rel_0[:], in_=rel_rows[:, 0, :])
-        for u in range(4):
-            nc.sync.dma_start(out=w2_raw[u][:], in_=w2.rearrange("(p k) c -> p k c", k=4)[:, :, u * 128 : (u + 1) * 128])
+        nc.sync.dma_start(out=w_raw[W2][:], in_=w2.rearrange("(p k) c -> p k c", k=4))
         nc.sync.dma_start(out=b1_raw[:], in_=b1.rearrange("(p t) -> p t", t=4))
         nc.sync.dma_start(out=rel_raw[:, 1:, 0:12], in_=rel_rows[:, 1:, :])
         nc.sync.dma_start(out=b2_raw[:], in_=b2.rearrange("(p t) -> p t", t=4))
@@ -50,40 +52,42 @@ def tile_rangeviewmetakernelfourneighbour_x1_kernel(tc, rel, w1, b1, w2, b2, f, 
         for a in range(TILES):
             nc.sync.dma_start(out=f_sb[a][:], in_=f[a * 128 : (a + 1) * 128])
 
+        nc.vector.memset(w1_pad[:, 0:8], FLOOR)
         ident = keep.tile([128, 128], F32, name="ident")
         make_identity(nc, ident[:])
 
         relf = keep.tile([128, TILES, 12], F32, name="relf")
-        rel_last = keep.tile([128, TILES, J], BF16, name="rel_last")
-        w1c = keep.tile([128, 4], F32, name="w1c")
-        w1p = [keep.tile([128, 4, 128], BF16, name=f"w1p{i}") for i in range(3)]
+        b1_f = keep.tile([128, 4], F32, name="b1_f")
+        largest = keep.tile([128, 1], F32, name="largest")
+        pivot = keep.tile([128, 4], F32, name="pivot")
+        inverse = keep.tile([128, 4], F32, name="inverse")
+        ratio = keep.tile([128, 2, 4], F32, name="ratio")
+        ratio_row = [keep.tile([128, 512], F32, name=f"ratio_row{i}") for i in range(2)]
         w_q = [keep.tile([128, 512], U32, name=f"w_q{x}", align_bytes=64) for x in range(J + 1)]
         w_s = [keep.tile([128, 512], U8, name=f"w_s{x}", align_bytes=64) for x in range(J + 1)]
         o_q = keep.tile([128, N], U32, name="o_q", align_bytes=64)
         o_s = keep.tile([128, N], U8, name="o_s", align_bytes=64)
         o_bf = keep.tile([128, 4 * N], BF16, name="o_bf", align_bytes=64)
 
-        w_grp, rel_g, prods, a_ps, r_ps, u_sb, a_sb, m_bf, m_q = {}, {}, {}, {}, {}, {}, {}, {}, {}
+        w_grp, rel_g, prods, a_ps, a_sb, m_bf, m_q = {}, {}, {}, {}, {}, {}, {}
         k_ps, k_sb, f_ps, p_bf, p_q = {}, {}, {}, {}, {}
         o_ps, r_sb, o_w, t_ps = {}, {}, {}, {}
+        sums = set()
 
-        def group_w2(u):
-            if u == 0:
-                w_grp[W2] = work.tile([128, 2048], BF16, name="w_grp", align_bytes=64, bufs=3)
-            dst = w_grp[W2][:].rearrange("p (t m k) -> p m k t", t=4, k=4)[:, u * 32 : (u + 1) * 32]
-            nc.vector.tensor_copy(out=dst, in_=w2_raw[u][:].rearrange("p k (m t) -> p m k t", t=4))
-
-        def group_w(x):
-            w_grp[x] = work.tile([128, 2048], BF16, name="w_grp", align_bytes=64, bufs=3)
-            dst = w_grp[x][:].rearrange("p (t m e g) -> p m g e t", t=4, e=2, g=2)
-            nc.vector.tensor_copy(out=dst, in_=w_raw[x][:].rearrange("p (g e) (m t) -> p m g e t", t=4, e=2))
-
-        def group_w_part(x, part):
-            if part == 0:
+        def group_w(x, part0, part1, engine):
+            if x not in w_grp:
                 w_grp[x] = work.tile([128, 2048], BF16, name="w_grp", align_bytes=64, bufs=3)
-            ms = slice(part * 32, (part + 1) * 32)
-            dst = w_grp[x][:].rearrange("p (t m e g) -> p m g e t", t=4, e=2, g=2)[:, ms]
-            nc.scalar.copy(dst, w_raw[x][:].rearrange("p (g e) (m t) -> p m g e t", t=4, e=2)[:, ms])
+            ms = slice(part0 * 32, part1 * 32)
+            if x == W2:
+                dst = w_grp[x][:].rearrange("p (t m k) -> p m k t", t=4, k=4)[:, ms]
+                src = w_raw[x][:].rearrange("p k (m t) -> p m k t", t=4)[:, ms]
+            else:
+                dst = w_grp[x][:].rearrange("p (t m e g) -> p m g e t", t=4, e=2, g=2)[:, ms]
+                src = w_raw[x][:].rearrange("p (g e) (m t) -> p m g e t", t=4, e=2)[:, ms]
+            if engine == "scalar":
+                nc.scalar.copy(dst, src)
+            else:
+                nc.vector.tensor_copy(out=dst, in_=src)
 
         def quant_w(x):
             nc.vector.quantize_mx(out=w_q[x][:].bitcast(FP8X4), scales=w_s[x][:], in_=w_grp[x][:])
@@ -94,48 +98,41 @@ def tile_rangeviewmetakernelfourneighbour_x1_kernel(tc, rel, w1, b1, w2, b2, f, 
 
         def products(a, xs, engine):
             for x in xs:
-                width = 256 if x % 3 == 2 and a < LAST else 512
-                prods[a, x] = work.tile([128, width], F32, name="prod", bufs=28)
-                src = w1p[x % 3][:].rearrange("p t m -> p (t m)")[:, :width]
-                if engine == "gpsimd":
-                    nc.gpsimd.tensor_scalar(out=prods[a, x][:], in0=src, scalar1=rel_g[a][:, x : x + 1], scalar2=0.0, op0=ALU.mult, op1=ALU.add)
-                elif engine == "scalar":
-                    nc.scalar.activation(prods[a, x][:], src, ACT.Identity, scale=relf[:, a, x : x + 1])
+                j, i = divmod(x, 2)
+                prods[a, x] = work.tile([128, 512], F32, name="prod", bufs=PRODS)
+                offsets = rel_g[a] if engine == "gpsimd" else relf[:, a, :]
+                factor = offsets[:, 3 * j + 1 + i : 3 * j + 2 + i]
+                first = offsets[:, 3 * j : 3 * j + 1] if i == 0 else 0.0
+                if engine == "scalar":
+                    nc.scalar.activation(prods[a, x][:], ratio_row[i][:], ACT.Identity, scale=factor, bias=first)
                 else:
-                    nc.vector.tensor_scalar(out=prods[a, x][:], in0=src, scalar1=relf[:, a, x : x + 1], scalar2=None, op0=ALU.mult)
+                    queue = nc.gpsimd if engine == "gpsimd" else nc.vector
+                    queue.tensor_scalar(out=prods[a, x][:], in0=ratio_row[i][:], scalar1=factor, scalar2=first, op0=ALU.mult, op1=ALU.add)
 
-        def turn_a(a, t, js=range(J)):
+        def summed(a, j):
+            prods[a, 2 * j + 1] = work.tile([128, 512], F32, name="prod", bufs=PRODS)
+            nc.vector.scalar_tensor_tensor(out=prods[a, 2 * j + 1][:], in0=ratio_row[1][:], scalar=relf[:, a, 3 * j + 2 : 3 * j + 3], in1=prods[a, 2 * j][:], op0=ALU.mult, op1=ALU.add)
+            sums.add((a, j))
+
+        def turn_a(a, t, js=range(J), tag="a_ps", bufs=3):
             if (a, t) not in a_ps:
-                a_ps[a, t] = psum.tile([128, 512], F32, name="a_ps", bufs=3)
+                a_ps[a, t] = psum.tile([128, 512], F32, name=tag, bufs=bufs)
             for j in js:
-                terms = range(3 * j, 3 * j + (3 if t < 2 or a == LAST else 2))
-                for x in terms:
-                    nc.tensor.matmul(a_ps[a, t][:, j * 128 : (j + 1) * 128], lhsT=prods[a, x][:, t * 128 : (t + 1) * 128], rhs=ident[:], start=(x == terms[0]), stop=(x == terms[-1]), is_transpose=True)
-
-        def spread_rel(a):
-            r_ps[a] = psum.tile([128, 2, 128], F32, name="o_ps")
-            words = rel_last[:, a, :].bitcast(F32)
-            for u in range(2):
-                nc.tensor.transpose(r_ps[a][:, u, :], words[:, u : u + 1].to_broadcast([128, 128]), ident[:])
-
-        def last_term(a, t):
-            u_sb[a, t] = work.tile([128, 512], F32, name="u_sb", bufs=4)
-            src = r_ps[a][:].bitcast(BF16).rearrange("p u x -> p (u x)")
-            nc.scalar.activation(u_sb[a, t][:], src, ACT.Identity, scale=w1c[:, t : t + 1], bias=b1_raw[:, t : t + 1])
+                terms = (1,) if (a, j) in sums else (0, 1)
+                for i in terms:
+                    nc.tensor.matmul(a_ps[a, t][:, j * 128 : (j + 1) * 128], lhsT=prods[a, 2 * j + i][:, t * 128 : (t + 1) * 128], rhs=ident[:], start=(i == terms[0]), stop=(i == 1), is_transpose=True)
 
         def take_a(a):
             if a not in a_sb:
                 a_sb[a] = work.tile([128, 128, 4, J], F32, name="a_sb")
 
-        def add_a(a, t):
-            take_a(a)
-            out = a_sb[a][:, :, t, :].rearrange("p n (u e) -> p n u e", e=2)
-            sums = a_ps[a, t][:].rearrange("p (u e n) -> p n u e", u=2, e=2)
-            nc.vector.tensor_tensor(out=out, in0=sums, in1=u_sb[a, t][:].rearrange("p (u n e) -> p n u e", u=2, e=2), op=ALU.add)
-
         def empty_a(a, t):
             take_a(a)
-            nc.scalar.activation(a_sb[a][:, :, t, :], a_ps[a, t][:].rearrange("p (j n) -> p n j", j=J), ACT.Identity, bias=b1_raw[:, t : t + 1])
+            nc.scalar.activation(a_sb[a][:, :, t, :], a_ps[a, t][:].rearrange("p (j n) -> p n j", j=J), ACT.Identity, scale=pivot[:, t : t + 1], bias=b1_raw[:, t : t + 1])
+
+        def empty_a_vector(a, t):
+            take_a(a)
+            nc.vector.tensor_scalar(out=a_sb[a][:, :, t, :], in0=a_ps[a, t][:].rearrange("p (j n) -> p n j", j=J), scalar1=pivot[:, t : t + 1], scalar2=b1_f[:, t : t + 1], op0=ALU.mult, op1=ALU.add)
 
         def take_m(a):
             m_bf[a] = work.tile([128, 2048], BF16, name="m_bf", align_bytes=64)
@@ -251,139 +248,116 @@ def tile_rangeviewmetakernelfourneighbour_x1_kernel(tc, rel, w1, b1, w2, b2, f, 
             mx1(a, 2, "a_ps", 3)
             mx1(a, 3, "a_ps", 3)
 
-        nc.vector.tensor_copy(out=rel_last[:, 0, :], in_=rel_0[:, 2:12:3])
+        nc.vector.tensor_reduce(out=largest[:], in_=w1_pad[:], op=ALU.max, axis=mybir.AxisListType.X, apply_absolute_value=True)
         nc.scalar.activation(relf[:, 0, :], rel_0[:], ACT.Identity)
-        nc.scalar.activation(w1c[:], w1_col[:, 2, :], ACT.Identity)
-        group_w2(0)
-        for i in range(3):
-            bank = psum.tile([128, 2, 128], F32, name="a_ps", bufs=3)
-            for u in range(2):
-                nc.tensor.transpose(bank[:, u, :], w1_col[:, i, :].bitcast(F32)[:, u : u + 1].to_broadcast([128, 128]), ident[:])
-            src = bank[:].bitcast(BF16).rearrange("p u (m e) -> p u e m", e=2)
-            dst = w1p[i][:].rearrange("p (u e) m -> p u e m", e=2)
-            if i > 0:
-                nc.scalar.copy(dst, src)
-            else:
-                nc.vector.tensor_copy(out=dst, in_=src)
-        spread_rel(0)
-        group_w2(1)
-        products(0, (0, 1, 3, 4, 6, 9), "vector")
-        nc.scalar.activation(relf[:, 1:, :], rel_raw[:, 1:, 0:12], ACT.Identity)
-        products(0, (7, 10), "scalar")
-        products(0, (2, 5, 8, 11), "vector")
-        nc.vector.tensor_copy(out=rel_last[:, 1:, :], in_=rel_raw[:, 1:, 2:12:3])
-        for j in range(J):
-            turn_a(0, 2, (j,))
-            turn_a(0, 3, (j,))
-        turn_a(0, 0)
-        last_term(0, 2)
-        last_term(0, 3)
-        group_w2(2)
-        group_w2(3)
-        products(1, (0,), "vector")
-        cast_rel(1)
+        nc.vector.scalar_tensor_tensor(out=pivot[:], in0=largest[:].to_broadcast([128, 4]), scalar=GUARD, in1=w1_col[:, 0, :], op0=ALU.mult, op1=ALU.add)
+        nc.vector.reciprocal(out=inverse[:], in_=pivot[:])
+        nc.vector.tensor_tensor(out=ratio[:], in0=w1_col[:, 1:3, :], in1=inverse[:].unsqueeze(1).to_broadcast([128, 2, 4]), op=ALU.mult)
+        group_w(W2, 0, 3, "vector")
+        group_w(W2, 3, 4, "scalar")
         quant_w(W2)
-        products(1, (10, 11), "gpsimd")
-        add_a(0, 2)
-        add_a(0, 3)
-        turn_a(0, 1)
-        spread_rel(1)
-        products(1, (1, 2, 3, 5), "vector")
-        products(1, (4, 6, 7, 8), "scalar")
-        products(2, (4,), "scalar")
+        for i in range(2):
+            bank = psum.tile([128, 4, 128], F32, name="f_ps", bufs=2)
+            for t in range(4):
+                nc.tensor.transpose(bank[:, t, :], ratio[:, i, t : t + 1].to_broadcast([128, 128]), ident[:])
+            if i == 0:
+                nc.scalar.copy(ratio_row[i][:], bank[:].rearrange("p t m -> p (t m)"))
+            else:
+                nc.vector.tensor_copy(out=ratio_row[i][:], in_=bank[:].rearrange("p t m -> p (t m)"))
+        products(0, (0, 2), "vector")
+        products(0, (4, 6), "scalar")
+        nc.scalar.activation(relf[:, 1:, :], rel_raw[:, 1:, 0:12], ACT.Identity)
+        nc.scalar.activation(b1_f[:], b1_raw[:], ACT.Identity)
+        for j in range(J):
+            summed(0, j)
+        products(1, (0, 1, 2, 3), "scalar")
+        for j in range(2):
+            for t in range(3):
+                turn_a(0, t, (j,))
+            turn_a(0, 3, (j,), "k_ps", 2)
+        for t in range(4):
+            turn_a(0, t, (2, 3))
+        products(1, (4, 5), "vector")
+        cast_rel(1)
+        group_w(0, 0, 2, "vector")
+        products(1, (6, 7), "gpsimd")
         empty_a(0, 0)
-        products(1, (9,), "scalar")
-        products(2, (9,), "scalar")
+        empty_a_vector(0, 2)
         empty_a(0, 1)
-        group_w(0)
+        empty_a_vector(0, 3)
         turn_a(1, 0)
         turn_a(1, 1)
-        products(2, (0, 1), "vector")
-        leaky(0)
-        quant_w(0)
-        quant_m(0)
-        last_term(1, 2)
-        last_term(1, 3)
-        group_w_part(1, 0)
-        empty_a(1, 0)
-        group_w_part(1, 1)
-        group_w_part(1, 2)
         turn_a(1, 2)
-        turn_a(1, 3)
+        leaky(0, 0, 2)
+        leaky(0, 2, 4)
+        group_w(0, 2, 4, "scalar")
+        empty_a(1, 0)
+        products(2, (0,), "scalar")
+        quant_m(0, 0, 2)
+        quant_m(0, 2, 4)
+        empty_a(1, 1)
+        products(2, (1, 2), "scalar")
         mx1(0, 0)
         mx1(0, 1)
+        turn_a(1, 3)
         turn_f(0, 0)
         turn_f(0, 1)
-        empty_a(1, 1)
-        group_w_part(1, 3)
-        group_w_part(2, 0)
-        products(2, (2, 3, 5, 6, 8), "vector")
-        products(2, (7,), "scalar")
-        group_w(3)
-        group_w_part(2, 1)
+        products(2, (3, 4, 5, 6, 7), "vector")
+        group_w(3, 0, 4, "vector")
+        quant_w(0)
+        empty_a(1, 2)
         empty_k(0, 0)
         empty_k(0, 1)
+        empty_a(1, 3)
         mx1(0, 2)
         mx1(0, 3)
-        spread_rel(2)
-        cast_rel(2)
-        quant_w(1)
-        products(2, (10, 11), "gpsimd")
-        add_a(1, 2)
-        add_a(1, 3)
-        quant_w(3)
-        products(3, (2,), "vector")
         turn_a(2, 0)
         turn_a(2, 1)
-        group_w_part(2, 2)
+        group_w(1, 0, 2, "scalar")
+        quant_w(3)
         empty_k(0, 2)
         empty_k(0, 3)
-        group_w_part(2, 3)
 
         for s in range(2, LAST):
-            short = s + 1 < LAST
-            on_g = (4, 6, 7, 9) if short else (1, 3, 4, 5)
-            on_s = (1, 3, 5, 10, 11) if short else (6, 7, 8, 9)
-            late = (8,) if short else (10, 11)
             leaky(s - 1)
             empty_a(s, 0)
-            last_term(s, 2)
-            last_term(s, 3)
             products(s + 1, (0,), "vector")
             cast_rel(s + 1)
             empty_a(s, 1)
             turn_a(s, 2)
             turn_a(s, 3)
+            if s == 3:
+                quant_w(2)
             quant_m(s - 1)
-            products(s + 1, on_g, "gpsimd")
+            products(s + 1, (2, 3, 4), "gpsimd")
             times_f(s - 2, 0, 2)
             times_f(s - 2, 2, 4)
-            add_a(s, 2)
-            add_a(s, 3)
-            products(s + 1, on_s[:2], "scalar")
-            if s > 2:
-                mx2(s - 3, 0, 4)
+            empty_a(s, 2)
+            empty_a(s, 3)
+            products(s + 1, (1,), "scalar")
             mx1(s - 1, 0)
             mx1(s - 1, 1)
             if s > 2:
-                empty_o(s - 3)
+                mx2(s - 3, 0, 4)
+            else:
+                group_w(1, 2, 4, "scalar")
             empty_k(s - 1, 0)
             empty_k(s - 1, 1)
+            if s > 2:
+                empty_o(s - 3)
+            products(s + 1, (5,), "scalar")
             turn_f(s - 1, 0)
             turn_f(s - 1, 1)
             mx1(s - 1, 2)
             mx1(s - 1, 3)
-            products(s + 1, on_s[2:], "scalar")
-            products(s + 1, late, "vector")
+            products(s + 1, (6, 7), "vector")
             if s == 2:
-                quant_w(2)
-            if short:
-                products(s + 2, (2,), "vector")
-                spread_rel(s + 1)
+                quant_w(1)
+                group_w(2, 0, 2, "vector")
+                group_w(2, 2, 4, "scalar")
             quant_p(s - 2)
-            for js in (range(J),) if short else (range(J - 1), (J - 1,)):
-                turn_a(s + 1, 0, js)
-                turn_a(s + 1, 1, js)
+            turn_a(s + 1, 0)
+            turn_a(s + 1, 1)
             empty_k(s - 1, 2)
             empty_k(s - 1, 3)
 
@@ -392,7 +366,6 @@ def tile_rangeviewmetakernelfourneighbour_x1_kernel(tc, rel, w1, b1, w2, b2, f, 
         leaky(a - 1, 2, 4)
         empty_a(a, 0)
         empty_a(a, 1)
-        round_o((2, 3), "scalar")
         turn_a(a, 2)
         turn_a(a, 3)
         quant_m(a - 1, 0, 2)
@@ -404,37 +377,42 @@ def tile_rangeviewmetakernelfourneighbour_x1_kernel(tc, rel, w1, b1, w2, b2, f, 
         empty_a(a, 2)
         first_stage(a - 1)
         empty_a(a, 3)
+        round_o((2,), "scalar")
         turn_f(a - 1, 0)
         turn_f(a - 1, 1)
-        leaky(a)
-        turn_o(0, 2)
-        for t in (3, 2, 0, 1):
-            empty_k(a - 1, t)
-        turn_o(2, 4)
         mx2(a - 3, 0, 4)
+        quant_p(a - 2)
+        leaky(a, 0, 2)
+        leaky(a, 2, 4)
+        for t in (3, 2, 0):
+            empty_k(a - 1, t)
+        empty_o(a - 3)
+        turn_o(0, 2)
+        empty_k(a - 1, 1)
+        turn_o(2, 3)
         turn_f(a, 0, "a_ps", 3)
         empty_t(0, 2)
-        empty_t(2, 4)
-        empty_o(a - 3)
-        quant_p(a - 2)
-        quant_m(a)
+        empty_t(2, 3)
+        quant_m(a, 0, 2)
+        quant_m(a, 2, 4)
+        round_o((3,), "scalar")
         round_o((4,), "gpsimd")
-        first_stage(a)
         mx2(a - 2, 0, 4)
+        first_stage(a)
+        empty_o(a - 2)
         times_f(a - 1, 0, 2)
         times_f(a - 1, 2, 4)
         for t in range(4):
             empty_k(a, t, 0, 2)
         for t in range(4):
             empty_k(a, t, 2, 4)
-        empty_o(a - 2)
         turn_f(a, 1)
-        turn_o(4, 5, "f_ps", 2)
+        turn_o(3, 5, "f_ps", 2)
         quant_p(a - 1, 0, 2)
         quant_p(a - 1, 2, 4)
-        mx2(a - 1, 0, 4, "k_ps", 2)
-        empty_t(4, 5)
+        mx2(a - 1, 0, 4)
         round_o((5,), "scalar")
+        empty_t(3, 5)
         round_from_bank(a - 1)
         empty_o(a - 1)
         times_f(a, 0, 1)
@@ -443,7 +421,7 @@ def tile_rangeviewmetakernelfourneighbour_x1_kernel(tc, rel, w1, b1, w2, b2, f, 
         times_f(a, 2, 3)
         quant_p(a, 1, 2)
         mx2_turned(a, 0, 1)
-        mx2(a, 0, 1)
+        mx2(a, 0, 1, "k_ps", 2)
         mx2_turned(a, 1, 2)
         mx2(a, 1, 2)
         turn_o(5, 7)
@@ -453,11 +431,11 @@ def tile_rangeviewmetakernelfourneighbour_x1_kernel(tc, rel, w1, b1, w2, b2, f, 
         quant_p(a, 3, 4)
         mx2_turned(a, 2, 4)
         mx2(a, 2, 4)
-        quant_o(0, 4)
-        quant_o(4, 5)
+        quant_o(0, 3)
+        quant_o(3, 5)
+        quant_o(5, 7)
         empty_turned(a)
         empty_o(a)
-        quant_o(5, 7)
         quant_o(7, 8)
         for q, queue in enumerate((nc.scalar, nc.scalar, nc.sync, nc.sync)):
             queue.dma_start(out=out_2[0, 4 * q : 4 * q + 4, :].bitcast(I32), in_=o_s[32 * q : 32 * q + 4, :].bitcast(I32))

@@ -20,7 +20,7 @@ LAST = TILES - 1
 W2 = J
 GUARD = (1.0 + 2.0**-10) * 2.0**-48
 FLOOR = 2.0**-70
-PRODS = 26
+PRODS = 22
 
 
 def tile_rangeviewmetakernelfourneighbour_x1_kernel(tc, rel, w1, b1, w2, b2, f, wo, out_0, out_1, out_2):
@@ -69,7 +69,7 @@ def tile_rangeviewmetakernelfourneighbour_x1_kernel(tc, rel, w1, b1, w2, b2, f, 
         o_s = keep.tile([128, N], U8, name="o_s", align_bytes=64)
         o_bf = keep.tile([128, 4 * N], BF16, name="o_bf", align_bytes=64)
 
-        w_grp, rel_g, prods, a_ps, a_sb, m_bf, m_q = {}, {}, {}, {}, {}, {}, {}
+        w_grp, prods, a_ps, a_sb, m_bf, m_q = {}, {}, {}, {}, {}, {}
         k_ps, k_sb, f_ps, p_bf, p_q = {}, {}, {}, {}, {}
         o_ps, r_sb, o_w, t_ps = {}, {}, {}, {}
         sums = set()
@@ -92,26 +92,26 @@ def tile_rangeviewmetakernelfourneighbour_x1_kernel(tc, rel, w1, b1, w2, b2, f, 
         def quant_w(x):
             nc.vector.quantize_mx(out=w_q[x][:].bitcast(FP8X4), scales=w_s[x][:], in_=w_grp[x][:])
 
-        def cast_rel(a):
-            rel_g[a] = work.tile([128, 12], F32, name="rel_g")
-            nc.vector.tensor_copy(out=rel_g[a][:], in_=rel_raw[:, a, 0:12])
-
-        def products(a, xs, engine):
+        def products(a, xs, engine, cols=slice(0, 512)):
+            if engine == "gpsimd":
+                pair = work.tile([128, 2, 512], F32, name="m_bf", align_bytes=64, bufs=3)
             for x in xs:
                 j, i = divmod(x, 2)
-                prods[a, x] = work.tile([128, 512], F32, name="prod", bufs=PRODS)
-                offsets = rel_g[a] if engine == "gpsimd" else relf[:, a, :]
-                factor = offsets[:, 3 * j + 1 + i : 3 * j + 2 + i]
-                first = offsets[:, 3 * j : 3 * j + 1] if i == 0 else 0.0
+                if engine == "gpsimd":
+                    prods[a, x] = pair[:, xs.index(x), :]
+                elif (a, x) not in prods:
+                    prods[a, x] = work.tile([128, 512], F32, name="prod", bufs=PRODS)[:]
+                factor = relf[:, a, 3 * j + 1 + i : 3 * j + 2 + i]
+                first = relf[:, a, 3 * j : 3 * j + 1] if i == 0 else 0.0
                 if engine == "scalar":
-                    nc.scalar.activation(prods[a, x][:], ratio_row[i][:], ACT.Identity, scale=factor, bias=first)
+                    nc.scalar.activation(prods[a, x][:, cols], ratio_row[i][:, cols], ACT.Identity, scale=factor, bias=first)
                 else:
                     queue = nc.gpsimd if engine == "gpsimd" else nc.vector
-                    queue.tensor_scalar(out=prods[a, x][:], in0=ratio_row[i][:], scalar1=factor, scalar2=first, op0=ALU.mult, op1=ALU.add)
+                    queue.tensor_scalar(out=prods[a, x][:, cols], in0=ratio_row[i][:, cols], scalar1=factor, scalar2=first, op0=ALU.mult, op1=ALU.add)
 
         def summed(a, j):
-            prods[a, 2 * j + 1] = work.tile([128, 512], F32, name="prod", bufs=PRODS)
-            nc.vector.scalar_tensor_tensor(out=prods[a, 2 * j + 1][:], in0=ratio_row[1][:], scalar=relf[:, a, 3 * j + 2 : 3 * j + 3], in1=prods[a, 2 * j][:], op0=ALU.mult, op1=ALU.add)
+            prods[a, 2 * j + 1] = work.tile([128, 512], F32, name="prod", bufs=PRODS)[:]
+            nc.vector.scalar_tensor_tensor(out=prods[a, 2 * j + 1], in0=ratio_row[1][:], scalar=relf[:, a, 3 * j + 2 : 3 * j + 3], in1=prods[a, 2 * j], op0=ALU.mult, op1=ALU.add)
             sums.add((a, j))
 
         def turn_a(a, t, js=range(J), tag="a_ps", bufs=3):
@@ -135,7 +135,7 @@ def tile_rangeviewmetakernelfourneighbour_x1_kernel(tc, rel, w1, b1, w2, b2, f, 
             nc.vector.tensor_scalar(out=a_sb[a][:, :, t, :], in0=a_ps[a, t][:].rearrange("p (j n) -> p n j", j=J), scalar1=pivot[:, t : t + 1], scalar2=b1_f[:, t : t + 1], op0=ALU.mult, op1=ALU.add)
 
         def take_m(a):
-            m_bf[a] = work.tile([128, 2048], BF16, name="m_bf", align_bytes=64)
+            m_bf[a] = work.tile([128, 2048], BF16, name="m_bf", align_bytes=64, bufs=3)
 
         def leaky(a, j0=0, j1=J):
             if a not in m_bf:
@@ -180,7 +180,7 @@ def tile_rangeviewmetakernelfourneighbour_x1_kernel(tc, rel, w1, b1, w2, b2, f, 
 
         def quant_p(a, j0=0, j1=J):
             if a not in p_q:
-                p_q[a] = (work.tile([128, 512], U32, name="p_q", align_bytes=64, bufs=3), work.tile([128, 512], U8, name="p_s", align_bytes=64, bufs=3))
+                p_q[a] = (work.tile([128, 512], U32, name="p_q", align_bytes=64, bufs=4), work.tile([128, 512], U8, name="p_s", align_bytes=64, bufs=4))
             cols = slice(j0 * 128, j1 * 128)
             nc.vector.quantize_mx(out=p_q[a][0][:, cols].bitcast(FP8X4), scales=p_q[a][1][:, cols], in_=p_bf[a][:, j0 * 512 : j1 * 512])
 
@@ -210,8 +210,7 @@ def tile_rangeviewmetakernelfourneighbour_x1_kernel(tc, rel, w1, b1, w2, b2, f, 
             nc.sync.dma_start(out=out_0[a * 128 : (a + 1) * 128, :], in_=r_sb[a][:])
 
         def round_o(tiles, engine):
-            tag = "m_bf" if engine == "gpsimd" else "o_w"
-            words = work.tile([128, len(tiles), 2, 128, 2], BF16, name=tag, align_bytes=64)
+            words = work.tile([128, len(tiles), 2, 128, 2], BF16, name="m_bf", align_bytes=64, bufs=3)
             for x, a in enumerate(tiles):
                 o_w[a] = words[:, x]
                 src = r_sb[a][:].rearrange("n (m h e) -> n h m e", h=2, e=2)
@@ -221,7 +220,7 @@ def tile_rangeviewmetakernelfourneighbour_x1_kernel(tc, rel, w1, b1, w2, b2, f, 
                     nc.scalar.activation(o_w[a], src, ACT.Identity)
 
         def round_from_bank(a):
-            words = work.tile([128, 1, 2, 128, 2], BF16, name="o_w", align_bytes=64)
+            words = work.tile([128, 1, 2, 128, 2], BF16, name="o_w", align_bytes=64, bufs=1)
             o_w[a] = words[:, 0]
             nc.scalar.activation(o_w[a], o_ps[a][:].rearrange("n (h e m) -> n h m e", h=2, e=2), ACT.Identity)
 
@@ -239,12 +238,14 @@ def tile_rangeviewmetakernelfourneighbour_x1_kernel(tc, rel, w1, b1, w2, b2, f, 
         def quant_o(a0, a1):
             cols = slice(a0 * 128, a1 * 128)
             nc.vector.quantize_mx(out=o_q[:, cols].bitcast(FP8X4), scales=o_s[:, cols], in_=o_bf[:, a0 * 512 : a1 * 512])
+
+        def store_codes(a0, a1):
+            cols = slice(a0 * 128, a1 * 128)
             nc.sync.dma_start(out=out_1[0, :, cols, :].rearrange("p m t -> p (m t)").bitcast(I32), in_=o_q[:, cols].bitcast(I32))
 
         def first_stage(a):
             mx1(a, 0)
             mx1(a, 1)
-            k_ps[a, 3] = psum.tile([128, 512], F32, name="a_ps", bufs=3)
             mx1(a, 2, "a_ps", 3)
             mx1(a, 3, "a_ps", 3)
 
@@ -260,106 +261,97 @@ def tile_rangeviewmetakernelfourneighbour_x1_kernel(tc, rel, w1, b1, w2, b2, f, 
             bank = psum.tile([128, 4, 128], F32, name="f_ps", bufs=2)
             for t in range(4):
                 nc.tensor.transpose(bank[:, t, :], ratio[:, i, t : t + 1].to_broadcast([128, 128]), ident[:])
-            if i == 0:
-                nc.scalar.copy(ratio_row[i][:], bank[:].rearrange("p t m -> p (t m)"))
-            else:
-                nc.vector.tensor_copy(out=ratio_row[i][:], in_=bank[:].rearrange("p t m -> p (t m)"))
-        products(0, (0, 2), "vector")
-        products(0, (4, 6), "scalar")
+            nc.scalar.copy(ratio_row[i][:], bank[:].rearrange("p t m -> p (t m)"))
+        products(0, (0, 2, 1, 3, 4, 5, 7), "vector")
+        products(0, (6,), "scalar")
         nc.scalar.activation(relf[:, 1:, :], rel_raw[:, 1:, 0:12], ACT.Identity)
-        nc.scalar.activation(b1_f[:], b1_raw[:], ACT.Identity)
-        for j in range(J):
-            summed(0, j)
-        products(1, (0, 1, 2, 3), "scalar")
+        products(1, (1, 0, 2), "scalar")
         for j in range(2):
             for t in range(3):
                 turn_a(0, t, (j,))
             turn_a(0, 3, (j,), "k_ps", 2)
         for t in range(4):
             turn_a(0, t, (2, 3))
-        products(1, (4, 5), "vector")
-        cast_rel(1)
-        group_w(0, 0, 2, "vector")
-        products(1, (6, 7), "gpsimd")
-        empty_a(0, 0)
-        empty_a_vector(0, 2)
-        empty_a(0, 1)
-        empty_a_vector(0, 3)
+        products(1, (3, 4, 5, 6, 7), "vector")
+        group_w(0, 0, 2, "scalar")
+        group_w(0, 2, 4, "vector")
+        for t in range(4):
+            empty_a(0, t)
+        products(2, (0, 1, 2, 3), "vector")
+        quant_w(0)
         turn_a(1, 0)
         turn_a(1, 1)
         turn_a(1, 2)
         leaky(0, 0, 2)
         leaky(0, 2, 4)
-        group_w(0, 2, 4, "scalar")
         empty_a(1, 0)
-        products(2, (0,), "scalar")
+        turn_a(1, 3)
+        group_w(1, 0, 1, "scalar")
         quant_m(0, 0, 2)
         quant_m(0, 2, 4)
         empty_a(1, 1)
-        products(2, (1, 2), "scalar")
+        group_w(1, 1, 2, "scalar")
+        empty_a(1, 2)
         mx1(0, 0)
         mx1(0, 1)
-        turn_a(1, 3)
         turn_f(0, 0)
         turn_f(0, 1)
-        products(2, (3, 4, 5, 6, 7), "vector")
-        group_w(3, 0, 4, "vector")
-        quant_w(0)
-        empty_a(1, 2)
+        products(2, (4, 5, 6, 7), "vector")
+        empty_a(1, 3)
+        group_w(3, 0, 2, "scalar")
+        group_w(3, 2, 4, "vector")
         empty_k(0, 0)
         empty_k(0, 1)
-        empty_a(1, 3)
+        group_w(1, 2, 4, "scalar")
         mx1(0, 2)
         mx1(0, 3)
         turn_a(2, 0)
         turn_a(2, 1)
-        group_w(1, 0, 2, "scalar")
-        quant_w(3)
         empty_k(0, 2)
         empty_k(0, 3)
+        take_m(1)
 
         for s in range(2, LAST):
             leaky(s - 1)
             empty_a(s, 0)
             products(s + 1, (0,), "vector")
-            cast_rel(s + 1)
+            if s == 2:
+                quant_w(3)
             empty_a(s, 1)
+            products(s + 1, (5,), "scalar", slice(0, 256))
             turn_a(s, 2)
             turn_a(s, 3)
-            if s == 3:
-                quant_w(2)
             quant_m(s - 1)
-            products(s + 1, (2, 3, 4), "gpsimd")
+            take_m(s)
+            products(s + 1, (1, 3), "gpsimd")
             times_f(s - 2, 0, 2)
             times_f(s - 2, 2, 4)
             empty_a(s, 2)
             empty_a(s, 3)
-            products(s + 1, (1,), "scalar")
             mx1(s - 1, 0)
             mx1(s - 1, 1)
-            if s > 2:
-                mx2(s - 3, 0, 4)
-            else:
-                group_w(1, 2, 4, "scalar")
             empty_k(s - 1, 0)
             empty_k(s - 1, 1)
-            if s > 2:
-                empty_o(s - 3)
-            products(s + 1, (5,), "scalar")
+            if s == 2:
+                group_w(2, 0, 2, "scalar")
+                group_w(2, 2, 4, "vector")
+                quant_w(1)
+            products(s + 1, (6, 7), "scalar")
             turn_f(s - 1, 0)
             turn_f(s - 1, 1)
             mx1(s - 1, 2)
             mx1(s - 1, 3)
-            products(s + 1, (6, 7), "vector")
+            products(s + 1, (2, 4), "vector")
             if s == 2:
-                quant_w(1)
-                group_w(2, 0, 2, "vector")
-                group_w(2, 2, 4, "scalar")
+                quant_w(2)
             quant_p(s - 2)
+            products(s + 1, (5,), "vector", slice(256, 512))
+            mx2(s - 2, 0, 4)
             turn_a(s + 1, 0)
             turn_a(s + 1, 1)
             empty_k(s - 1, 2)
             empty_k(s - 1, 3)
+            empty_o(s - 2)
 
         a = LAST
         leaky(a - 1, 0, 2)
@@ -377,44 +369,41 @@ def tile_rangeviewmetakernelfourneighbour_x1_kernel(tc, rel, w1, b1, w2, b2, f, 
         empty_a(a, 2)
         first_stage(a - 1)
         empty_a(a, 3)
-        round_o((2,), "scalar")
         turn_f(a - 1, 0)
         turn_f(a - 1, 1)
-        mx2(a - 3, 0, 4)
         quant_p(a - 2)
         leaky(a, 0, 2)
         leaky(a, 2, 4)
-        for t in (3, 2, 0):
+        for t in range(4):
             empty_k(a - 1, t)
-        empty_o(a - 3)
+        mx2(a - 2, 0, 2)
         turn_o(0, 2)
-        empty_k(a - 1, 1)
-        turn_o(2, 3)
         turn_f(a, 0, "a_ps", 3)
+        mx2(a - 2, 2, 4)
+        round_o((4,), "scalar")
         empty_t(0, 2)
-        empty_t(2, 3)
         quant_m(a, 0, 2)
         quant_m(a, 2, 4)
-        round_o((3,), "scalar")
-        round_o((4,), "gpsimd")
-        mx2(a - 2, 0, 4)
+        round_o((2, 3), "gpsimd")
         first_stage(a)
         empty_o(a - 2)
         times_f(a - 1, 0, 2)
         times_f(a - 1, 2, 4)
         for t in range(4):
             empty_k(a, t, 0, 2)
+        round_o((5,), "scalar")
         for t in range(4):
             empty_k(a, t, 2, 4)
         turn_f(a, 1)
-        turn_o(3, 5, "f_ps", 2)
+        turn_o(2, 4, "f_ps", 2)
         quant_p(a - 1, 0, 2)
         quant_p(a - 1, 2, 4)
         mx2(a - 1, 0, 4)
-        round_o((5,), "scalar")
-        empty_t(3, 5)
+        turn_o(4, 6, "k_ps", 2)
+        empty_t(2, 4)
         round_from_bank(a - 1)
         empty_o(a - 1)
+        empty_t(4, 6)
         times_f(a, 0, 1)
         times_f(a, 1, 2)
         quant_p(a, 0, 1)
@@ -424,18 +413,20 @@ def tile_rangeviewmetakernelfourneighbour_x1_kernel(tc, rel, w1, b1, w2, b2, f, 
         mx2(a, 0, 1, "k_ps", 2)
         mx2_turned(a, 1, 2)
         mx2(a, 1, 2)
-        turn_o(5, 7)
-        empty_t(5, 7)
+        turn_o(6, 7)
+        empty_t(6, 7)
         times_f(a, 3, 4)
         quant_p(a, 2, 3)
         quant_p(a, 3, 4)
         mx2_turned(a, 2, 4)
         mx2(a, 2, 4)
-        quant_o(0, 3)
-        quant_o(3, 5)
-        quant_o(5, 7)
+        quant_o(0, 4)
+        quant_o(4, 6)
+        quant_o(6, 7)
+        store_codes(0, 7)
         empty_turned(a)
         empty_o(a)
         quant_o(7, 8)
+        store_codes(7, 8)
         for q, queue in enumerate((nc.scalar, nc.scalar, nc.sync, nc.sync)):
             queue.dma_start(out=out_2[0, 4 * q : 4 * q + 4, :].bitcast(I32), in_=o_s[32 * q : 32 * q + 4, :].bitcast(I32))

@@ -265,19 +265,18 @@ def tile_rangeviewmetakernelfourneighbour_x1_kernel(tc, rel, w1, b1, w2, b2, f, 
         products(0, (0, 2, 1, 3, 4, 5, 7), "vector")
         products(0, (6,), "scalar")
         nc.scalar.activation(relf[:, 1:, :], rel_raw[:, 1:, 0:12], ACT.Identity)
-        products(1, (1, 0, 2), "scalar")
+        products(1, (1, 0, 2, 3, 4), "scalar")
         for j in range(2):
             for t in range(3):
                 turn_a(0, t, (j,))
             turn_a(0, 3, (j,), "k_ps", 2)
         for t in range(4):
             turn_a(0, t, (2, 3))
-        products(1, (3, 4, 5, 6, 7), "vector")
-        group_w(0, 0, 2, "scalar")
-        group_w(0, 2, 4, "vector")
+        products(1, (5, 6, 7), "vector")
+        group_w(0, 0, 4, "vector")
         for t in range(4):
             empty_a(0, t)
-        products(2, (0, 1, 2, 3), "vector")
+        products(2, (0, 1, 2, 3, 4), "vector")
         quant_w(0)
         turn_a(1, 0)
         turn_a(1, 1)
@@ -286,27 +285,29 @@ def tile_rangeviewmetakernelfourneighbour_x1_kernel(tc, rel, w1, b1, w2, b2, f, 
         leaky(0, 2, 4)
         empty_a(1, 0)
         turn_a(1, 3)
-        group_w(1, 0, 1, "scalar")
+        products(2, (5,), "scalar")
         quant_m(0, 0, 2)
         quant_m(0, 2, 4)
         empty_a(1, 1)
-        group_w(1, 1, 2, "scalar")
+        products(2, (6,), "scalar")
         empty_a(1, 2)
         mx1(0, 0)
         mx1(0, 1)
         turn_f(0, 0)
         turn_f(0, 1)
-        products(2, (4, 5, 6, 7), "vector")
+        group_w(1, 0, 4, "vector")
         empty_a(1, 3)
-        group_w(3, 0, 2, "scalar")
-        group_w(3, 2, 4, "vector")
+        products(2, (7,), "scalar")
+        products(3, (0,), "scalar")
+        group_w(3, 0, 4, "vector")
         empty_k(0, 0)
         empty_k(0, 1)
-        group_w(1, 2, 4, "scalar")
+        products(3, (2, 4), "scalar")
         mx1(0, 2)
         mx1(0, 3)
         turn_a(2, 0)
         turn_a(2, 1)
+        quant_w(1)
         empty_k(0, 2)
         empty_k(0, 3)
         take_m(1)
@@ -314,9 +315,10 @@ def tile_rangeviewmetakernelfourneighbour_x1_kernel(tc, rel, w1, b1, w2, b2, f, 
         for s in range(2, LAST):
             leaky(s - 1)
             empty_a(s, 0)
-            products(s + 1, (0,), "vector")
             if s == 2:
                 quant_w(3)
+            else:
+                products(s + 1, (4,) if s == 3 else (0,), "vector")
             empty_a(s, 1)
             products(s + 1, (5,), "scalar", slice(0, 256))
             turn_a(s, 2)
@@ -333,24 +335,24 @@ def tile_rangeviewmetakernelfourneighbour_x1_kernel(tc, rel, w1, b1, w2, b2, f, 
             empty_k(s - 1, 0)
             empty_k(s - 1, 1)
             if s == 2:
-                group_w(2, 0, 2, "scalar")
-                group_w(2, 2, 4, "vector")
-                quant_w(1)
+                group_w(2, 0, 4, "vector")
             products(s + 1, (6, 7), "scalar")
             turn_f(s - 1, 0)
             turn_f(s - 1, 1)
             mx1(s - 1, 2)
             mx1(s - 1, 3)
-            products(s + 1, (2, 4), "vector")
+            products(s + 1, () if s < 4 else (2, 4), "vector")
             if s == 2:
                 quant_w(2)
-            quant_p(s - 2)
             products(s + 1, (5,), "vector", slice(256, 512))
+            quant_p(s - 2)
             mx2(s - 2, 0, 4)
             turn_a(s + 1, 0)
             turn_a(s + 1, 1)
             empty_k(s - 1, 2)
             empty_k(s - 1, 3)
+            if s == 2:
+                products(s + 2, (0, 2), "scalar")
             empty_o(s - 2)
 
         a = LAST
@@ -376,17 +378,16 @@ def tile_rangeviewmetakernelfourneighbour_x1_kernel(tc, rel, w1, b1, w2, b2, f, 
         leaky(a, 2, 4)
         for t in range(4):
             empty_k(a - 1, t)
-        mx2(a - 2, 0, 2)
         turn_o(0, 2)
+        mx2(a - 2, 0, 4)
         turn_f(a, 0, "a_ps", 3)
-        mx2(a - 2, 2, 4)
         round_o((4,), "scalar")
         empty_t(0, 2)
+        empty_o(a - 2)
         quant_m(a, 0, 2)
         quant_m(a, 2, 4)
         round_o((2, 3), "gpsimd")
         first_stage(a)
-        empty_o(a - 2)
         times_f(a - 1, 0, 2)
         times_f(a - 1, 2, 4)
         for t in range(4):
@@ -398,11 +399,12 @@ def tile_rangeviewmetakernelfourneighbour_x1_kernel(tc, rel, w1, b1, w2, b2, f, 
         turn_o(2, 4, "f_ps", 2)
         quant_p(a - 1, 0, 2)
         quant_p(a - 1, 2, 4)
+        quant_o(0, 2)
+        store_codes(0, 2)
         mx2(a - 1, 0, 4)
         turn_o(4, 6, "k_ps", 2)
-        empty_t(2, 4)
         round_from_bank(a - 1)
-        empty_o(a - 1)
+        empty_t(2, 4)
         empty_t(4, 6)
         times_f(a, 0, 1)
         times_f(a, 1, 2)
@@ -411,19 +413,19 @@ def tile_rangeviewmetakernelfourneighbour_x1_kernel(tc, rel, w1, b1, w2, b2, f, 
         quant_p(a, 1, 2)
         mx2_turned(a, 0, 1)
         mx2(a, 0, 1, "k_ps", 2)
+        turn_o(6, 7)
+        empty_o(a - 1)
+        empty_t(6, 7)
         mx2_turned(a, 1, 2)
         mx2(a, 1, 2)
-        turn_o(6, 7)
-        empty_t(6, 7)
         times_f(a, 3, 4)
         quant_p(a, 2, 3)
         quant_p(a, 3, 4)
         mx2_turned(a, 2, 4)
         mx2(a, 2, 4)
-        quant_o(0, 4)
-        quant_o(4, 6)
+        quant_o(2, 6)
         quant_o(6, 7)
-        store_codes(0, 7)
+        store_codes(2, 7)
         empty_turned(a)
         empty_o(a)
         quant_o(7, 8)

@@ -48,7 +48,8 @@ def tile_rangeviewmetakernelfourneighbour_x1_kernel(tc, rel, w1, b1, w2, b2, f, 
         nc.sync.dma_start(out=rel_raw[:, 1:, 0:12], in_=rel_rows[:, 1:, :])
         nc.sync.dma_start(out=b2_raw[:], in_=b2.rearrange("(p t) -> p t", t=4))
         for j in range(J):
-            nc.sync.dma_start(out=w_raw[j][:], in_=wo[j].rearrange("(p k) c -> p k c", k=4))
+            for e in range(2):
+                nc.sync.dma_start(out=w_raw[j][:, 2 * e : 2 * e + 2, :], in_=wo[j].rearrange("(p g e) c -> p e g c", g=2, e=2)[:, e])
         for a in range(TILES):
             nc.sync.dma_start(out=f_sb[a][:], in_=f[a * 128 : (a + 1) * 128])
 
@@ -77,13 +78,9 @@ def tile_rangeviewmetakernelfourneighbour_x1_kernel(tc, rel, w1, b1, w2, b2, f, 
         def group_w(x, part0, part1, engine):
             if x not in w_grp:
                 w_grp[x] = work.tile([128, 2048], BF16, name="w_grp", align_bytes=64, bufs=3)
-            ms = slice(part0 * 32, part1 * 32)
-            if x == W2:
-                dst = w_grp[x][:].rearrange("p (t m k) -> p m k t", t=4, k=4)[:, ms]
-                src = w_raw[x][:].rearrange("p k (m t) -> p m k t", t=4)[:, ms]
-            else:
-                dst = w_grp[x][:].rearrange("p (t m e g) -> p m g e t", t=4, e=2, g=2)[:, ms]
-                src = w_raw[x][:].rearrange("p (g e) (m t) -> p m g e t", t=4, e=2)[:, ms]
+            ms = slice(part0 * 16, part1 * 16)
+            dst = w_grp[x][:].rearrange("p (t m d k) -> p m t d k", t=4, d=2, k=4)[:, ms]
+            src = w_raw[x][:].rearrange("p k (m d t) -> p m t d k", t=4, d=2)[:, ms]
             if engine == "scalar":
                 nc.scalar.copy(dst, src)
             else:

@@ -77,7 +77,7 @@ def tile_rangeviewmetakernelfourneighbour_x1_kernel(tc, rel, w1, b1, w2, b2, f, 
 
         def group_w(x, part0, part1, engine):
             if x not in w_grp:
-                w_grp[x] = work.tile([128, 2048], BF16, name="w_grp", align_bytes=64, bufs=3)
+                w_grp[x] = work.tile([128, 2048], BF16, name="w_grp", align_bytes=64, bufs=4)
             ms = slice(part0 * 16, part1 * 16)
             dst = w_grp[x][:].rearrange("p (t m d k) -> p m t d k", t=4, d=2, k=4)[:, ms]
             src = w_raw[x][:].rearrange("p k (m d t) -> p m t d k", t=4, d=2)[:, ms]
@@ -89,22 +89,23 @@ def tile_rangeviewmetakernelfourneighbour_x1_kernel(tc, rel, w1, b1, w2, b2, f, 
         def quant_w(x):
             nc.vector.quantize_mx(out=w_q[x][:].bitcast(FP8X4), scales=w_s[x][:], in_=w_grp[x][:])
 
-        def products(a, xs, engine, cols=slice(0, 512)):
-            if engine == "gpsimd":
+        def products(a, xs, engine, paired=False):
+            paired = paired or engine == "gpsimd"
+            if paired:
                 pair = work.tile([128, 2, 512], F32, name="m_bf", align_bytes=64, bufs=3)
             for x in xs:
                 j, i = divmod(x, 2)
-                if engine == "gpsimd":
+                if paired:
                     prods[a, x] = pair[:, xs.index(x), :]
-                elif (a, x) not in prods:
+                else:
                     prods[a, x] = work.tile([128, 512], F32, name="prod", bufs=PRODS)[:]
                 factor = relf[:, a, 3 * j + 1 + i : 3 * j + 2 + i]
                 first = relf[:, a, 3 * j : 3 * j + 1] if i == 0 else 0.0
                 if engine == "scalar":
-                    nc.scalar.activation(prods[a, x][:, cols], ratio_row[i][:, cols], ACT.Identity, scale=factor, bias=first)
+                    nc.scalar.activation(prods[a, x], ratio_row[i][:], ACT.Identity, scale=factor, bias=first)
                 else:
                     queue = nc.gpsimd if engine == "gpsimd" else nc.vector
-                    queue.tensor_scalar(out=prods[a, x][:, cols], in0=ratio_row[i][:, cols], scalar1=factor, scalar2=first, op0=ALU.mult, op1=ALU.add)
+                    queue.tensor_scalar(out=prods[a, x], in0=ratio_row[i][:], scalar1=factor, scalar2=first, op0=ALU.mult, op1=ALU.add)
 
         def summed(a, j):
             prods[a, 2 * j + 1] = work.tile([128, 512], F32, name="prod", bufs=PRODS)[:]
@@ -251,30 +252,29 @@ def tile_rangeviewmetakernelfourneighbour_x1_kernel(tc, rel, w1, b1, w2, b2, f, 
         nc.vector.scalar_tensor_tensor(out=pivot[:], in0=largest[:].to_broadcast([128, 4]), scalar=GUARD, in1=w1_col[:, 0, :], op0=ALU.mult, op1=ALU.add)
         nc.vector.reciprocal(out=inverse[:], in_=pivot[:])
         nc.vector.tensor_tensor(out=ratio[:], in0=w1_col[:, 1:3, :], in1=inverse[:].unsqueeze(1).to_broadcast([128, 2, 4]), op=ALU.mult)
-        group_w(W2, 0, 3, "vector")
-        group_w(W2, 3, 4, "scalar")
+        group_w(W2, 0, 2, "vector")
+        group_w(W2, 2, 4, "scalar")
         quant_w(W2)
         for i in range(2):
             bank = psum.tile([128, 4, 128], F32, name="f_ps", bufs=2)
             for t in range(4):
                 nc.tensor.transpose(bank[:, t, :], ratio[:, i, t : t + 1].to_broadcast([128, 128]), ident[:])
             nc.scalar.copy(ratio_row[i][:], bank[:].rearrange("p t m -> p (t m)"))
-        products(0, (0, 2, 1, 3, 4, 5, 7), "vector")
-        products(0, (6,), "scalar")
+        products(0, (0, 2, 1, 3, 4, 5, 6, 7), "vector")
         nc.scalar.activation(relf[:, 1:, :], rel_raw[:, 1:, 0:12], ACT.Identity)
-        products(1, (1, 0, 2, 3, 4), "scalar")
+        group_w(0, 0, 4, "scalar")
         for j in range(2):
             for t in range(3):
                 turn_a(0, t, (j,))
             turn_a(0, 3, (j,), "k_ps", 2)
         for t in range(4):
             turn_a(0, t, (2, 3))
-        products(1, (5, 6, 7), "vector")
-        group_w(0, 0, 4, "vector")
+        products(1, (0, 1, 2, 3, 4, 5, 6, 7), "vector")
+        group_w(1, 0, 1, "scalar")
         for t in range(4):
             empty_a(0, t)
-        products(2, (0, 1, 2, 3, 4), "vector")
         quant_w(0)
+        products(2, (0, 1, 2), "vector")
         turn_a(1, 0)
         turn_a(1, 1)
         turn_a(1, 2)
@@ -282,42 +282,39 @@ def tile_rangeviewmetakernelfourneighbour_x1_kernel(tc, rel, w1, b1, w2, b2, f, 
         leaky(0, 2, 4)
         empty_a(1, 0)
         turn_a(1, 3)
-        products(2, (5,), "scalar")
         quant_m(0, 0, 2)
         quant_m(0, 2, 4)
         empty_a(1, 1)
-        products(2, (6,), "scalar")
         empty_a(1, 2)
+        group_w(1, 1, 2, "scalar")
         mx1(0, 0)
         mx1(0, 1)
         turn_f(0, 0)
         turn_f(0, 1)
-        group_w(1, 0, 4, "vector")
+        take_m(1)
+        products(2, (3, 4), "vector", paired=True)
+        products(2, (5, 6, 7), "vector")
         empty_a(1, 3)
-        products(2, (7,), "scalar")
-        products(3, (0,), "scalar")
-        group_w(3, 0, 4, "vector")
+        group_w(1, 2, 4, "scalar")
         empty_k(0, 0)
         empty_k(0, 1)
-        products(3, (2, 4), "scalar")
         mx1(0, 2)
         mx1(0, 3)
         turn_a(2, 0)
         turn_a(2, 1)
-        quant_w(1)
+        group_w(3, 0, 1, "vector")
+        group_w(3, 1, 3, "scalar")
         empty_k(0, 2)
         empty_k(0, 3)
-        take_m(1)
+        group_w(3, 3, 4, "scalar")
 
         for s in range(2, LAST):
             leaky(s - 1)
             empty_a(s, 0)
+            products(s + 1, (4,) if s == 3 else (0,), "vector")
             if s == 2:
-                quant_w(3)
-            else:
-                products(s + 1, (4,) if s == 3 else (0,), "vector")
+                quant_w(1)
             empty_a(s, 1)
-            products(s + 1, (5,), "scalar", slice(0, 256))
             turn_a(s, 2)
             turn_a(s, 3)
             quant_m(s - 1)
@@ -327,22 +324,27 @@ def tile_rangeviewmetakernelfourneighbour_x1_kernel(tc, rel, w1, b1, w2, b2, f, 
             times_f(s - 2, 2, 4)
             empty_a(s, 2)
             empty_a(s, 3)
+            if s == 2:
+                group_w(2, 0, 2, "scalar")
             mx1(s - 1, 0)
             mx1(s - 1, 1)
             empty_k(s - 1, 0)
             empty_k(s - 1, 1)
             if s == 2:
-                group_w(2, 0, 4, "vector")
-            products(s + 1, (6, 7), "scalar")
+                group_w(2, 2, 3, "scalar")
+                quant_w(3)
+                group_w(2, 3, 4, "vector")
+            products(s + 1, (6, 7), "vector" if s == 2 else "scalar")
             turn_f(s - 1, 0)
             turn_f(s - 1, 1)
             mx1(s - 1, 2)
             mx1(s - 1, 3)
-            products(s + 1, () if s < 4 else (2, 4), "vector")
+            products(s + 1, (5,) if s == 3 else (2, 4), "vector")
+            quant_p(s - 2)
+            if s != 3:
+                products(s + 1, (5,), "vector")
             if s == 2:
                 quant_w(2)
-            products(s + 1, (5,), "vector", slice(256, 512))
-            quant_p(s - 2)
             mx2(s - 2, 0, 4)
             turn_a(s + 1, 0)
             turn_a(s + 1, 1)

@@ -377,16 +377,17 @@ def tile_rangeviewmetakernelfourneighbour_x1_kernel(tc, rel, w1, b1, w2, b2, f, 
         leaky(a, 2, 4)
         for t in range(4):
             empty_k(a - 1, t)
+        mx2(a - 2, 0, 2)
         turn_o(0, 2)
-        mx2(a - 2, 0, 4)
         turn_f(a, 0, "a_ps", 3)
+        mx2(a - 2, 2, 4)
         round_o((4,), "scalar")
         empty_t(0, 2)
-        empty_o(a - 2)
         quant_m(a, 0, 2)
         quant_m(a, 2, 4)
         round_o((2, 3), "gpsimd")
         first_stage(a)
+        empty_o(a - 2)
         times_f(a - 1, 0, 2)
         times_f(a - 1, 2, 4)
         for t in range(4):
@@ -398,12 +399,11 @@ def tile_rangeviewmetakernelfourneighbour_x1_kernel(tc, rel, w1, b1, w2, b2, f, 
         turn_o(2, 4, "f_ps", 2)
         quant_p(a - 1, 0, 2)
         quant_p(a - 1, 2, 4)
-        quant_o(0, 2)
-        store_codes(0, 2)
         mx2(a - 1, 0, 4)
         turn_o(4, 6, "k_ps", 2)
-        round_from_bank(a - 1)
         empty_t(2, 4)
+        round_from_bank(a - 1)
+        empty_o(a - 1)
         empty_t(4, 6)
         times_f(a, 0, 1)
         times_f(a, 1, 2)
@@ -412,19 +412,19 @@ def tile_rangeviewmetakernelfourneighbour_x1_kernel(tc, rel, w1, b1, w2, b2, f, 
         quant_p(a, 1, 2)
         mx2_turned(a, 0, 1)
         mx2(a, 0, 1, "k_ps", 2)
-        turn_o(6, 7)
-        empty_o(a - 1)
-        empty_t(6, 7)
         mx2_turned(a, 1, 2)
         mx2(a, 1, 2)
+        turn_o(6, 7)
+        empty_t(6, 7)
         times_f(a, 3, 4)
         quant_p(a, 2, 3)
         quant_p(a, 3, 4)
         mx2_turned(a, 2, 4)
         mx2(a, 2, 4)
-        quant_o(2, 6)
+        quant_o(0, 4)
+        quant_o(4, 6)
         quant_o(6, 7)
-        store_codes(2, 7)
+        store_codes(0, 7)
         empty_turned(a)
         empty_o(a)
         quant_o(7, 8)

@@ -79,8 +79,8 @@ def tile_rangeviewmetakernelfourneighbour_x1_kernel(tc, rel, w1, b1, w2, b2, f, 
             if x not in w_grp:
                 w_grp[x] = work.tile([128, 2048], BF16, name="w_grp", align_bytes=64, bufs=4)
             ms = slice(part0 * 16, part1 * 16)
-            dst = w_grp[x][:].rearrange("p (t m d k) -> p m t d k", t=4, d=2, k=4)[:, ms]
-            src = w_raw[x][:].rearrange("p k (m d t) -> p m t d k", t=4, d=2)[:, ms]
+            dst = w_grp[x][:].rearrange("p (t m k) -> p m k t", t=4, k=4)[:, ms]
+            src = w_raw[x][:].rearrange("p k (m t) -> p m k t", t=4)[:, ms]
             if engine == "scalar":
                 nc.scalar.copy(dst, src)
             else:
@@ -252,8 +252,8 @@ def tile_rangeviewmetakernelfourneighbour_x1_kernel(tc, rel, w1, b1, w2, b2, f, 
         nc.vector.scalar_tensor_tensor(out=pivot[:], in0=largest[:].to_broadcast([128, 4]), scalar=GUARD, in1=w1_col[:, 0, :], op0=ALU.mult, op1=ALU.add)
         nc.vector.reciprocal(out=inverse[:], in_=pivot[:])
         nc.vector.tensor_tensor(out=ratio[:], in0=w1_col[:, 1:3, :], in1=inverse[:].unsqueeze(1).to_broadcast([128, 2, 4]), op=ALU.mult)
-        group_w(W2, 0, 2, "vector")
-        group_w(W2, 2, 4, "scalar")
+        group_w(W2, 0, 5, "vector")
+        group_w(W2, 5, 8, "scalar")
         quant_w(W2)
         for i in range(2):
             bank = psum.tile([128, 4, 128], F32, name="f_ps", bufs=2)
@@ -262,7 +262,7 @@ def tile_rangeviewmetakernelfourneighbour_x1_kernel(tc, rel, w1, b1, w2, b2, f, 
             nc.scalar.copy(ratio_row[i][:], bank[:].rearrange("p t m -> p (t m)"))
         products(0, (0, 2, 1, 3, 4, 5, 6, 7), "vector")
         nc.scalar.activation(relf[:, 1:, :], rel_raw[:, 1:, 0:12], ACT.Identity)
-        group_w(0, 0, 4, "scalar")
+        group_w(0, 0, 8, "scalar")
         for j in range(2):
             for t in range(3):
                 turn_a(0, t, (j,))
@@ -270,7 +270,7 @@ def tile_rangeviewmetakernelfourneighbour_x1_kernel(tc, rel, w1, b1, w2, b2, f, 
         for t in range(4):
             turn_a(0, t, (2, 3))
         products(1, (0, 1, 2, 3, 4, 5, 6, 7), "vector")
-        group_w(1, 0, 1, "scalar")
+        group_w(1, 0, 2, "scalar")
         for t in range(4):
             empty_a(0, t)
         quant_w(0)
@@ -286,7 +286,7 @@ def tile_rangeviewmetakernelfourneighbour_x1_kernel(tc, rel, w1, b1, w2, b2, f, 
         quant_m(0, 2, 4)
         empty_a(1, 1)
         empty_a(1, 2)
-        group_w(1, 1, 2, "scalar")
+        group_w(1, 2, 4, "scalar")
         mx1(0, 0)
         mx1(0, 1)
         turn_f(0, 0)
@@ -295,18 +295,18 @@ def tile_rangeviewmetakernelfourneighbour_x1_kernel(tc, rel, w1, b1, w2, b2, f, 
         products(2, (3, 4), "vector", paired=True)
         products(2, (5, 6, 7), "vector")
         empty_a(1, 3)
-        group_w(1, 2, 4, "scalar")
+        group_w(1, 4, 8, "scalar")
         empty_k(0, 0)
         empty_k(0, 1)
         mx1(0, 2)
         mx1(0, 3)
         turn_a(2, 0)
         turn_a(2, 1)
-        group_w(3, 0, 1, "vector")
-        group_w(3, 1, 3, "scalar")
+        group_w(3, 0, 2, "vector")
+        group_w(3, 2, 6, "scalar")
         empty_k(0, 2)
         empty_k(0, 3)
-        group_w(3, 3, 4, "scalar")
+        group_w(3, 6, 8, "scalar")
 
         for s in range(2, LAST):
             leaky(s - 1)
@@ -331,9 +331,9 @@ def tile_rangeviewmetakernelfourneighbour_x1_kernel(tc, rel, w1, b1, w2, b2, f, 
             empty_k(s - 1, 0)
             empty_k(s - 1, 1)
             if s == 2:
-                group_w(2, 2, 3, "scalar")
+                group_w(2, 2, 4, "scalar")
                 quant_w(3)
-                group_w(2, 3, 4, "vector")
+                group_w(2, 4, 8, "vector")
             products(s + 1, (6, 7), "vector" if s == 2 else "scalar")
             turn_f(s - 1, 0)
             turn_f(s - 1, 1)

@@ -48,8 +48,7 @@ def tile_rangeviewmetakernelfourneighbour_x1_kernel(tc, rel, w1, b1, w2, b2, f, 
         nc.sync.dma_start(out=rel_raw[:, 1:, 0:12], in_=rel_rows[:, 1:, :])
         nc.sync.dma_start(out=b2_raw[:], in_=b2.rearrange("(p t) -> p t", t=4))
         for j in range(J):
-            for e in range(2):
-                nc.sync.dma_start(out=w_raw[j][:, 2 * e : 2 * e + 2, :], in_=wo[j].rearrange("(p g e) c -> p e g c", g=2, e=2)[:, e])
+            nc.sync.dma_start(out=w_raw[j][:], in_=wo[j].rearrange("(p k) c -> p k c", k=4))
         for a in range(TILES):
             nc.sync.dma_start(out=f_sb[a][:], in_=f[a * 128 : (a + 1) * 128])
 
@@ -79,8 +78,12 @@ def tile_rangeviewmetakernelfourneighbour_x1_kernel(tc, rel, w1, b1, w2, b2, f, 
             if x not in w_grp:
                 w_grp[x] = work.tile([128, 2048], BF16, name="w_grp", align_bytes=64, bufs=4)
             ms = slice(part0 * 16, part1 * 16)
-            dst = w_grp[x][:].rearrange("p (t m k) -> p m k t", t=4, k=4)[:, ms]
-            src = w_raw[x][:].rearrange("p k (m t) -> p m k t", t=4)[:, ms]
+            if x == W2:
+                dst = w_grp[x][:].rearrange("p (t m k) -> p m k t", t=4, k=4)[:, ms]
+                src = w_raw[x][:].rearrange("p k (m t) -> p m k t", t=4)[:, ms]
+            else:
+                dst = w_grp[x][:].rearrange("p (t m e g) -> p m g e t", t=4, e=2, g=2)[:, ms]
+                src = w_raw[x][:].rearrange("p (g e) (m t) -> p m g e t", t=4, e=2)[:, ms]
             if engine == "scalar":
                 nc.scalar.copy(dst, src)
             else:
@@ -89,23 +92,20 @@ def tile_rangeviewmetakernelfourneighbour_x1_kernel(tc, rel, w1, b1, w2, b2, f, 
         def quant_w(x):
             nc.vector.quantize_mx(out=w_q[x][:].bitcast(FP8X4), scales=w_s[x][:], in_=w_grp[x][:])
 
-        def products(a, xs, engine, paired=False):
-            paired = paired or engine == "gpsimd"
-            if paired:
-                pair = work.tile([128, 2, 512], F32, name="m_bf", align_bytes=64, bufs=3)
+        def products(a, xs, engine, cols=slice(0, 512)):
             for x in xs:
                 j, i = divmod(x, 2)
-                if paired:
-                    prods[a, x] = pair[:, xs.index(x), :]
-                else:
+                if engine == "gpsimd" and x == xs[0]:
+                    prods[a, x] = m_bf[a - 2][:, 0:1024].bitcast(F32)
+                elif (a, x) not in prods:
                     prods[a, x] = work.tile([128, 512], F32, name="prod", bufs=PRODS)[:]
                 factor = relf[:, a, 3 * j + 1 + i : 3 * j + 2 + i]
                 first = relf[:, a, 3 * j : 3 * j + 1] if i == 0 else 0.0
                 if engine == "scalar":
-                    nc.scalar.activation(prods[a, x], ratio_row[i][:], ACT.Identity, scale=factor, bias=first)
+                    nc.scalar.activation(prods[a, x][:, cols], ratio_row[i][:, cols], ACT.Identity, scale=factor, bias=first)
                 else:
                     queue = nc.gpsimd if engine == "gpsimd" else nc.vector
-                    queue.tensor_scalar(out=prods[a, x], in0=ratio_row[i][:], scalar1=factor, scalar2=first, op0=ALU.mult, op1=ALU.add)
+                    queue.tensor_scalar(out=prods[a, x][:, cols], in0=ratio_row[i][:, cols], scalar1=factor, scalar2=first, op0=ALU.mult, op1=ALU.add)
 
         def summed(a, j):
             prods[a, 2 * j + 1] = work.tile([128, 512], F32, name="prod", bufs=PRODS)[:]
@@ -132,12 +132,9 @@ def tile_rangeviewmetakernelfourneighbour_x1_kernel(tc, rel, w1, b1, w2, b2, f, 
             take_a(a)
             nc.vector.tensor_scalar(out=a_sb[a][:, :, t, :], in0=a_ps[a, t][:].rearrange("p (j n) -> p n j", j=J), scalar1=pivot[:, t : t + 1], scalar2=b1_f[:, t : t + 1], op0=ALU.mult, op1=ALU.add)
 
-        def take_m(a):
-            m_bf[a] = work.tile([128, 2048], BF16, name="m_bf", align_bytes=64, bufs=3)
-
         def leaky(a, j0=0, j1=J):
             if a not in m_bf:
-                take_m(a)
+                m_bf[a] = work.tile([128, 2048], BF16, name="m_bf", align_bytes=64, bufs=3)
             src = a_sb[a][:].rearrange("p n t j -> p (n t) j")[:, :, j0:j1]
             out = m_bf[a][:].rearrange("p (j x) -> p x j", j=J)[:, :, j0:j1]
             nc.vector.scalar_tensor_tensor(out=out, in0=src, scalar=SLOPE, in1=src, op0=ALU.mult, op1=ALU.max)
@@ -207,10 +204,13 @@ def tile_rangeviewmetakernelfourneighbour_x1_kernel(tc, rel, w1, b1, w2, b2, f, 
             nc.scalar.activation(r_sb[a][:].rearrange("n (m t) -> n m t", t=4), o_ps[a][:].rearrange("n (t m) -> n m t", t=4), ACT.Identity)
             nc.sync.dma_start(out=out_0[a * 128 : (a + 1) * 128, :], in_=r_sb[a][:])
 
-        def round_o(tiles, engine):
-            words = work.tile([128, len(tiles), 2, 128, 2], BF16, name="m_bf", align_bytes=64, bufs=3)
+        def round_o(tiles, engine, spent=None):
+            if spent is None:
+                words = work.tile([128, 512 * len(tiles)], BF16, name="o_w", align_bytes=64, bufs=3)
+            else:
+                words = m_bf[spent]
             for x, a in enumerate(tiles):
-                o_w[a] = words[:, x]
+                o_w[a] = words[:, x * 512 : (x + 1) * 512].rearrange("n (h m e) -> n h m e", h=2, e=2)
                 src = r_sb[a][:].rearrange("n (m h e) -> n h m e", h=2, e=2)
                 if engine == "gpsimd":
                     nc.gpsimd.tensor_scalar(out=o_w[a], in0=src, scalar1=1.0, scalar2=0.0, op0=ALU.mult, op1=ALU.add)
@@ -218,7 +218,7 @@ def tile_rangeviewmetakernelfourneighbour_x1_kernel(tc, rel, w1, b1, w2, b2, f, 
                     nc.scalar.activation(o_w[a], src, ACT.Identity)
 
         def round_from_bank(a):
-            words = work.tile([128, 1, 2, 128, 2], BF16, name="o_w", align_bytes=64, bufs=1)
+            words = work.tile([128, 1, 2, 128, 2], BF16, name="o_w", align_bytes=64, bufs=3)
             o_w[a] = words[:, 0]
             nc.scalar.activation(o_w[a], o_ps[a][:].rearrange("n (h e m) -> n h m e", h=2, e=2), ACT.Identity)
 
@@ -262,19 +262,19 @@ def tile_rangeviewmetakernelfourneighbour_x1_kernel(tc, rel, w1, b1, w2, b2, f, 
             nc.scalar.copy(ratio_row[i][:], bank[:].rearrange("p t m -> p (t m)"))
         products(0, (0, 2, 1, 3, 4, 5, 6, 7), "vector")
         nc.scalar.activation(relf[:, 1:, :], rel_raw[:, 1:, 0:12], ACT.Identity)
-        group_w(0, 0, 8, "scalar")
         for j in range(2):
             for t in range(3):
                 turn_a(0, t, (j,))
             turn_a(0, 3, (j,), "k_ps", 2)
         for t in range(4):
             turn_a(0, t, (2, 3))
-        products(1, (0, 1, 2, 3, 4, 5, 6, 7), "vector")
-        group_w(1, 0, 2, "scalar")
+        products(1, (0,), "scalar")
+        group_w(0, 0, 8, "scalar")
+        products(1, (1, 2, 3, 4, 5, 6, 7), "vector")
         for t in range(4):
             empty_a(0, t)
         quant_w(0)
-        products(2, (0, 1, 2), "vector")
+        products(2, (1, 3, 5), "vector")
         turn_a(1, 0)
         turn_a(1, 1)
         turn_a(1, 2)
@@ -286,14 +286,12 @@ def tile_rangeviewmetakernelfourneighbour_x1_kernel(tc, rel, w1, b1, w2, b2, f, 
         quant_m(0, 2, 4)
         empty_a(1, 1)
         empty_a(1, 2)
-        group_w(1, 2, 4, "scalar")
+        group_w(1, 0, 4, "scalar")
         mx1(0, 0)
         mx1(0, 1)
         turn_f(0, 0)
         turn_f(0, 1)
-        take_m(1)
-        products(2, (3, 4), "vector", paired=True)
-        products(2, (5, 6, 7), "vector")
+        products(2, (0, 2, 4, 6, 7), "vector")
         empty_a(1, 3)
         group_w(1, 4, 8, "scalar")
         empty_k(0, 0)
@@ -302,56 +300,51 @@ def tile_rangeviewmetakernelfourneighbour_x1_kernel(tc, rel, w1, b1, w2, b2, f, 
         mx1(0, 3)
         turn_a(2, 0)
         turn_a(2, 1)
-        group_w(3, 0, 2, "vector")
-        group_w(3, 2, 6, "scalar")
+        group_w(3, 0, 4, "scalar")
         empty_k(0, 2)
         empty_k(0, 3)
-        group_w(3, 6, 8, "scalar")
+        group_w(3, 4, 8, "scalar")
 
         for s in range(2, LAST):
             leaky(s - 1)
             empty_a(s, 0)
-            products(s + 1, (4,) if s == 3 else (0,), "vector")
+            products(s + 1, (1,), "vector")
             if s == 2:
                 quant_w(1)
             empty_a(s, 1)
             turn_a(s, 2)
             turn_a(s, 3)
-            quant_m(s - 1)
-            take_m(s)
-            products(s + 1, (1, 3), "gpsimd")
+            quant_m(s - 1, 0, 2)
+            quant_m(s - 1, 2, 4)
+            products(s + 1, (0, 2, 4), "gpsimd")
             times_f(s - 2, 0, 2)
             times_f(s - 2, 2, 4)
             empty_a(s, 2)
             empty_a(s, 3)
             if s == 2:
-                group_w(2, 0, 2, "scalar")
+                group_w(2, 0, 4, "scalar")
             mx1(s - 1, 0)
             mx1(s - 1, 1)
             empty_k(s - 1, 0)
             empty_k(s - 1, 1)
             if s == 2:
-                group_w(2, 2, 4, "scalar")
                 quant_w(3)
                 group_w(2, 4, 8, "vector")
-            products(s + 1, (6, 7), "vector" if s == 2 else "scalar")
+            products(s + 1, (6, 7), "scalar")
             turn_f(s - 1, 0)
             turn_f(s - 1, 1)
             mx1(s - 1, 2)
             mx1(s - 1, 3)
-            products(s + 1, (5,) if s == 3 else (2, 4), "vector")
+            products(s + 1, (3,), "vector")
             quant_p(s - 2)
-            if s != 3:
-                products(s + 1, (5,), "vector")
             if s == 2:
                 quant_w(2)
+            products(s + 1, (5,), "vector", slice(0 if s > 2 else 0, 512))
             mx2(s - 2, 0, 4)
             turn_a(s + 1, 0)
             turn_a(s + 1, 1)
             empty_k(s - 1, 2)
             empty_k(s - 1, 3)
-            if s == 2:
-                products(s + 2, (0, 2), "scalar")
             empty_o(s - 2)
 
         a = LAST
@@ -363,8 +356,7 @@ def tile_rangeviewmetakernelfourneighbour_x1_kernel(tc, rel, w1, b1, w2, b2, f, 
         turn_a(a, 3)
         quant_m(a - 1, 0, 2)
         quant_m(a - 1, 2, 4)
-        take_m(a)
-        round_o((0, 1), "gpsimd")
+        round_o((0, 1), "gpsimd", a - 1)
         times_f(a - 2, 0, 2)
         times_f(a - 2, 2, 4)
         empty_a(a, 2)
@@ -385,7 +377,7 @@ def tile_rangeviewmetakernelfourneighbour_x1_kernel(tc, rel, w1, b1, w2, b2, f, 
         empty_t(0, 2)
         quant_m(a, 0, 2)
         quant_m(a, 2, 4)
-        round_o((2, 3), "gpsimd")
+        round_o((2, 3), "gpsimd", a)
         first_stage(a)
         empty_o(a - 2)
         times_f(a - 1, 0, 2)

@@ -21,6 +21,7 @@ W2 = J
 GUARD = (1.0 + 2.0**-10) * 2.0**-48
 FLOOR = 2.0**-70
 PRODS = 22
+ROUND = 3
 
 
 def tile_rangeviewmetakernelfourneighbour_x1_kernel(tc, rel, w1, b1, w2, b2, f, wo, out_0, out_1, out_2):
@@ -44,11 +45,11 @@ def tile_rangeviewmetakernelfourneighbour_x1_kernel(tc, rel, w1, b1, w2, b2, f, 
         nc.sync.dma_start(out=w1_col, in_=w1.rearrange("i (p t) -> p i t", t=4))
         nc.sync.dma_start(out=rel_0[:], in_=rel_rows[:, 0, :])
         nc.sync.dma_start(out=w_raw[W2][:], in_=w2.rearrange("(p k) c -> p k c", k=4))
-        nc.sync.dma_start(out=b1_raw[:], in_=b1.rearrange("(p t) -> p t", t=4))
         nc.sync.dma_start(out=rel_raw[:, 1:, 0:12], in_=rel_rows[:, 1:, :])
-        nc.sync.dma_start(out=b2_raw[:], in_=b2.rearrange("(p t) -> p t", t=4))
         for j in range(J):
             nc.sync.dma_start(out=w_raw[j][:], in_=wo[j].rearrange("(p k) c -> p k c", k=4))
+            if j < 2:
+                nc.sync.dma_start(out=(b1_raw, b2_raw)[j][:], in_=(b1, b2)[j].rearrange("(p t) -> p t", t=4))
         for a in range(TILES):
             nc.sync.dma_start(out=f_sb[a][:], in_=f[a * 128 : (a + 1) * 128])
 
@@ -57,7 +58,6 @@ def tile_rangeviewmetakernelfourneighbour_x1_kernel(tc, rel, w1, b1, w2, b2, f, 
         make_identity(nc, ident[:])
 
         relf = keep.tile([128, TILES, 12], F32, name="relf")
-        b1_f = keep.tile([128, 4], F32, name="b1_f")
         largest = keep.tile([128, 1], F32, name="largest")
         pivot = keep.tile([128, 4], F32, name="pivot")
         inverse = keep.tile([128, 4], F32, name="inverse")
@@ -69,10 +69,9 @@ def tile_rangeviewmetakernelfourneighbour_x1_kernel(tc, rel, w1, b1, w2, b2, f, 
         o_s = keep.tile([128, N], U8, name="o_s", align_bytes=64)
         o_bf = keep.tile([128, 4 * N], BF16, name="o_bf", align_bytes=64)
 
-        w_grp, prods, a_ps, a_sb, m_bf, m_q = {}, {}, {}, {}, {}, {}
+        w_grp, prods, a_ps, a_sb, m_buf, m_bf, m_q = {}, {}, {}, {}, {}, {}, {}
         k_ps, k_sb, f_ps, p_bf, p_q = {}, {}, {}, {}, {}
-        o_ps, r_sb, o_w, t_ps = {}, {}, {}, {}
-        sums = set()
+        o_ps, r_grp, r_sb, o_w, t_ps = {}, {}, {}, {}, {}
 
         def group_w(x, part0, part1, engine):
             if x not in w_grp:
@@ -92,51 +91,40 @@ def tile_rangeviewmetakernelfourneighbour_x1_kernel(tc, rel, w1, b1, w2, b2, f, 
         def quant_w(x):
             nc.vector.quantize_mx(out=w_q[x][:].bitcast(FP8X4), scales=w_s[x][:], in_=w_grp[x][:])
 
-        def products(a, xs, engine, cols=slice(0, 512)):
+        def products(a, xs, engine):
             for x in xs:
                 j, i = divmod(x, 2)
                 if engine == "gpsimd" and x == xs[0]:
                     prods[a, x] = m_bf[a - 2][:, 0:1024].bitcast(F32)
-                elif (a, x) not in prods:
+                else:
                     prods[a, x] = work.tile([128, 512], F32, name="prod", bufs=PRODS)[:]
                 factor = relf[:, a, 3 * j + 1 + i : 3 * j + 2 + i]
                 first = relf[:, a, 3 * j : 3 * j + 1] if i == 0 else 0.0
                 if engine == "scalar":
-                    nc.scalar.activation(prods[a, x][:, cols], ratio_row[i][:, cols], ACT.Identity, scale=factor, bias=first)
+                    nc.scalar.activation(prods[a, x], ratio_row[i][:], ACT.Identity, scale=factor, bias=first)
                 else:
                     queue = nc.gpsimd if engine == "gpsimd" else nc.vector
-                    queue.tensor_scalar(out=prods[a, x][:, cols], in0=ratio_row[i][:, cols], scalar1=factor, scalar2=first, op0=ALU.mult, op1=ALU.add)
-
-        def summed(a, j):
-            prods[a, 2 * j + 1] = work.tile([128, 512], F32, name="prod", bufs=PRODS)[:]
-            nc.vector.scalar_tensor_tensor(out=prods[a, 2 * j + 1], in0=ratio_row[1][:], scalar=relf[:, a, 3 * j + 2 : 3 * j + 3], in1=prods[a, 2 * j], op0=ALU.mult, op1=ALU.add)
-            sums.add((a, j))
+                    queue.tensor_scalar(out=prods[a, x], in0=ratio_row[i][:], scalar1=factor, scalar2=first, op0=ALU.mult, op1=ALU.add)
 
         def turn_a(a, t, js=range(J), tag="a_ps", bufs=3):
             if (a, t) not in a_ps:
                 a_ps[a, t] = psum.tile([128, 512], F32, name=tag, bufs=bufs)
             for j in js:
-                terms = (1,) if (a, j) in sums else (0, 1)
-                for i in terms:
-                    nc.tensor.matmul(a_ps[a, t][:, j * 128 : (j + 1) * 128], lhsT=prods[a, 2 * j + i][:, t * 128 : (t + 1) * 128], rhs=ident[:], start=(i == terms[0]), stop=(i == 1), is_transpose=True)
-
-        def take_a(a):
-            if a not in a_sb:
-                a_sb[a] = work.tile([128, 128, 4, J], F32, name="a_sb")
+                for i in range(2):
+                    nc.tensor.matmul(a_ps[a, t][:, j * 128 : (j + 1) * 128], lhsT=prods[a, 2 * j + i][:, t * 128 : (t + 1) * 128], rhs=ident[:], start=(i == 0), stop=(i == 1), is_transpose=True)
 
         def empty_a(a, t):
-            take_a(a)
+            if a not in a_sb:
+                a_sb[a] = work.tile([128, 128, 4, J], F32, name="a_sb")
             nc.scalar.activation(a_sb[a][:, :, t, :], a_ps[a, t][:].rearrange("p (j n) -> p n j", j=J), ACT.Identity, scale=pivot[:, t : t + 1], bias=b1_raw[:, t : t + 1])
-
-        def empty_a_vector(a, t):
-            take_a(a)
-            nc.vector.tensor_scalar(out=a_sb[a][:, :, t, :], in0=a_ps[a, t][:].rearrange("p (j n) -> p n j", j=J), scalar1=pivot[:, t : t + 1], scalar2=b1_f[:, t : t + 1], op0=ALU.mult, op1=ALU.add)
 
         def leaky(a, j0=0, j1=J):
             if a not in m_bf:
-                m_bf[a] = work.tile([128, 2048], BF16, name="m_bf", align_bytes=64, bufs=3)
+                spare = 512 if a == LAST - 1 else 0
+                m_buf[a] = work.tile([128, spare + 2048], BF16, name="m_bf", align_bytes=64, bufs=3)
+                m_bf[a] = m_buf[a][:, spare:]
             src = a_sb[a][:].rearrange("p n t j -> p (n t) j")[:, :, j0:j1]
-            out = m_bf[a][:].rearrange("p (j x) -> p x j", j=J)[:, :, j0:j1]
+            out = m_bf[a].rearrange("p (j x) -> p x j", j=J)[:, :, j0:j1]
             nc.vector.scalar_tensor_tensor(out=out, in0=src, scalar=SLOPE, in1=src, op0=ALU.mult, op1=ALU.max)
 
         def quant_m(a, j0=0, j1=J):
@@ -200,25 +188,22 @@ def tile_rangeviewmetakernelfourneighbour_x1_kernel(tc, rel, w1, b1, w2, b2, f, 
             nc.vector.tensor_copy(out=out, in_=t_ps[a][:].rearrange("p t n -> p n t"))
 
         def empty_o(a):
-            r_sb[a] = work.tile([128, 512], F32, name="r_sb", bufs=TILES)
-            nc.scalar.activation(r_sb[a][:].rearrange("n (m t) -> n m t", t=4), o_ps[a][:].rearrange("n (t m) -> n m t", t=4), ACT.Identity)
-            nc.sync.dma_start(out=out_0[a * 128 : (a + 1) * 128, :], in_=r_sb[a][:])
+            if a % ROUND == 0:
+                r_grp[a // ROUND] = work.tile([128, min(ROUND, TILES - a) * 512], F32, name="r_sb", bufs=3)
+            r_sb[a] = r_grp[a // ROUND][:, a % ROUND * 512 : (a % ROUND + 1) * 512]
+            nc.scalar.activation(r_sb[a].rearrange("n (m t) -> n m t", t=4), o_ps[a][:].rearrange("n (t m) -> n m t", t=4), ACT.Identity)
+            queue = nc.scalar if a == LAST else nc.sync
+            queue.dma_start(out=out_0[a * 128 : (a + 1) * 128, :], in_=r_sb[a])
 
-        def round_o(tiles, engine, spent=None):
-            if spent is None:
-                words = work.tile([128, 512 * len(tiles)], BF16, name="o_w", align_bytes=64, bufs=3)
-            else:
-                words = m_bf[spent]
-            for x, a in enumerate(tiles):
-                o_w[a] = words[:, x * 512 : (x + 1) * 512].rearrange("n (h m e) -> n h m e", h=2, e=2)
-                src = r_sb[a][:].rearrange("n (m h e) -> n h m e", h=2, e=2)
-                if engine == "gpsimd":
-                    nc.gpsimd.tensor_scalar(out=o_w[a], in0=src, scalar1=1.0, scalar2=0.0, op0=ALU.mult, op1=ALU.add)
-                else:
-                    nc.scalar.activation(o_w[a], src, ACT.Identity)
+        def round_o(a0, a1, spent):
+            words = spent[:, 0 : (a1 - a0) * 512].rearrange("n (h m e) -> n h m e", h=2, e=2)
+            src = r_grp[a0 // ROUND][:, a0 % ROUND * 512 : (a0 % ROUND + a1 - a0) * 512].rearrange("n (m h e) -> n h m e", h=2, e=2)
+            nc.gpsimd.tensor_scalar(out=words, in0=src, scalar1=1.0, scalar2=0.0, op0=ALU.mult, op1=ALU.add)
+            for a in range(a0, a1):
+                o_w[a] = words[:, :, (a - a0) * 128 : (a - a0 + 1) * 128, :]
 
         def round_from_bank(a):
-            words = work.tile([128, 1, 2, 128, 2], BF16, name="o_w", align_bytes=64, bufs=3)
+            words = work.tile([128, 1, 2, 128, 2], BF16, name="o_w", align_bytes=64, bufs=1)
             o_w[a] = words[:, 0]
             nc.scalar.activation(o_w[a], o_ps[a][:].rearrange("n (h e m) -> n h m e", h=2, e=2), ACT.Identity)
 
@@ -339,7 +324,7 @@ def tile_rangeviewmetakernelfourneighbour_x1_kernel(tc, rel, w1, b1, w2, b2, f, 
             quant_p(s - 2)
             if s == 2:
                 quant_w(2)
-            products(s + 1, (5,), "vector", slice(0 if s > 2 else 0, 512))
+            products(s + 1, (5,), "vector")
             mx2(s - 2, 0, 4)
             turn_a(s + 1, 0)
             turn_a(s + 1, 1)
@@ -356,7 +341,7 @@ def tile_rangeviewmetakernelfourneighbour_x1_kernel(tc, rel, w1, b1, w2, b2, f, 
         turn_a(a, 3)
         quant_m(a - 1, 0, 2)
         quant_m(a - 1, 2, 4)
-        round_o((0, 1), "gpsimd", a - 1)
+        round_o(0, 3, m_buf[a - 1])
         times_f(a - 2, 0, 2)
         times_f(a - 2, 2, 4)
         empty_a(a, 2)
@@ -364,7 +349,8 @@ def tile_rangeviewmetakernelfourneighbour_x1_kernel(tc, rel, w1, b1, w2, b2, f, 
         empty_a(a, 3)
         turn_f(a - 1, 0)
         turn_f(a - 1, 1)
-        quant_p(a - 2)
+        quant_p(a - 2, 0, 2)
+        quant_p(a - 2, 2, 4)
         leaky(a, 0, 2)
         leaky(a, 2, 4)
         for t in range(4):
@@ -373,25 +359,24 @@ def tile_rangeviewmetakernelfourneighbour_x1_kernel(tc, rel, w1, b1, w2, b2, f, 
         turn_o(0, 2)
         turn_f(a, 0, "a_ps", 3)
         mx2(a - 2, 2, 4)
-        round_o((4,), "scalar")
         empty_t(0, 2)
+        empty_o(a - 2)
         quant_m(a, 0, 2)
         quant_m(a, 2, 4)
-        round_o((2, 3), "gpsimd", a)
+        round_o(3, 5, m_bf[a])
         first_stage(a)
-        empty_o(a - 2)
         times_f(a - 1, 0, 2)
         times_f(a - 1, 2, 4)
         for t in range(4):
             empty_k(a, t, 0, 2)
-        round_o((5,), "scalar")
         for t in range(4):
             empty_k(a, t, 2, 4)
         turn_f(a, 1)
-        turn_o(2, 4, "f_ps", 2)
+        turn_o(2, 4, "o_ps", 1)
         quant_p(a - 1, 0, 2)
         quant_p(a - 1, 2, 4)
-        mx2(a - 1, 0, 4)
+        round_o(5, 6, p_bf[a - 1])
+        mx2(a - 1, 0, 4, "f_ps", 2)
         turn_o(4, 6, "k_ps", 2)
         empty_t(2, 4)
         round_from_bank(a - 1)
@@ -414,9 +399,10 @@ def tile_rangeviewmetakernelfourneighbour_x1_kernel(tc, rel, w1, b1, w2, b2, f, 
         mx2_turned(a, 2, 4)
         mx2(a, 2, 4)
         quant_o(0, 4)
+        store_codes(0, 4)
         quant_o(4, 6)
         quant_o(6, 7)
-        store_codes(0, 7)
+        store_codes(4, 7)
         empty_turned(a)
         empty_o(a)
         quant_o(7, 8)

@@ -21,7 +21,8 @@ W2 = J
 GUARD = (1.0 + 2.0**-10) * 2.0**-48
 FLOOR = 2.0**-70
 PRODS = 22
-ROUND = 3
+ROUND = 2
+RING = 6
 
 
 def tile_rangeviewmetakernelfourneighbour_x1_kernel(tc, rel, w1, b1, w2, b2, f, wo, out_0, out_1, out_2):
@@ -69,9 +70,20 @@ def tile_rangeviewmetakernelfourneighbour_x1_kernel(tc, rel, w1, b1, w2, b2, f, 
         o_s = keep.tile([128, N], U8, name="o_s", align_bytes=64)
         o_bf = keep.tile([128, 4 * N], BF16, name="o_bf", align_bytes=64)
 
-        w_grp, prods, a_ps, a_sb, m_buf, m_bf, m_q = {}, {}, {}, {}, {}, {}, {}
+        w_grp, prods, a_ps, a_sb, m_bf, m_q = {}, {}, {}, {}, {}, {}
         k_ps, k_sb, f_ps, p_bf, p_q = {}, {}, {}, {}, {}
         o_ps, r_grp, r_sb, o_w, t_ps = {}, {}, {}, {}, {}
+
+        ring, held = [0], set()
+
+        def take_bank(shape, hold=False):
+            while ring[0] % RING in held:
+                ring[0] += 1
+            slot = ring[0] % RING
+            ring[0] += 1
+            if hold:
+                held.add(slot)
+            return psum.tile(shape, F32, name=f"bank{slot}")
 
         def group_w(x, part0, part1, engine):
             if x not in w_grp:
@@ -106,9 +118,9 @@ def tile_rangeviewmetakernelfourneighbour_x1_kernel(tc, rel, w1, b1, w2, b2, f, 
                     queue = nc.gpsimd if engine == "gpsimd" else nc.vector
                     queue.tensor_scalar(out=prods[a, x], in0=ratio_row[i][:], scalar1=factor, scalar2=first, op0=ALU.mult, op1=ALU.add)
 
-        def turn_a(a, t, js=range(J), tag="a_ps", bufs=3):
+        def turn_a(a, t, js=range(J)):
             if (a, t) not in a_ps:
-                a_ps[a, t] = psum.tile([128, 512], F32, name=tag, bufs=bufs)
+                a_ps[a, t] = take_bank([128, 512])
             for j in js:
                 for i in range(2):
                     nc.tensor.matmul(a_ps[a, t][:, j * 128 : (j + 1) * 128], lhsT=prods[a, 2 * j + i][:, t * 128 : (t + 1) * 128], rhs=ident[:], start=(i == 0), stop=(i == 1), is_transpose=True)
@@ -120,11 +132,9 @@ def tile_rangeviewmetakernelfourneighbour_x1_kernel(tc, rel, w1, b1, w2, b2, f, 
 
         def leaky(a, j0=0, j1=J):
             if a not in m_bf:
-                spare = 512 if a == LAST - 1 else 0
-                m_buf[a] = work.tile([128, spare + 2048], BF16, name="m_bf", align_bytes=64, bufs=3)
-                m_bf[a] = m_buf[a][:, spare:]
+                m_bf[a] = work.tile([128, 2048], BF16, name="m_bf", align_bytes=64, bufs=3)
             src = a_sb[a][:].rearrange("p n t j -> p (n t) j")[:, :, j0:j1]
-            out = m_bf[a].rearrange("p (j x) -> p x j", j=J)[:, :, j0:j1]
+            out = m_bf[a][:].rearrange("p (j x) -> p x j", j=J)[:, :, j0:j1]
             nc.vector.scalar_tensor_tensor(out=out, in0=src, scalar=SLOPE, in1=src, op0=ALU.mult, op1=ALU.max)
 
         def quant_m(a, j0=0, j1=J):
@@ -133,9 +143,8 @@ def tile_rangeviewmetakernelfourneighbour_x1_kernel(tc, rel, w1, b1, w2, b2, f, 
             cols = slice(j0 * 128, j1 * 128)
             nc.vector.quantize_mx(out=m_q[a][0][:, cols].bitcast(FP8X4), scales=m_q[a][1][:, cols], in_=m_bf[a][:, j0 * 512 : j1 * 512])
 
-        def mx1(a, t, tag="k_ps", bufs=2):
-            if (a, t) not in k_ps:
-                k_ps[a, t] = psum.tile([128, 512], F32, name=tag, bufs=bufs)
+        def mx1(a, t):
+            k_ps[a, t] = take_bank([128, 512])
             cols = slice(t * 128, (t + 1) * 128)
             nc.tensor.matmul_mx(k_ps[a, t][:], lhsT=w_q[W2][:, cols].bitcast(FP8X4), lhsT_scale=w_s[W2][:, cols], rhs=m_q[a][0][:].bitcast(FP8X4), rhs_scale=m_q[a][1][:], start=True, stop=True)
 
@@ -145,8 +154,8 @@ def tile_rangeviewmetakernelfourneighbour_x1_kernel(tc, rel, w1, b1, w2, b2, f, 
             src = k_ps[a, t][:, j0 * 128 : j1 * 128].rearrange("p (n i) -> p n i", i=4)
             nc.scalar.activation(k_sb[a][:, j0 * 32 : j1 * 32, t % 2, t // 2, :], src, ACT.Identity, bias=b2_raw[:, t : t + 1])
 
-        def turn_f(a, h, tag="f_ps", bufs=2):
-            f_ps[a, h] = psum.tile([128, 2, 256], F32, name=tag, bufs=bufs)
+        def turn_f(a, h, from_ring=False):
+            f_ps[a, h] = take_bank([128, 2, 256], hold=True) if from_ring else psum.tile([128, 2, 256], F32, name="f_ps", bufs=2)
             for jj in range(2):
                 words = f_sb[a][:, 2 * h + jj, :].bitcast(F32)
                 for g in range(2):
@@ -167,17 +176,17 @@ def tile_rangeviewmetakernelfourneighbour_x1_kernel(tc, rel, w1, b1, w2, b2, f, 
             cols = slice(j0 * 128, j1 * 128)
             nc.vector.quantize_mx(out=p_q[a][0][:, cols].bitcast(FP8X4), scales=p_q[a][1][:, cols], in_=p_bf[a][:, j0 * 512 : j1 * 512])
 
-        def mx2(a, j0, j1, tag="o_ps", bufs=1):
+        def mx2(a, j0, j1, from_ring=True):
             for j in range(j0, j1):
                 if j == 0:
-                    o_ps[a] = psum.tile([128, 512], F32, name=tag, bufs=bufs)
+                    o_ps[a] = take_bank([128, 512]) if from_ring else psum.tile([128, 512], F32, name="f_ps", bufs=2)
                 cols = slice(j * 128, (j + 1) * 128)
                 nc.tensor.matmul_mx(o_ps[a][:], lhsT=p_q[a][0][:, cols].bitcast(FP8X4), lhsT_scale=p_q[a][1][:, cols], rhs=w_q[j][:].bitcast(FP8X4), rhs_scale=w_s[j][:], start=(j == 0), stop=(j == J - 1))
 
         def mx2_turned(a, j0, j1):
             for j in range(j0, j1):
                 if j == 0:
-                    t_ps[a] = psum.tile([128, 4, 128], F32, name="a_ps", bufs=3)
+                    t_ps[a] = take_bank([128, 4, 128])
                 rows = slice(j * 128, (j + 1) * 128)
                 for t in range(4):
                     cols = slice(t * 128, (t + 1) * 128)
@@ -189,9 +198,9 @@ def tile_rangeviewmetakernelfourneighbour_x1_kernel(tc, rel, w1, b1, w2, b2, f, 
 
         def empty_o(a):
             if a % ROUND == 0:
-                r_grp[a // ROUND] = work.tile([128, min(ROUND, TILES - a) * 512], F32, name="r_sb", bufs=3)
+                r_grp[a // ROUND] = work.tile([128, ROUND * 512], F32, name="r_sb", bufs=TILES // ROUND)
             r_sb[a] = r_grp[a // ROUND][:, a % ROUND * 512 : (a % ROUND + 1) * 512]
-            nc.scalar.activation(r_sb[a].rearrange("n (m t) -> n m t", t=4), o_ps[a][:].rearrange("n (t m) -> n m t", t=4), ACT.Identity)
+            nc.scalar.copy(r_sb[a].rearrange("n (m t) -> n m t", t=4), o_ps[a][:].rearrange("n (t m) -> n m t", t=4))
             queue = nc.scalar if a == LAST else nc.sync
             queue.dma_start(out=out_0[a * 128 : (a + 1) * 128, :], in_=r_sb[a])
 
@@ -202,13 +211,18 @@ def tile_rangeviewmetakernelfourneighbour_x1_kernel(tc, rel, w1, b1, w2, b2, f, 
             for a in range(a0, a1):
                 o_w[a] = words[:, :, (a - a0) * 128 : (a - a0 + 1) * 128, :]
 
-        def round_from_bank(a):
-            words = work.tile([128, 1, 2, 128, 2], BF16, name="o_w", align_bytes=64, bufs=1)
+        def round_scalar(a):
+            words = work.tile([128, 1, 2, 128, 2], BF16, name="o_w", align_bytes=64, bufs=2)
             o_w[a] = words[:, 0]
-            nc.scalar.activation(o_w[a], o_ps[a][:].rearrange("n (h e m) -> n h m e", h=2, e=2), ACT.Identity)
+            nc.scalar.copy(o_w[a], r_sb[a].rearrange("n (m h e) -> n h m e", h=2, e=2))
 
-        def turn_o(a0, a1, tag="a_ps", bufs=3):
-            t_ps[a0] = psum.tile([128, 2, 2, 128], F32, name=tag, bufs=bufs)
+        def round_from_bank(a):
+            words = work.tile([128, 1, 2, 128, 2], BF16, name="o_w", align_bytes=64, bufs=2)
+            o_w[a] = words[:, 0]
+            nc.scalar.copy(o_w[a], o_ps[a][:].rearrange("n (h e m) -> n h m e", h=2, e=2))
+
+        def turn_o(a0, a1):
+            t_ps[a0] = take_bank([128, 2, 2, 128])
             for a in range(a0, a1):
                 words = o_w[a].rearrange("n h m e -> n h (m e)").bitcast(F32)
                 for h in range(2):
@@ -227,10 +241,8 @@ def tile_rangeviewmetakernelfourneighbour_x1_kernel(tc, rel, w1, b1, w2, b2, f, 
             nc.sync.dma_start(out=out_1[0, :, cols, :].rearrange("p m t -> p (m t)").bitcast(I32), in_=o_q[:, cols].bitcast(I32))
 
         def first_stage(a):
-            mx1(a, 0)
-            mx1(a, 1)
-            mx1(a, 2, "a_ps", 3)
-            mx1(a, 3, "a_ps", 3)
+            for t in range(4):
+                mx1(a, t)
 
         nc.vector.tensor_reduce(out=largest[:], in_=w1_pad[:], op=ALU.max, axis=mybir.AxisListType.X, apply_absolute_value=True)
         nc.scalar.activation(relf[:, 0, :], rel_0[:], ACT.Identity)
@@ -245,12 +257,12 @@ def tile_rangeviewmetakernelfourneighbour_x1_kernel(tc, rel, w1, b1, w2, b2, f, 
             for t in range(4):
                 nc.tensor.transpose(bank[:, t, :], ratio[:, i, t : t + 1].to_broadcast([128, 128]), ident[:])
             nc.scalar.copy(ratio_row[i][:], bank[:].rearrange("p t m -> p (t m)"))
+            if i == 0:
+                nc.scalar.activation(relf[:, 1:, :], rel_raw[:, 1:, 0:12], ACT.Identity)
         products(0, (0, 2, 1, 3, 4, 5, 6, 7), "vector")
-        nc.scalar.activation(relf[:, 1:, :], rel_raw[:, 1:, 0:12], ACT.Identity)
         for j in range(2):
-            for t in range(3):
+            for t in range(4):
                 turn_a(0, t, (j,))
-            turn_a(0, 3, (j,), "k_ps", 2)
         for t in range(4):
             turn_a(0, t, (2, 3))
         products(1, (0,), "scalar")
@@ -322,9 +334,9 @@ def tile_rangeviewmetakernelfourneighbour_x1_kernel(tc, rel, w1, b1, w2, b2, f, 
             mx1(s - 1, 3)
             products(s + 1, (3,), "vector")
             quant_p(s - 2)
+            products(s + 1, (5,), "vector")
             if s == 2:
                 quant_w(2)
-            products(s + 1, (5,), "vector")
             mx2(s - 2, 0, 4)
             turn_a(s + 1, 0)
             turn_a(s + 1, 1)
@@ -341,7 +353,7 @@ def tile_rangeviewmetakernelfourneighbour_x1_kernel(tc, rel, w1, b1, w2, b2, f, 
         turn_a(a, 3)
         quant_m(a - 1, 0, 2)
         quant_m(a - 1, 2, 4)
-        round_o(0, 3, m_buf[a - 1])
+        round_o(0, 2, m_bf[a - 1])
         times_f(a - 2, 0, 2)
         times_f(a - 2, 2, 4)
         empty_a(a, 2)
@@ -355,15 +367,16 @@ def tile_rangeviewmetakernelfourneighbour_x1_kernel(tc, rel, w1, b1, w2, b2, f, 
         leaky(a, 2, 4)
         for t in range(4):
             empty_k(a - 1, t)
-        mx2(a - 2, 0, 2)
         turn_o(0, 2)
-        turn_f(a, 0, "a_ps", 3)
+        mx2(a - 2, 0, 2)
+        turn_f(a, 0, from_ring=True)
         mx2(a - 2, 2, 4)
         empty_t(0, 2)
+        round_scalar(4)
         empty_o(a - 2)
         quant_m(a, 0, 2)
         quant_m(a, 2, 4)
-        round_o(3, 5, m_bf[a])
+        round_o(2, 4, m_bf[a])
         first_stage(a)
         times_f(a - 1, 0, 2)
         times_f(a - 1, 2, 4)
@@ -372,12 +385,12 @@ def tile_rangeviewmetakernelfourneighbour_x1_kernel(tc, rel, w1, b1, w2, b2, f, 
         for t in range(4):
             empty_k(a, t, 2, 4)
         turn_f(a, 1)
-        turn_o(2, 4, "o_ps", 1)
+        turn_o(2, 4)
         quant_p(a - 1, 0, 2)
         quant_p(a - 1, 2, 4)
         round_o(5, 6, p_bf[a - 1])
-        mx2(a - 1, 0, 4, "f_ps", 2)
-        turn_o(4, 6, "k_ps", 2)
+        mx2(a - 1, 0, 4, from_ring=False)
+        turn_o(4, 6)
         empty_t(2, 4)
         round_from_bank(a - 1)
         empty_o(a - 1)
@@ -388,7 +401,7 @@ def tile_rangeviewmetakernelfourneighbour_x1_kernel(tc, rel, w1, b1, w2, b2, f, 
         times_f(a, 2, 3)
         quant_p(a, 1, 2)
         mx2_turned(a, 0, 1)
-        mx2(a, 0, 1, "k_ps", 2)
+        mx2(a, 0, 1)
         mx2_turned(a, 1, 2)
         mx2(a, 1, 2)
         turn_o(6, 7)

@@ -103,20 +103,20 @@ def tile_rangeviewmetakernelfourneighbour_x1_kernel(tc, rel, w1, b1, w2, b2, f, 
         def quant_w(x):
             nc.vector.quantize_mx(out=w_q[x][:].bitcast(FP8X4), scales=w_s[x][:], in_=w_grp[x][:])
 
-        def products(a, xs, engine):
+        def products(a, xs, engine, cols=slice(0, 512)):
             for x in xs:
                 j, i = divmod(x, 2)
-                if engine == "gpsimd" and x == xs[0]:
+                if engine == "gpsimd" and x == 0:
                     prods[a, x] = m_bf[a - 2][:, 0:1024].bitcast(F32)
-                else:
+                elif (a, x) not in prods:
                     prods[a, x] = work.tile([128, 512], F32, name="prod", bufs=PRODS)[:]
                 factor = relf[:, a, 3 * j + 1 + i : 3 * j + 2 + i]
                 first = relf[:, a, 3 * j : 3 * j + 1] if i == 0 else 0.0
                 if engine == "scalar":
-                    nc.scalar.activation(prods[a, x], ratio_row[i][:], ACT.Identity, scale=factor, bias=first)
+                    nc.scalar.activation(prods[a, x][:, cols], ratio_row[i][:, cols], ACT.Identity, scale=factor, bias=first)
                 else:
                     queue = nc.gpsimd if engine == "gpsimd" else nc.vector
-                    queue.tensor_scalar(out=prods[a, x], in0=ratio_row[i][:], scalar1=factor, scalar2=first, op0=ALU.mult, op1=ALU.add)
+                    queue.tensor_scalar(out=prods[a, x][:, cols], in0=ratio_row[i][:, cols], scalar1=factor, scalar2=first, op0=ALU.mult, op1=ALU.add)
 
         def turn_a(a, t, js=range(J)):
             if (a, t) not in a_ps:
@@ -205,28 +205,28 @@ def tile_rangeviewmetakernelfourneighbour_x1_kernel(tc, rel, w1, b1, w2, b2, f, 
             queue.dma_start(out=out_0[a * 128 : (a + 1) * 128, :], in_=r_sb[a])
 
         def round_o(a0, a1, spent):
-            words = spent[:, 0 : (a1 - a0) * 512].rearrange("n (h m e) -> n h m e", h=2, e=2)
-            src = r_grp[a0 // ROUND][:, a0 % ROUND * 512 : (a0 % ROUND + a1 - a0) * 512].rearrange("n (m h e) -> n h m e", h=2, e=2)
-            nc.gpsimd.tensor_scalar(out=words, in0=src, scalar1=1.0, scalar2=0.0, op0=ALU.mult, op1=ALU.add)
+            rounded = spent[:, 0 : (a1 - a0) * 512]
+            src = r_grp[a0 // ROUND][:, a0 % ROUND * 512 : (a0 % ROUND + a1 - a0) * 512]
+            nc.gpsimd.tensor_scalar(out=rounded, in0=src, scalar1=1.0, scalar2=0.0, op0=ALU.mult, op1=ALU.add)
             for a in range(a0, a1):
-                o_w[a] = words[:, :, (a - a0) * 128 : (a - a0 + 1) * 128, :]
+                words = rounded[:, (a - a0) * 512 : (a - a0 + 1) * 512].bitcast(F32)
+                o_w[a] = [words[:, h:256:2] for h in range(2)]
 
         def round_scalar(a):
             words = work.tile([128, 1, 2, 128, 2], BF16, name="o_w", align_bytes=64, bufs=2)
-            o_w[a] = words[:, 0]
-            nc.scalar.copy(o_w[a], r_sb[a].rearrange("n (m h e) -> n h m e", h=2, e=2))
+            nc.scalar.copy(words[:, 0], r_sb[a].rearrange("n (m h e) -> n h m e", h=2, e=2))
+            o_w[a] = [words[:, 0, h].rearrange("n m e -> n (m e)").bitcast(F32) for h in range(2)]
 
         def round_from_bank(a):
             words = work.tile([128, 1, 2, 128, 2], BF16, name="o_w", align_bytes=64, bufs=2)
-            o_w[a] = words[:, 0]
-            nc.scalar.copy(o_w[a], o_ps[a][:].rearrange("n (h e m) -> n h m e", h=2, e=2))
+            nc.scalar.copy(words[:, 0], o_ps[a][:].rearrange("n (h e m) -> n h m e", h=2, e=2))
+            o_w[a] = [words[:, 0, h].rearrange("n m e -> n (m e)").bitcast(F32) for h in range(2)]
 
         def turn_o(a0, a1):
             t_ps[a0] = take_bank([128, 2, 2, 128])
             for a in range(a0, a1):
-                words = o_w[a].rearrange("n h m e -> n h (m e)").bitcast(F32)
                 for h in range(2):
-                    nc.tensor.transpose(t_ps[a0][:, a - a0, h, :], words[:, h, :], ident[:])
+                    nc.tensor.transpose(t_ps[a0][:, a - a0, h, :], o_w[a][h], ident[:])
 
         def empty_t(a0, a1):
             out = o_bf[:, a0 * 512 : a1 * 512].bitcast(F32).rearrange("p (a n h) -> p a n h", n=128, h=2)
@@ -313,7 +313,8 @@ def tile_rangeviewmetakernelfourneighbour_x1_kernel(tc, rel, w1, b1, w2, b2, f, 
             turn_a(s, 3)
             quant_m(s - 1, 0, 2)
             quant_m(s - 1, 2, 4)
-            products(s + 1, (0, 2, 4), "gpsimd")
+            products(s + 1, (0, 2), "gpsimd")
+            products(s + 1, (4,), "gpsimd", slice(0, 384 if s > 2 else 512))
             times_f(s - 2, 0, 2)
             times_f(s - 2, 2, 4)
             empty_a(s, 2)
@@ -322,15 +323,17 @@ def tile_rangeviewmetakernelfourneighbour_x1_kernel(tc, rel, w1, b1, w2, b2, f, 
                 group_w(2, 0, 4, "scalar")
             mx1(s - 1, 0)
             mx1(s - 1, 1)
+            mx1(s - 1, 2)
             empty_k(s - 1, 0)
             empty_k(s - 1, 1)
             if s == 2:
                 quant_w(3)
                 group_w(2, 4, 8, "vector")
             products(s + 1, (6, 7), "scalar")
+            if s > 2:
+                products(s + 1, (4,), "scalar", slice(384, 512))
             turn_f(s - 1, 0)
             turn_f(s - 1, 1)
-            mx1(s - 1, 2)
             mx1(s - 1, 3)
             products(s + 1, (3,), "vector")
             quant_p(s - 2)
@@ -403,14 +406,13 @@ def tile_rangeviewmetakernelfourneighbour_x1_kernel(tc, rel, w1, b1, w2, b2, f, 
         mx2_turned(a, 0, 1)
         mx2(a, 0, 1)
         mx2_turned(a, 1, 2)
-        mx2(a, 1, 2)
         turn_o(6, 7)
         empty_t(6, 7)
         times_f(a, 3, 4)
         quant_p(a, 2, 3)
         quant_p(a, 3, 4)
         mx2_turned(a, 2, 4)
-        mx2(a, 2, 4)
+        mx2(a, 1, 4)
         quant_o(0, 4)
         store_codes(0, 4)
         quant_o(4, 6)

@@ -90,11 +90,11 @@ def tile_rangeviewmetakernelfourneighbour_x1_kernel(tc, rel, w1, b1, w2, b2, f, 
                 w_grp[x] = work.tile([128, 2048], BF16, name="w_grp", align_bytes=64, bufs=4)
             ms = slice(part0 * 16, part1 * 16)
             if x == W2:
-                dst = w_grp[x][:].rearrange("p (t m k) -> p m k t", t=4, k=4)[:, ms]
-                src = w_raw[x][:].rearrange("p k (m t) -> p m k t", t=4)[:, ms]
+                dst = w_grp[x][:].rearrange("p (t m e g) -> p m e t g", t=4, e=2, g=2)[:, ms]
+                src = w_raw[x][:].rearrange("p (e g) (m t) -> p m e t g", t=4, g=2)[:, ms]
             else:
-                dst = w_grp[x][:].rearrange("p (t m e g) -> p m g e t", t=4, e=2, g=2)[:, ms]
-                src = w_raw[x][:].rearrange("p (g e) (m t) -> p m g e t", t=4, e=2)[:, ms]
+                dst = w_grp[x][:].rearrange("p (t m e g) -> p m e t g", t=4, e=2, g=2)[:, ms]
+                src = w_raw[x][:].rearrange("p (g e) (m t) -> p m e t g", t=4, e=2)[:, ms]
             if engine == "scalar":
                 nc.scalar.copy(dst, src)
             else:
@@ -314,7 +314,7 @@ def tile_rangeviewmetakernelfourneighbour_x1_kernel(tc, rel, w1, b1, w2, b2, f, 
             quant_m(s - 1, 0, 2)
             quant_m(s - 1, 2, 4)
             products(s + 1, (0, 2), "gpsimd")
-            products(s + 1, (4,), "gpsimd", slice(0, 384 if s > 2 else 512))
+            products(s + 1, (4,), "gpsimd", slice(0, 384))
             times_f(s - 2, 0, 2)
             times_f(s - 2, 2, 4)
             empty_a(s, 2)
@@ -330,8 +330,7 @@ def tile_rangeviewmetakernelfourneighbour_x1_kernel(tc, rel, w1, b1, w2, b2, f, 
                 quant_w(3)
                 group_w(2, 4, 8, "vector")
             products(s + 1, (6, 7), "scalar")
-            if s > 2:
-                products(s + 1, (4,), "scalar", slice(384, 512))
+            products(s + 1, (4,), "scalar", slice(384, 512))
             turn_f(s - 1, 0)
             turn_f(s - 1, 1)
             mx1(s - 1, 3)

from contextlib import ExitStack

import concourse.mybir as mybir
from concourse.masks import make_identity

F32 = mybir.dt.float32
BF16 = mybir.dt.bfloat16
U32 = mybir.dt.uint32
I32 = mybir.dt.int32
U8 = mybir.dt.uint8
FP8X4 = mybir.dt.float8_e4m3fn_x4
ALU = mybir.AluOpType
ACT = mybir.ActivationFunctionType

N, J, H, C, O = 1024, 4, 512, 512, 512
FLOPS = 2 * N * J * H * C + 2 * N * J * C * O
SLOPE = 0.2
TILES = N // 128
LAST = TILES - 1
W2 = J
GUARD = (1.0 + 2.0**-10) * 2.0**-48
FLOOR = 2.0**-70
PRODS = 22
ROUND = 2
RING = 6


def tile_rangeviewmetakernelfourneighbour_x1_kernel(tc, rel, w1, b1, w2, b2, f, wo, out_0, out_1, out_2):
    nc = tc.nc
    with ExitStack() as ctx:
        keep = ctx.enter_context(tc.tile_pool(name="keep", bufs=1))
        work = ctx.enter_context(tc.tile_pool(name="work", bufs=2))
        psum = ctx.enter_context(tc.psum_pool(name="psum", bufs=1))
        ctx.enter_context(tc.manual_schedule())

        rel_0 = keep.tile([128, 12], BF16, name="rel_0")
        rel_raw = keep.tile([128, TILES, 16], BF16, name="rel_raw")
        w1_pad = keep.tile([128, 20], BF16, name="w1_pad")
        w1_col = w1_pad[:, 8:20].rearrange("p (i t) -> p i t", t=4)
        b1_raw = keep.tile([128, 4], BF16, name="b1_raw")
        b2_raw = keep.tile([128, 4], BF16, name="b2_raw")
        w_raw = [keep.tile([128, 4, 512], BF16, name=f"w_raw{x}") for x in range(J + 1)]
        f_sb = [keep.tile([128, J, 512], BF16, name=f"f_sb{a}") for a in range(TILES)]

        rel_rows = rel.rearrange("(a p) j i -> p a (j i)", p=128)
        nc.sync.dma_start(out=w1_col, in_=w1.rearrange("i (p t) -> p i t", t=4))
        nc.sync.dma_start(out=rel_0[:], in_=rel_rows[:, 0, :])
        nc.sync.dma_start(out=w_raw[W2][:], in_=w2.rearrange("(p k) c -> p k c", k=4))
        nc.sync.dma_start(out=rel_raw[:, 1:, 0:12], in_=rel_rows[:, 1:, :])
        for j in range(J):
            nc.sync.dma_start(out=w_raw[j][:], in_=wo[j].rearrange("(p k) c -> p k c", k=4))
            if j < 2:
                nc.sync.dma_start(out=(b1_raw, b2_raw)[j][:], in_=(b1, b2)[j].rearrange("(p t) -> p t", t=4))
        for a in range(TILES):
            nc.sync.dma_start(out=f_sb[a][:], in_=f[a * 128 : (a + 1) * 128])

        nc.vector.memset(w1_pad[:, 0:8], FLOOR)
        ident = keep.tile([128, 128], F32, name="ident")
        make_identity(nc, ident[:])

        relf = keep.tile([128, TILES, 12], F32, name="relf")
        largest = keep.tile([128, 1], F32, name="largest")
        pivot = keep.tile([128, 4], F32, name="pivot")
        inverse = keep.tile([128, 4], F32, name="inverse")
        ratio = keep.tile([128, 2, 4], F32, name="ratio")
        ratio_row = [keep.tile([128, 512], F32, name=f"ratio_row{i}") for i in range(2)]
        w_q = [keep.tile([128, 512], U32, name=f"w_q{x}", align_bytes=64) for x in range(J + 1)]
        w_s = [keep.tile([128, 512], U8, name=f"w_s{x}", align_bytes=64) for x in range(J + 1)]
        o_q = keep.tile([128, N], U32, name="o_q", align_bytes=64)
        o_s = keep.tile([128, N], U8, name="o_s", align_bytes=64)
        o_bf = keep.tile([128, 4 * N], BF16, name="o_bf", align_bytes=64)

        w_grp, prods, a_ps, a_sb, m_bf, m_q = {}, {}, {}, {}, {}, {}
        k_ps, k_sb, f_ps, p_bf, p_q = {}, {}, {}, {}, {}
        o_ps, r_grp, r_sb, o_w, t_ps = {}, {}, {}, {}, {}

        ring, held = [0], set()

        def take_bank(shape, hold=False):
            while ring[0] % RING in held:
                ring[0] += 1
            slot = ring[0] % RING
            ring[0] += 1
            if hold:
                held.add(slot)
            return psum.tile(shape, F32, name=f"bank{slot}")

        def group_w(x, part0, part1, engine):
            if x not in w_grp:
                w_grp[x] = work.tile([128, 2048], BF16, name="w_grp", align_bytes=64, bufs=4)
            ms = slice(part0 * 16, part1 * 16)
            if x == W2:
                dst = w_grp[x][:].rearrange("p (t m e g) -> p m e t g", t=4, e=2, g=2)[:, ms]
                src = w_raw[x][:].rearrange("p (e g) (m t) -> p m e t g", t=4, g=2)[:, ms]
            else:
                dst = w_grp[x][:].rearrange("p (t m e g) -> p m e t g", t=4, e=2, g=2)[:, ms]
                src = w_raw[x][:].rearrange("p (g e) (m t) -> p m e t g", t=4, e=2)[:, ms]
            if engine == "scalar":
                nc.scalar.copy(dst, src)
            else:
                nc.vector.tensor_copy(out=dst, in_=src)

        def quant_w(x):
            nc.vector.quantize_mx(out=w_q[x][:].bitcast(FP8X4), scales=w_s[x][:], in_=w_grp[x][:])

        def products(a, xs, engine, cols=slice(0, 512)):
            for x in xs:
                j, i = divmod(x, 2)
                if engine == "gpsimd" and x == 0:
                    prods[a, x] = m_bf[a - 2][:, 0:1024].bitcast(F32)
                elif (a, x) not in prods:
                    prods[a, x] = work.tile([128, 512], F32, name="prod", bufs=PRODS)[:]
                factor = relf[:, a, 3 * j + 1 + i : 3 * j + 2 + i]
                first = relf[:, a, 3 * j : 3 * j + 1] if i == 0 else 0.0
                if engine == "scalar":
                    nc.scalar.activation(prods[a, x][:, cols], ratio_row[i][:, cols], ACT.Identity, scale=factor, bias=first)
                else:
                    queue = nc.gpsimd if engine == "gpsimd" else nc.vector
                    queue.tensor_scalar(out=prods[a, x][:, cols], in0=ratio_row[i][:, cols], scalar1=factor, scalar2=first, op0=ALU.mult, op1=ALU.add)

        def turn_a(a, t, js=range(J)):
            if (a, t) not in a_ps:
                a_ps[a, t] = take_bank([128, 512])
            for j in js:
                for i in range(2):
                    nc.tensor.matmul(a_ps[a, t][:, j * 128 : (j + 1) * 128], lhsT=prods[a, 2 * j + i][:, t * 128 : (t + 1) * 128], rhs=ident[:], start=(i == 0), stop=(i == 1), is_transpose=True)

        def empty_a(a, t):
            if a not in a_sb:
                a_sb[a] = work.tile([128, 128, 4, J], F32, name="a_sb")
            nc.scalar.activation(a_sb[a][:, :, t, :], a_ps[a, t][:].rearrange("p (j n) -> p n j", j=J), ACT.Identity, scale=pivot[:, t : t + 1], bias=b1_raw[:, t : t + 1])

        def leaky(a, j0=0, j1=J):
            if a not in m_bf:
                m_bf[a] = work.tile([128, 2048], BF16, name="m_bf", align_bytes=64, bufs=3)
            src = a_sb[a][:].rearrange("p n t j -> p (n t) j")[:, :, j0:j1]
            out = m_bf[a][:].rearrange("p (j x) -> p x j", j=J)[:, :, j0:j1]
            nc.vector.scalar_tensor_tensor(out=out, in0=src, scalar=SLOPE, in1=src, op0=ALU.mult, op1=ALU.max)

        def quant_m(a, j0=0, j1=J):
            if a not in m_q:
                m_q[a] = (work.tile([128, 512], U32, name="m_q", align_bytes=64), work.tile([128, 512], U8, name="m_s", align_bytes=64))
            cols = slice(j0 * 128, j1 * 128)
            nc.vector.quantize_mx(out=m_q[a][0][:, cols].bitcast(FP8X4), scales=m_q[a][1][:, cols], in_=m_bf[a][:, j0 * 512 : j1 * 512])

        def mx1(a, t):
            k_ps[a, t] = take_bank([128, 512])
            cols = slice(t * 128, (t + 1) * 128)
            nc.tensor.matmul_mx(k_ps[a, t][:], lhsT=w_q[W2][:, cols].bitcast(FP8X4), lhsT_scale=w_s[W2][:, cols], rhs=m_q[a][0][:].bitcast(FP8X4), rhs_scale=m_q[a][1][:], start=True, stop=True)

        def empty_k(a, t, j0=0, j1=J):
            if a not in k_sb:
                k_sb[a] = work.tile([128, 128, 2, 2, 4], F32, name="k_sb")
            src = k_ps[a, t][:, j0 * 128 : j1 * 128].rearrange("p (n i) -> p n i", i=4)
            nc.scalar.activation(k_sb[a][:, j0 * 32 : j1 * 32, t % 2, t // 2, :], src, ACT.Identity, bias=b2_raw[:, t : t + 1])

        def turn_f(a, h, from_ring=False):
            f_ps[a, h] = take_bank([128, 2, 256], hold=True) if from_ring else psum.tile([128, 2, 256], F32, name="f_ps", bufs=2)
            for jj in range(2):
                words = f_sb[a][:, 2 * h + jj, :].bitcast(F32)
                for g in range(2):
                    nc.tensor.transpose(f_ps[a, h][:, g, jj * 128 : (jj + 1) * 128], words[:, g:256:2], ident[:])

        def times_f(a, j0, j1):
            if a not in p_bf:
                p_bf[a] = work.tile([128, 2048], BF16, name="p_bf", align_bytes=64)
            words = f_ps[a, j0 // 2][:, :, j0 % 2 * 128 : (j0 % 2 + j1 - j0) * 128]
            fv = words.bitcast(BF16).rearrange("p g (n i e) -> p n g i e", i=4, e=2)
            kv = k_sb[a][:, j0 * 32 : j1 * 32].rearrange("p n e g i -> p n g i e")
            out = p_bf[a][:, j0 * 512 : j1 * 512].rearrange("p (n i e g) -> p n g i e", i=4, e=2, g=2)
            nc.vector.tensor_tensor(out=out, in0=fv, in1=kv, op=ALU.mult)

        def quant_p(a, j0=0, j1=J):
            if a not in p_q:
                p_q[a] = (work.tile([128, 512], U32, name="p_q", align_bytes=64, bufs=4), work.tile([128, 512], U8, name="p_s", align_bytes=64, bufs=4))
            cols = slice(j0 * 128, j1 * 128)
            nc.vector.quantize_mx(out=p_q[a][0][:, cols].bitcast(FP8X4), scales=p_q[a][1][:, cols], in_=p_bf[a][:, j0 * 512 : j1 * 512])

        def mx2(a, j0, j1, from_ring=True):
            for j in range(j0, j1):
                if j == 0:
                    o_ps[a] = take_bank([128, 512]) if from_ring else psum.tile([128, 512], F32, name="f_ps", bufs=2)
                cols = slice(j * 128, (j + 1) * 128)
                nc.tensor.matmul_mx(o_ps[a][:], lhsT=p_q[a][0][:, cols].bitcast(FP8X4), lhsT_scale=p_q[a][1][:, cols], rhs=w_q[j][:].bitcast(FP8X4), rhs_scale=w_s[j][:], start=(j == 0), stop=(j == J - 1))

        def mx2_turned(a, j0, j1):
            for j in range(j0, j1):
                if j == 0:
                    t_ps[a] = take_bank([128, 4, 128])
                rows = slice(j * 128, (j + 1) * 128)
                for t in range(4):
                    cols = slice(t * 128, (t + 1) * 128)
                    nc.tensor.matmul_mx(t_ps[a][:, t, :], lhsT=w_q[j][:, cols].bitcast(FP8X4), lhsT_scale=w_s[j][:, cols], rhs=p_q[a][0][:, rows].bitcast(FP8X4), rhs_scale=p_q[a][1][:, rows], start=(j == 0 and t == 0), stop=(j == J - 1 and t == 3))

        def empty_turned(a):
            out = o_bf[:, a * 512 : (a + 1) * 512].rearrange("p (n t) -> p n t", t=4)
            nc.vector.tensor_copy(out=out, in_=t_ps[a][:].rearrange("p t n -> p n t"))

        def empty_o(a):
            if a % ROUND == 0:
                r_grp[a // ROUND] = work.tile([128, ROUND * 512], F32, name="r_sb", bufs=TILES // ROUND)
            r_sb[a] = r_grp[a // ROUND][:, a % ROUND * 512 : (a % ROUND + 1) * 512]
            nc.scalar.copy(r_sb[a].rearrange("n (m t) -> n m t", t=4), o_ps[a][:].rearrange("n (t m) -> n m t", t=4))
            queue = nc.scalar if a == LAST else nc.sync
            queue.dma_start(out=out_0[a * 128 : (a + 1) * 128, :], in_=r_sb[a])

        def round_o(a0, a1, spent):
            rounded = spent[:, 0 : (a1 - a0) * 512]
            src = r_grp[a0 // ROUND][:, a0 % ROUND * 512 : (a0 % ROUND + a1 - a0) * 512]
            nc.gpsimd.tensor_scalar(out=rounded, in0=src, scalar1=1.0, scalar2=0.0, op0=ALU.mult, op1=ALU.add)
            for a in range(a0, a1):
                words = rounded[:, (a - a0) * 512 : (a - a0 + 1) * 512].bitcast(F32)
                o_w[a] = [words[:, h:256:2] for h in range(2)]

        def round_scalar(a):
            words = work.tile([128, 1, 2, 128, 2], BF16, name="o_w", align_bytes=64, bufs=2)
            nc.scalar.copy(words[:, 0], r_sb[a].rearrange("n (m h e) -> n h m e", h=2, e=2))
            o_w[a] = [words[:, 0, h].rearrange("n m e -> n (m e)").bitcast(F32) for h in range(2)]

        def round_from_bank(a):
            words = work.tile([128, 1, 2, 128, 2], BF16, name="o_w", align_bytes=64, bufs=2)
            nc.scalar.copy(words[:, 0], o_ps[a][:].rearrange("n (h e m) -> n h m e", h=2, e=2))
            o_w[a] = [words[:, 0, h].rearrange("n m e -> n (m e)").bitcast(F32) for h in range(2)]

        def turn_o(a0, a1):
            t_ps[a0] = take_bank([128, 2, 2, 128])
            for a in range(a0, a1):
                for h in range(2):
                    nc.tensor.transpose(t_ps[a0][:, a - a0, h, :], o_w[a][h], ident[:])

        def empty_t(a0, a1):
            out = o_bf[:, a0 * 512 : a1 * 512].bitcast(F32).rearrange("p (a n h) -> p a n h", n=128, h=2)
            nc.scalar.copy(out, t_ps[a0][:, 0 : a1 - a0].rearrange("p a h n -> p a n h"))

        def quant_o(a0, a1):
            cols = slice(a0 * 128, a1 * 128)
            nc.vector.quantize_mx(out=o_q[:, cols].bitcast(FP8X4), scales=o_s[:, cols], in_=o_bf[:, a0 * 512 : a1 * 512])

        def store_codes(a0, a1):
            cols = slice(a0 * 128, a1 * 128)
            nc.sync.dma_start(out=out_1[0, :, cols, :].rearrange("p m t -> p (m t)").bitcast(I32), in_=o_q[:, cols].bitcast(I32))

        def first_stage(a):
            for t in range(4):
                mx1(a, t)

        nc.vector.tensor_reduce(out=largest[:], in_=w1_pad[:], op=ALU.max, axis=mybir.AxisListType.X, apply_absolute_value=True)
        nc.scalar.activation(relf[:, 0, :], rel_0[:], ACT.Identity)
        nc.vector.scalar_tensor_tensor(out=pivot[:], in0=largest[:].to_broadcast([128, 4]), scalar=GUARD, in1=w1_col[:, 0, :], op0=ALU.mult, op1=ALU.add)
        nc.vector.reciprocal(out=inverse[:], in_=pivot[:])
        nc.vector.tensor_tensor(out=ratio[:], in0=w1_col[:, 1:3, :], in1=inverse[:].unsqueeze(1).to_broadcast([128, 2, 4]), op=ALU.mult)
        group_w(W2, 0, 5, "vector")
        group_w(W2, 5, 8, "scalar")
        quant_w(W2)
        for i in range(2):
            bank = psum.tile([128, 4, 128], F32, name="f_ps", bufs=2)
            for t in range(4):
                nc.tensor.transpose(bank[:, t, :], ratio[:, i, t : t + 1].to_broadcast([128, 128]), ident[:])
            nc.scalar.copy(ratio_row[i][:], bank[:].rearrange("p t m -> p (t m)"))
            if i == 0:
                nc.scalar.activation(relf[:, 1:, :], rel_raw[:, 1:, 0:12], ACT.Identity)
        products(0, (0, 2, 1, 3, 4, 5, 6, 7), "vector")
        for j in range(2):
            for t in range(4):
                turn_a(0, t, (j,))
        for t in range(4):
            turn_a(0, t, (2, 3))
        products(1, (0,), "scalar")
        group_w(0, 0, 8, "scalar")
        products(1, (1, 2, 3, 4, 5, 6, 7), "vector")
        for t in range(4):
            empty_a(0, t)
        quant_w(0)
        products(2, (1, 3, 5), "vector")
        turn_a(1, 0)
        turn_a(1, 1)
        turn_a(1, 2)
        leaky(0, 0, 2)
        leaky(0, 2, 4)
        empty_a(1, 0)
        turn_a(1, 3)
        quant_m(0, 0, 2)
        quant_m(0, 2, 4)
        empty_a(1, 1)
        empty_a(1, 2)
        group_w(1, 0, 4, "scalar")
        mx1(0, 0)
        mx1(0, 1)
        turn_f(0, 0)
        turn_f(0, 1)
        products(2, (0, 2, 4, 6, 7), "vector")
        empty_a(1, 3)
        group_w(1, 4, 8, "scalar")
        empty_k(0, 0)
        empty_k(0, 1)
        mx1(0, 2)
        mx1(0, 3)
        turn_a(2, 0)
        turn_a(2, 1)
        group_w(3, 0, 4, "scalar")
        empty_k(0, 2)
        empty_k(0, 3)
        group_w(3, 4, 8, "scalar")

        for s in range(2, LAST):
            leaky(s - 1)
            empty_a(s, 0)
            products(s + 1, (1,), "vector")
            if s == 2:
                quant_w(1)
            empty_a(s, 1)
            turn_a(s, 2)
            turn_a(s, 3)
            quant_m(s - 1, 0, 2)
            quant_m(s - 1, 2, 4)
            products(s + 1, (0, 2), "gpsimd")
            products(s + 1, (4,), "gpsimd", slice(0, 384))
            times_f(s - 2, 0, 2)
            times_f(s - 2, 2, 4)
            empty_a(s, 2)
            empty_a(s, 3)
            if s == 2:
                group_w(2, 0, 4, "scalar")
            mx1(s - 1, 0)
            mx1(s - 1, 1)
            mx1(s - 1, 2)
            empty_k(s - 1, 0)
            empty_k(s - 1, 1)
            if s == 2:
                quant_w(3)
                group_w(2, 4, 8, "vector")
            products(s + 1, (6, 7), "scalar")
            products(s + 1, (4,), "scalar", slice(384, 512))
            turn_f(s - 1, 0)
            turn_f(s - 1, 1)
            mx1(s - 1, 3)
            products(s + 1, (3,), "vector")
            quant_p(s - 2)
            products(s + 1, (5,), "vector")
            if s == 2:
                quant_w(2)
            mx2(s - 2, 0, 4)
            turn_a(s + 1, 0)
            turn_a(s + 1, 1)
            empty_k(s - 1, 2)
            empty_k(s - 1, 3)
            empty_o(s - 2)

        a = LAST
        leaky(a - 1, 0, 2)
        leaky(a - 1, 2, 4)
        empty_a(a, 0)
        empty_a(a, 1)
        turn_a(a, 2)
        turn_a(a, 3)
        quant_m(a - 1, 0, 2)
        quant_m(a - 1, 2, 4)
        round_o(0, 2, m_bf[a - 1])
        times_f(a - 2, 0, 2)
        times_f(a - 2, 2, 4)
        empty_a(a, 2)
        first_stage(a - 1)
        empty_a(a, 3)
        turn_f(a - 1, 0)
        turn_f(a - 1, 1)
        quant_p(a - 2, 0, 2)
        quant_p(a - 2, 2, 4)
        leaky(a, 0, 2)
        leaky(a, 2, 4)
        for t in range(4):
            empty_k(a - 1, t)
        turn_o(0, 2)
        mx2(a - 2, 0, 2)
        turn_f(a, 0, from_ring=True)
        mx2(a - 2, 2, 4)
        empty_t(0, 2)
        round_scalar(4)
        empty_o(a - 2)
        quant_m(a, 0, 2)
        quant_m(a, 2, 4)
        round_o(2, 4, m_bf[a])
        first_stage(a)
        times_f(a - 1, 0, 2)
        times_f(a - 1, 2, 4)
        for t in range(4):
            empty_k(a, t, 0, 2)
        for t in range(4):
            empty_k(a, t, 2, 4)
        turn_f(a, 1)
        turn_o(2, 4)
        quant_p(a - 1, 0, 2)
        quant_p(a - 1, 2, 4)
        round_o(5, 6, p_bf[a - 1])
        mx2(a - 1, 0, 4, from_ring=False)
        turn_o(4, 6)
        empty_t(2, 4)
        round_from_bank(a - 1)
        empty_o(a - 1)
        empty_t(4, 6)
        times_f(a, 0, 1)
        times_f(a, 1, 2)
        quant_p(a, 0, 1)
        times_f(a, 2, 3)
        quant_p(a, 1, 2)
        mx2_turned(a, 0, 1)
        mx2(a, 0, 1)
        mx2_turned(a, 1, 2)
        turn_o(6, 7)
        empty_t(6, 7)
        times_f(a, 3, 4)
        quant_p(a, 2, 3)
        quant_p(a, 3, 4)
        mx2_turned(a, 2, 4)
        mx2(a, 1, 4)
        quant_o(0, 4)
        store_codes(0, 4)
        quant_o(4, 6)
        quant_o(6, 7)
        store_codes(4, 7)
        empty_turned(a)
        empty_o(a)
        quant_o(7, 8)
        store_codes(7, 8)
        for q, queue in enumerate((nc.scalar, nc.scalar, nc.sync, nc.sync)):
            queue.dma_start(out=out_2[0, 4 * q : 4 * q + 4, :].bitcast(I32), in_=o_s[32 * q : 32 * q + 4, :].bitcast(I32))
